import numpy as np, ml_dtypes
CORES = [78,86,94,102,110,118]
N = 6
BF = ml_dtypes.bfloat16
def gentries(a):
    return np.ascontiguousarray(a.reshape(8, 16, -1).transpose(0, 2, 1)).reshape(8, -1)
def gtable(e):
    e = np.asarray(e); return np.ascontiguousarray(e.reshape(8, -1, 16).transpose(0, 2, 1)).reshape(128, -1).astype(np.int32)
V, R, L, ST, MF, SL, Q, TH = 3072, 2048, 256, 4, 5, 96, 2, 1365
def pairs(rng):
    a = rng.integers(0, R, (N, 8, L)); b = rng.integers(0, R, (N, 8, L))
    K = np.where(rng.random((N, 8, 1, L)) < 0.5, np.argsort(rng.random((N, 8, 16, L)), axis=2), rng.integers(0, 16, (N, 8, 16, L)))
    return a, b, K, rng.integers(0, 256, (N, 8, 16, L))
def pack(X, P, a, b, K, z, th):
    return {"ph": X.reshape(N, 128, V).astype(np.float32).astype(BF), "rp": np.ascontiguousarray(P.reshape(N, 128, R)).astype(np.int32),
            "av": np.stack([gtable(v) for v in a]), "bv": np.stack([gtable(v) for v in b]), "kc": np.ascontiguousarray(K.reshape(N, 128, L)).astype(np.int32),
            "zs": z.reshape(N, 128, L).astype(np.float32).astype(BF), "th": np.ascontiguousarray(th.reshape(N, 128, 1)).astype(np.int32)}
def camps(rng, M):
    h = V // 2; o = np.argsort(rng.random((N, 8, V)), axis=-1); side = np.zeros((N, 8, V), bool); np.put_along_axis(side, o[..., h:], True, 2)
    X = np.where(side[:, :, None], rng.integers(200, 256, (N, 8, 16, V)), rng.integers(0, 41, (N, 8, 16, V)))
    cl = np.broadcast_to(np.argsort(rng.random((M, 8, R)), axis=-1) & 3, (N, 8, R))
    up = np.argsort(rng.random((N, 8, 16, R)), axis=2) < np.array([0, 16, MF, MF + 1])[cl][:, :, None]
    pk = rng.integers(0, h, (N, 8, 16 * R))
    P = np.where(up, np.take_along_axis(o[..., h:2 * h], pk, 2).reshape(N, 8, 16, R), np.take_along_axis(o[..., :h], pk, 2).reshape(N, 8, 16, R))
    return X, P, np.argsort(cl, axis=-1, kind="stable")
def of(rng, birds, c):
    return np.take_along_axis(birds, c * (R // 4) + rng.integers(0, R // 4, c.shape), 2)
def setup_inputs(rng):
    a, b, K, z = pairs(rng)
    th = TH + 20 * rng.permutation(8)[None, :, None, None] + rng.integers(0, 40, (N, 8, 16, 1))
    return pack(rng.integers(0, 256, (N, 8, 16, V)), rng.integers(0, V, (N, 8, 16, R)), a, b, K, z, th)
def setup_inputs_spread(rng):
    a, b, K, z = pairs(rng)
    X = (np.exp2(8 * rng.random((N, 8, 1, V))) * rng.random((N, 8, 16, V))).astype(np.int64)
    z = (np.exp2(8 * rng.random((N, 8, 1, L))) * rng.random((N, 8, 16, L))).astype(np.int64)
    P = (V * rng.random((N, 8, 16, R)) ** 3).astype(np.int64); P[:, 1::2] = V - 1 - P[:, 1::2]
    a = (R * rng.random((N, 8, L)) ** 2).astype(np.int64); b = R - 1 - (R * rng.random((N, 8, L)) ** 3).astype(np.int64)
    K[:, ::2] = (16 * rng.random((N, 4, 16, L)) ** 2).astype(np.int64)
    th = np.minimum(4064, np.exp2(6 + 5 * rng.random((1, 8, 1, 1)) + rng.random((N, 8, 16, 1))).astype(np.int64))
    return pack(X, P, a, b, K, z, th)
def setup_inputs_ends(rng):
    s = 255 * rng.integers(0, 2, (N, 8, 1))
    kx = rng.integers(0, 3, (N, 8, 1, V)); X = np.where(kx < 2, 255 * kx, 255 * rng.integers(0, 2, (N, 8, 16, V))); X[..., 0] = s; X[..., V - 1] = 255 - s
    kz = rng.integers(0, 3, (N, 8, 1, L)); z = np.where(kz < 2, 255 * kz, 255 * rng.integers(0, 2, (N, 8, 16, L)))
    kp = rng.integers(0, 4, (N, 8, 1, R))
    P = np.where(kp < 2, (V - 1) * kp, np.where(kp == 2, (V - 1) * rng.integers(0, 2, (N, 8, 16, R)), rng.integers(0, V, (N, 8, 16, R))))
    P[..., 0] = (V - 1) * (np.argsort(rng.random((N, 8, 16)), axis=2) < rng.choice(np.array([MF, MF + 1, 3, 9]), (N, 8, 1)))
    P[..., 1] = V - 1; P[..., R - 1] = 0
    a, b = [np.where(rng.random((N, 8, L)) < 0.75, (R - 1) * rng.integers(0, 2, (N, 8, L)), rng.integers(0, R, (N, 8, L))) for i in range(2)]
    K = 15 * rng.integers(0, 2, (N, 8, 16, L)); th = 4064 * rng.integers(0, 2, (N, 8, 16, 1))
    e = np.array([0, 7, L - 1]); a[:, :, e] = R - 1; b[:, :, e] = R - 1; z[:, :, :, e] = (255 - s)[..., None]
    a[:, :, L - 2] = R - 1; b[:, :, L - 2] = 1
    return pack(X, P, a, b, K, z, th)
def setup_inputs_corners(rng):
    X, P, birds = camps(rng, N); a, b, K, z = pairs(rng); sh = int(rng.integers(0, 8))
    least = np.roll(np.array([SL, SL - 1, SL + 1, 0, L, 1, SL, L - 1]), sh); even = np.roll(np.arange(8) == 6, sh)
    C = least + ((L - least + 1) * rng.random((N, 8))).astype(np.int64); C[rng.integers(0, N, 8), np.arange(8)] = least; C = np.where(even, SL, C)
    kd = rng.integers(0, 3, (N, 8, 1)); ln = np.arange(L)
    div = np.argsort(np.argsort(np.where(kd == 0, rng.random((N, 8, L)), np.where(kd == 1, ln, -ln)), axis=-1), axis=-1) < C[..., None]
    s = rng.integers(0, 3, (N, 8, L))
    a = of(rng, birds, np.where(div, np.array([3, 1, 0])[s], np.array([0, 1, 2])[s])); b = of(rng, birds, np.where(div, np.array([0, 0, 1])[s], np.array([0, 1, 0])[s]))
    m = rng.integers(0, 6, (N, 8, 1, L)); row = np.arange(16)[:, None]
    K = np.where(m == 0, row, np.where(m == 1, 0, np.where(m == 2, 15, np.where(m == 3, 15 - row, K))))
    return pack(X, P, a, b, K, z, rng.integers(900, 2501, (N, 8, 16, 1)))
def setup_inputs_crowd(rng):
    X, P, birds = camps(rng, 1); a, b, K, z = pairs(rng); ln = np.arange(L)
    o = rng.permutation(np.array([0, 1, 2, 3, 6, 7])); p = int(rng.choice(np.array([0, 4, 6])))
    md = np.concatenate([o[:p], np.array([5, 4]), o[p:]])[None, :, None]
    two = np.take_along_axis(birds, (rng.integers(0, R // 4, (N, 8, 1)) + np.arange(2)) & (R // 4 - 1), 2)
    other = ((md == 1) & (ln == 0)) | ((md == 2) & (ln == L - 1)); same = (md < 3) | (md == 6)
    b = np.where(same, np.where(other, two[..., 1:], two[..., :1]), np.where(md == 3, np.take_along_axis(two, rng.integers(0, 2, (N, 8, L)), 2), np.where(md == 7, b, of(rng, birds, np.zeros((N, 8, L), np.int64)))))
    lone = ln == rng.integers(0, L, (N, 8, 1))
    high = (md == 4) | ((md == 5) & ~lone) | ((md == 6) & (ln < L // 2)) | ((md == 3) & (rng.random((N, 8, L)) < 0.5))
    a = np.where(md == 7, a, of(rng, birds, high.astype(np.int64)))
    K = np.where(same[:, :, None], rng.integers(0, 16, (N, 8, 1, 1)), K)
    th = np.where(md[:, :, None] < 3, 4064, rng.integers(900, 2501, (N, 8, 16, 1)))
    odd = (np.arange(N) & 1)[:, None, None] == 1; sure = (np.argsort(rng.random((N, 8, 16)), axis=2) < MF + 1)[..., None]
    near = ((md == 4) | ((md == 5) & odd))[:, :, None] & ~sure
    th = np.where(near, 4 * rng.integers(810, 851, (N, 8, 16, 1)) - rng.integers(0, 2, (N, 8, 16, 1)), th)
    return pack(X, P, a, b, K, z, th)
def setup_inputs_ties(rng):
    a, b, K, z = pairs(rng); pal = np.array([0, 60, 120, 120, 120, 120, 180, 180]); row = np.arange(16)[:, None]
    X = rng.choice(pal, (N, 8, 1, V)) + ((rng.random((N, 8, 1, V)) < 0.3) & (row == rng.integers(0, 16, (N, 8, 1, V))))
    z = rng.choice(pal, (N, 8, 1, L)) + ((rng.random((N, 8, 1, L)) < 0.3) & (row == rng.integers(0, 16, (N, 8, 1, L))))
    P = rng.integers(0, V, (N, 8, 16, R)); P[:, 1::2, 8:] = P[:, 1::2, :8]
    b = np.where(rng.random((N, 8, L)) < 0.3, a, b); a[:, :, 0] = 0; b[:, :, 0] = R - 1; a[:, :, L - 1] = R - 1; b[:, :, L - 1] = R - 1
    K = np.where(rng.random((N, 8, 1, L)) < 0.2, row, K); h = L // 2
    for v in (a, b, K, z): v[:, 2::3, ..., h:] = v[:, 2::3, ..., :h]
    th = 960 - rng.integers(-1, 33, (N, 8, 16, 1))
    Y, W, birds = camps(rng, 1); s = np.array([3, 4, 6]); lo = rng.integers(0, 156, (N, 8, 16, 1)); up = rng.integers(40, 100, (N, 8, 16, 1))
    rest = birds[0, 6, R // 4 + R // 128:]; W[:, 6][:, :, rest] = W[:, 6][:, :, birds[0, 6, rng.integers(0, R // 4, len(rest))]]
    cnt = (np.arange(N)[:, None] + rng.integers(0, 4, 3)) & 3; cnt[:, 1] = 1 + (np.arange(N) + int(rng.integers(0, 3))) % 3
    e = np.ones((N, 3), np.int64); e[:, 1] = cnt[:, 1] + rng.integers(0, 2, N); e[:, 2] = rng.integers(1, 4, N)
    hot = np.argsort(rng.random((N, 3, L)), axis=-1) < cnt[..., None]
    warm = np.take_along_axis(birds, R // 4 + rng.integers(0, R // 128, (N, 8, L)), 2); calm = of(rng, birds, np.zeros((N, 8, L), np.int64))
    X[:, s] = (lo + up * (Y[:, :, :1] >= 200))[:, s]; P[:, s] = W[:, s]; z[:, s] = rng.integers(0, 256, (N, 3, 16, L))
    a[:, s] = np.where(hot, warm[:, s], calm[:, s]); b[:, s] = of(rng, birds, np.zeros((N, 8, L), np.int64))[:, s]
    th[:, s] = np.add.reduce(up, axis=2, keepdims=True)[:, s] - e[:, :, None, None]
    return pack(X, P, a, b, K, z, th)
def check_inputs(d):
    bad = []
    for k, lo, hi in (("ph", 0, 255), ("rp", 0, V - 1), ("av", 0, R - 1), ("bv", 0, R - 1), ("kc", 0, 15), ("zs", 0, 255), ("th", 0, 4064)):
        v = np.asarray(d[k]).astype(np.float64)
        if not (np.min(v) >= lo and np.max(v) <= hi): bad.append("range of " + k)
        elif np.any(v != np.floor(v)): bad.append("whole numbers in " + k)
    return bad
def reference(ph, rp, av, bv, kc, zs, th):
    X = ph.astype(np.int32).reshape(N, 8, 16, V); P = rp.astype(np.int64).reshape(N, 8, 16, R); lim = th.astype(np.int64).reshape(N, 8, 16, 1)
    a = np.stack([gentries(v) for v in av]).astype(np.int64); b = np.stack([gentries(v) for v in bv]).astype(np.int64)
    K = kc.astype(np.int64).reshape(N, 8, 16, L); z = zs.astype(np.int32).reshape(N, 8, 16, L); A = np.zeros((N, 8), np.int64)
    wt = (2 * np.arange(16) + 1)[:, None]
    for t in range(ST):
        if t > 0: a, b, K, z = [np.roll(v, 1, axis=0) for v in (a, b, K, z)]
        ra = np.take_along_axis(P, a[:, :, None], 3); rb = np.take_along_axis(P, b[:, :, None], 3)
        x = np.take_along_axis(X, ra.reshape(N, 8, 1, 16 * L), 3).reshape(N, 8, 16, 16, L)
        y = np.take_along_axis(X, rb.reshape(N, 8, 1, 16 * L), 3).reshape(N, 8, 16, 16, L)
        w = np.take_along_axis(y, K[:, :, None], 3)
        d = np.add.reduce(np.abs(x - w), axis=2)
        mis = d > lim + (A & 31)[:, :, None, None]
        div = np.add.reduce(mis.astype(np.int64), axis=2) > MF
        k = np.argmin(np.add.reduce(np.abs(x - z[:, :, :, None]), axis=2), axis=2)
        xk = np.take_along_axis(x, k[:, :, None, None], 3)[:, :, :, 0]; wk = np.take_along_axis(w, k[:, :, None, None], 3)[:, :, :, 0]
        c = np.take_along_axis(rb, np.take_along_axis(K, k[:, :, None], 2), 2)[:, :, 0]
        half = (xk + wk) >> 1
        for h in range(N):
            for g in range(8):
                m = np.flatnonzero(~div[h, g]); col, first = np.unique(c[h, g, m], return_index=True)
                X[h, g][:, col] = half[h, g][:, m[first]]
        zn = np.where(div[:, :, None], (z + x[:, :, :, 0]) >> 1, np.abs(z - wk))
        an = np.where(div, a, (5 * a + np.add.reduce(zn * wt, axis=2)) & (R - 1))
        A = np.add.reduce(div.astype(np.int64), axis=2); n = np.minimum(SL, np.minimum.reduce(A, axis=0))
        bn = np.array(b); Kn = np.array(K)
        for h in range(N):
            q = (h + Q) % N
            for g in range(8):
                me = np.flatnonzero(div[h, g])[:n[g]]; mate = np.flatnonzero(div[q, g])[:n[g]]
                bn[h, g, me] = b[q, g, mate]; own = K[h, g][:, me]
                Kn[h, g][:, me] = np.where(mis[h, g][:, me], np.take_along_axis(K[q, g][:, mate], own, 0), own)
        a, b, K, z = an, bn, Kn, zn
    return {"yx": X.reshape(N, 128, V).astype(np.float32).astype(BF), "yk": K.reshape(N, 128, L).astype(np.float32).astype(BF),
            "ya": np.stack([gtable(v) for v in a]).astype(np.float32), "yb": np.stack([gtable(v) for v in b]).astype(np.float32), "yz": z.reshape(N, 128, L).astype(np.float32).astype(BF)}

@@ -1,0 +1,542 @@
+from concourse.bass import DstId, RemoteDMATransfer
+from concourse.mybir import AluOpType as Op, AxisListType as Ax, ActivationFunctionType as Fn
+
+N, V, L, ST = 6, 3072, 256, 4
+MAGIC = 12582912.0
+PLAN = {"y": ["V2 V2 V2 S2", "V1 S1 V2 V1 V1 S2"], "x": ["S1 V1 S2 S2 S2", "S2 S2 S2 S2"], "r": ["SVSV", "VSSV"], "CH": [0, 64, 128, 192, 256],
+        "z": ["SSSS", "SSSS"], "rounds": 400, "seed": 1, "jit": 4, "tol": 0, "p": 0.02, "mix": 1.0}
+CY, PC, GA, SC, WAKE = 1.04e-3, 0.52e-3, 1.56, 3.8, 0.06
+LAT = {"A": 5.0, "Q": 5.3, "a": 3.6, "z": 5.0, "small": 3.5, "RP": 9.0, "X": 13.0, "send": 0.6}
+
+
+def sb(n, dt="bfloat16"):
+    return ("sbuf", [128, n], dt)
+
+
+SCRATCH = {
+    "X": sb(V + L), "RP": sb(2048, "int32"), "xx": sb(4096), "yy": sb(4112), "dd": sb(4096), "rl": sb(4096), "az": sb(4096),
+    "avi": sb(16, "int32"), "bvi": sb(16, "int32"), "kci": sb(256, "int32"), "thi": sb(1, "int32"), "z0": sb(256),
+    "J": sb(256, "float32"), "pci": sb(8, "int32"), "pcj": sb(8, "int32"), "col": sb(24, "float32"),
+    "IS": sb(10 * 128), "I4f": sb(128, "float32"), "BO": sb(128), "Um": sb(128), "BOh": sb(128, "float16"), "Zh": sb(144, "float16"),
+    "ZS": sb(7 * 144), "ze": sb(4096), "zm": sb(256), "FA": sb(2048), "FB": sb(2048), "BA": sb(128), "BB": sb(128), "PM": sb(512), "ID": sb(16), "IDf": sb(16, "float32"),
+    "tA": sb(256, "float32"), "tB": sb(256, "float32"), "tI": sb(256, "int32"), "tJ": sb(256, "int32"), "tC": sb(256, "float32"),
+    "cm1": sb(256), "c32k": sb(256), "c16l": sb(256), "cmask": sb(256, "float32"), "crst": sb(256, "float32"),
+    "cf": sb(64, "float32"), "cb": sb(48), "pw": sb(112, "float32"),
+    "base": sb(32, "int32"), "expl": sb(16, "uint16"), "BT": sb(96), "bl": sb(32, "uint16"), "bli": sb(32, "int32"),
+    "ra": sb(256, "uint16"), "rb": sb(256, "uint16"), "rbv": sb(256, "float16"), "offY": sb(256, "uint16"), "bu": sb(16, "uint16"),
+    "KB": sb(1024), "WB": sb(4 * 352), "KT": sb(256), "KL": sb(256), "sg": sb(256), "sB": sb(256), "tt": sb(256), "zt": sb(512), "r32": sb(256, "float32"),
+    "r33": sb(256, "float32"), "thA": sb(1, "float32"), "thf": sb(1, "float32"), "Ai": sb(2, "int32"), "dv": sb(16), "cs": sb(16), "t1": sb(16),
+    "off": sb(16, "uint16"), "af": sb(16, "float32"), "mar": sb(16, "float32"), "m0": sb(320, "float32"), "vi": sb(16, "int32"),
+    "Li": sb(32, "int32"), "Lj": sb(32, "int32"), "Lu": sb(32, "uint16"), "Ku": sb(16, "uint16"), "wk": sb(256), "xk": sb(256), "hf": sb(256),
+    "mm": sb(256, "float16"), "cB": sb(256, "float32"), "cL": sb(16, "float32"), "cm": sb(16, "float32"), "eq": sb(256, "float32"),
+    "sc": sb(256, "float32"), "so": sb(16, "float32"), "su": sb(32, "uint16"), "an1": sb(16, "float32"), "an2": sb(16, "int32"), "an3": sb(16, "int32"),
+    "nn": sb(2, "float32"), "l1": sb(16, "float32"), "l2": sb(16, "float32"), "l2u": sb(16, "uint16"), "aW": sb(96), "b16": sb(192), "sn": sb(256),
+    "uu": sb(96), "u2": sb(96), "k2": sb(96), "TR": sb(1536), "oa": sb(16, "float32"), "ob": sb(16, "float32"), "ok": sb(256),
+    "PT": sb(3 * 288), "LT": sb(4 * 576), "AF": sb(4 * 16), "aS": sb(3 * 16, "uint16"), "aL": sb(4 * 16, "uint16"), "zS": sb(4 * 256), "zL": sb(3 * 256),
+    "pa": ("psum", [128, 1024], "float32"), "pb": ("psum", [128, 1024], "float32"), "pc": ("psum", [128, 1024], "float32"),
+    "pd": ("psum", [128, 512], "float32"), "pk": ("psum", [128, 512], "float32"),
+}
+SEMAPHORES = (["V", "S", "P", "G", "ld0", "ld1", "ld2", "out", "sent"]
+              + ["%s%d" % (s, t) for s in ("sA", "sQ", "sa", "sz", "sK") for t in range(ST)])
+ORDER = {}
+
+
+def place(eng, dur, pre, rank):
+    n = len(eng)
+    suc = [[] for _ in eng]
+    for i in range(n):
+        for p in pre[i]:
+            suc[p].append(i)
+    left = [len(p) for p in pre]
+    start, busy = [0.0] * n, {}
+    cand = sorted([(-rank[i], i) for i in range(n) if not left[i]])
+    while cand:
+        f = cand.pop()[1]
+        s = max([start[p] + dur[p] + lag for p, lag in pre[f].items()] + [0.0])
+        if eng[f] != "R":
+            b = busy.setdefault(eng[f], [])
+            k = len(b)
+            while k and b[k - 1][1] > s:
+                k -= 1
+            while k < len(b) and b[k][0] < s + dur[f] - 1e-9:
+                s = max(s, b[k][1])
+                k += 1
+            b.insert(k, (s, s + dur[f]))
+        start[f] = s
+        for k in suc[f]:
+            left[k] -= 1
+            if not left[k]:
+                cand.append((-rank[k], k))
+                cand.sort()
+    return start, max(start[i] + dur[i] for i in range(n))
+
+
+def schedule(ops):
+    n = len(ops)
+    eng, dur = [o["e"] for o in ops], [o["c"] for o in ops]
+    pre = [{p: WAKE if (eng[p] != o["e"] or raw) and eng[p] != "R" else 0.0 for p, raw in o["pre"].items()} for o in ops]
+    suc = [{} for _ in ops]
+    for i in range(n):
+        for p, lag in pre[i].items():
+            suc[p][i] = lag
+    tail = [0.0] * n
+    for i in range(n - 1, -1, -1):
+        tail[i] = dur[i] + max([tail[k] + lag for k, lag in suc[i].items()] + [0.0])
+    rank, best, x = [-v for v in tail], None, PLAN["seed"]
+    for _ in range(PLAN["rounds"]):
+        start, t = place(eng, dur, pre, rank)
+        if best is None or t < best[1]:
+            best = (start, t)
+        elif t > best[1] + PLAN["tol"]:
+            start = best[0]
+        back, tb = place(eng, dur, suc, [-(start[i] + dur[i]) for i in range(n)])
+        rank = []
+        for i in range(n):
+            x = (x * 1103515245 + 12345) % 2147483648
+            u = x / 2147483648
+            rank.append(PLAN["mix"] * (tb - back[i] - dur[i]) + (1 - PLAN["mix"]) * start[i]
+                        + (PLAN["jit"] * (2 * u / PLAN["p"] - 1) if u < PLAN["p"] else 0.0))
+    ORDER["dbg"] = (ops, best[0], pre, max(tail))
+    return sorted(range(n), key=lambda i: (best[0][i], i)), best[1]
+
+
+def rank_program(g, core, T, topo):
+    rank = T.rank_of(core)
+    if rank is None:
+        return
+    Q = {"V": g.vector, "S": g.scalar, "P": g.tensor, "G": g, "Y": g.sync}
+    ops, wr, rd, bank, alias = [], {}, {}, {}, {"K1": [], "K2": []}
+    sent = [0]
+
+    def op(e, f, c, r="", w="", b="", tok=None):
+        i = len(ops)
+        pre = {}
+        ws = []
+        for k in w.split():
+            if k in alias:
+                alias[k].append(i)
+            else:
+                ws.append(k)
+        for k in ws:
+            for p in rd.get(k, []) + wr.get(k, []):
+                pre[p] = True
+        for k in b.split():
+            if k in bank:
+                pre.setdefault(bank[k], False)
+            bank[k] = i
+        for k in r.split():
+            for p in (alias[k] if k in alias else wr.get(k, [])):
+                pre[p] = True
+            if k not in alias:
+                rd.setdefault(k, []).append(i)
+        for k in ws:
+            wr[k], rd[k] = [i], []
+        pre.pop(i, None)
+        ops.append({"e": e, "f": f, "c": c, "pre": pre, "tok": tok, "w": w or r})
+
+    def cost(out, per):
+        n = out.shape[1]
+        return {"g": 0.065 + n * GA * CY, "s": 0.065 + n * SC * CY}[per] if per in ("g", "s") else max(64, n * per) * CY
+
+    def ts(out, in0, s1, o0, s2=None, o1=None, r="", w="", b="", c=1):
+        if o1 is None:
+            op("V", lambda: g.vector.tensor_scalar(out, in0, s1, None, o0), cost(out, c), r, w, b)
+        else:
+            op("V", lambda: g.vector.tensor_scalar(out, in0, s1, s2, o0, o1), cost(out, c), r, w, b)
+
+    def tt(out, a, x, o, r="", w="", b="", c=None):
+        op("V", lambda: g.vector.tensor_tensor(out, a, x, o), cost(x, c or (1 if b else 2)), r, w, b)
+
+    def cp(out, a, r="", w="", b="", c=1):
+        op("V", lambda: g.vector.tensor_copy(out, a), cost(a if c == "s" else out, c), r, w, b)
+
+    def act(out, a, fn, r="", w="", b="", bias=0.0, scale=1.0, c=1):
+        op("S", lambda: g.scalar.activation(out, a, fn, bias=bias, scale=scale), cost(out, c), r, w, b)
+
+    def scan(out, a, x, ini, o0, o1, r, w):
+        op("V", lambda: g.vector.tensor_tensor_scan(out, a, x, ini, o0, o1), cost(out, 1), r, w)
+
+    def ms(ap, v, w):
+        op("V", lambda: g.vector.memset(ap, v), cost(ap, 0.5), w=w)
+
+    def mm(groups, r="", b="", first=True, end=True, extra=0):
+        def f():
+            ins = None
+            for out, terms in groups:
+                for i, (a, c) in enumerate(terms):
+                    ins = g.tensor.matmul(out, a, c, first and i == 0, end and i == len(terms) - 1)
+            return ins
+        op("P", f, PC * (extra + sum(max(64, o.shape[1]) * len(x) for o, x in groups)), r + " K1", "", b)
+
+    def dst(h):
+        a = topo.addr(T.cores[h % N])
+        return DstId(rid=a[0], pnc=a[1])
+
+    def engines(hs):
+        out = topo.engines(core, T.cores[hs[0] % N])
+        for h in hs[1:]:
+            out = [e for e in out if e in topo.engines(core, T.cores[h % N])]
+        return out
+
+    def send(transfers, r, name, kind, sem, count):
+        def f():
+            g.remote_dma_fused([RemoteDMATransfer(dst_ids=[dst(h) for h, _ in ds], dma_engine_mask=sum(1 << e for e in es), remote_sem=T.sem[sem],
+                                                  srcs=[src], dsts=[d for _, d in ds]) for src, ds, es in transfers], local_sem=T.sem.sent)
+        sent[0] += sum(len(x[2]) for x in transfers)
+        op("G", f, LAT["send"], r, "snd" + sem)
+        op("R", None, LAT[kind], "snd" + sem, name, tok=(sem, count))
+
+    def dma(e, o, i, sem, r=""):
+        def f():
+            Q[e].dma_start(o, i).then_inc(T.sem[sem], 16)
+        op(e, f, 0.1, r, "q" + e + sem)
+
+    ne = len(engines([rank + 1]))
+    pa, pb, pc, pd, pk = T.pa, T.pb, T.pc, T.pd, T.pk
+    col, J = T.col, T.J
+    kc_, gc_, pc_, hc_, zc_, w2_, wb_, wi_, bq_, k4_ = [col[:, i:i + 1] for i in range(10)]
+    I1, Im, I256, Ih, Iq, Im256, I4k, Im8, I8, I2k = [T.IS[:, 128 * i:128 * i + 128] for i in range(10)]
+    Z1, Z2, Zm, Zk, Zu, Zb, Zn = range(7)
+    lL, dum, one, c16i = [T.cf[:, 16 * i:16 * i + 16] for i in range(4)]
+    c256, c255, c1536 = [T.cb[:, 16 * i:16 * i + 16] for i in range(3)]
+
+    def E(z, r):
+        return T.Zh[:, 15 - r:143 - r] if z is None else T.ZS[:, 144 * z + 15 - r:144 * z + 143 - r]
+
+    for o, i in ((T.avi, T.av), (T.bvi, T.bv), (T.kci, T.kc), (T.z0, T.zs), (T.thi, T.th)):
+        dma("Y", o[:], i[:], "ld0")
+    dma("Y", T.RP[:], T.rp[:], "ld1", "qYld0")
+    dma("Y", T.X[:, 0:V], T.ph[:], "ld2", "qYld1")
+    op("R", None, LAT["small"], "qYld0", "avi bvi kci z0 thi", tok=("ld0", 80))
+    op("R", None, LAT["RP"], "qYld1", "RP", tok=("ld1", 16))
+    op("R", None, LAT["X"], "qYld2", "X", tok=("ld2", 16))
+
+    op("G", lambda: g.iota(T.pci[:, 0:1], [[0, 1]], 0, 1), 0.15, w="pci")
+    op("G", lambda: g.iota(J[:], [[1, 256]], 0, 0, allow_small_or_imprecise_dtypes=True), 0.65, w="J")
+    op("G", lambda: g.iota(T.tA[:], [[1, 16], [0, 16]], 0, 0, allow_small_or_imprecise_dtypes=True), 0.65, w="tA")
+    op("G", lambda: g.iota(T.tB[:], [[0, 16], [1, 16]], 0, 0, allow_small_or_imprecise_dtypes=True), 0.65, w="tB")
+    ms(T.yy[:, 4096:4112], 0.0, "yz")
+    ms(T.X[:, V:V + L], 0.0, "Xd")
+    ms(T.PT[:], 96.0, "PT0A PT1A PT2A PT0o PT1o PT2o PT0p PT1p PT2p")
+    ms(T.LT[:, 3 * 576:3 * 576 + 304], 96.0, "PT3A PT3o PT3p")
+    for t in range(ST):
+        ms(T.AF[:, 16 * t:16 * t + 8], 96.0, "AF%d" % t)
+    ms(T.cm1[:], -1.0, "K1")
+    ms(one, 1.0, "K1")
+    ms(c1536, 1536.0, "K1")
+    ms(T.su[:], 0, "su")
+    ts(T.pcj[:, 0:1], T.pci[:, 0:1], 15, Op.bitwise_and, r="pci", w="pj0")
+    ts(T.pcj[:, 1:2], T.pci[:, 0:1], 4, Op.arith_shift_right, r="pci", w="pj1")
+    ts(T.pcj[:, 3:4], T.pci[:, 0:1], 4, Op.arith_shift_right, 1, Op.bitwise_and, r="pci", w="pj3")
+    cp(T.pcj[:, 2:3], T.pci[:, 0:1], "pci", "pj2")
+    cp(col[:, 0:4], T.pcj[:, 0:4], "pj0 pj1 pj2 pj3", "kc gc pc hc")
+    ts(zc_, gc_, 16.0, Op.mult, 15.0, Op.add, r="gc", w="zc")
+    ts(w2_, kc_, 2.0, Op.mult, 1.0, Op.add, r="kc", w="w2")
+    ts(T.IDf[:], J[:, 0:16], kc_, Op.is_equal, r="J kc", w="IDf")
+    cp(T.ID[:], T.IDf[:], "IDf", "K1")
+    pw = [T.pw[:, 16 * i:16 * i + 16] for i in range(7)]
+    ms(pw[0], 2.0, "pw0")
+    ms(pw[1], 0.5, "pw1")
+    ms(pw[2], 0.0, "pw2")
+    scan(pw[3], pw[0], pw[2], 0.25, Op.mult, Op.add, "pw0 pw2", "pw3")
+    scan(pw[4], pw[1], pw[2], 65536.0, Op.mult, Op.add, "pw1 pw2", "pw4")
+    tt(pw[5], pw[3], T.IDf[:], Op.mult, "pw3 IDf", "pw5")
+    tt(pw[6], pw[4], T.IDf[:], Op.mult, "pw4 IDf", "pw6")
+    op("V", lambda: g.vector.tensor_reduce(wb_, pw[5], Ax.X, Op.add), 0.07, "pw5", "wb")
+    op("V", lambda: g.vector.tensor_reduce(wi_, pw[6], Ax.X, Op.add), 0.07, "pw6", "wi")
+    ts(I1, J[:, 0:128], pc_, Op.is_equal, r="J pc", w="I1 K1")
+    for buf, v in ((Im, -1.0), (I256, 256.0), (Ih, 0.5), (Iq, 0.25), (Im256, -256.0), (I4k, 4096.0), (I2k, 2048.0), (Im8, -8.0), (I8, 8.0), (T.I4f[:], 4.0)):
+        act(buf, I1, Fn.Identity, "I1", "K1", scale=v)
+    ts(T.ZS[:, 0:144], J[:, 0:144], zc_, Op.is_equal, r="J zc", w="Z1 K1")
+    ts(T.Zh[:], J[:, 0:144], zc_, Op.is_equal, r="J zc", w="K1")
+    for zi, v in ((Z2, 2.0), (Zm, -1.0), (Zk, 512.0), (Zn, -512.0), (Zu, w2_), (Zb, wb_)):
+        act(T.ZS[:, 144 * zi:144 * zi + 144], T.ZS[:, 0:144], Fn.Identity, "Z1 w2 wb", "K1", scale=v)
+    ts(T.BO[:], T.tA[:, 0:128], gc_, Op.is_equal, r="tA gc", w="BO K1")
+    ts(T.BOh[:], T.tA[:, 0:128], gc_, Op.is_equal, r="tA gc", w="K1")
+    ts(T.tC[:, 0:128], T.tB[:, 0:128], kc_, Op.is_lt, -1.0, Op.mult, r="tB kc", w="tC")
+    tt(T.Um[:], T.tC[:, 0:128], T.BO[:], Op.mult, "tC BO", "K1")
+    ts(lL, J[:, 0:16], 16.0, Op.mult, kc_, Op.add, r="J kc", w="lL")
+    ts(c256, lL, -1.0, Op.mult, 256.0, Op.add, r="lL", w="K1")
+    ts(c255, lL, -1.0, Op.mult, 255.0, Op.add, r="lL", w="K1")
+    ts(dum, lL, float(V), Op.add, r="lL", w="dum K1")
+    ts(c16i, lL, 96.0, Op.add, r="lL", w="K1")
+    ts(T.base[:, 16:32], lL, 16.0, Op.mult, r="lL", w="K1")
+    ts(T.base[:, 0:16], lL, 16.0, Op.mult, r="lL", w="K1")
+    cp(T.expl[:], J[:, 0:16], "J", "K1")
+    act(T.c32k[:], T.tA[:], Fn.Identity, "tA", "K1", scale=32.0)
+    ts(T.r32[:], T.tB[:], kc_, Op.is_ge, 16384.0, Op.mult, r="tB kc", w="r32")
+    act(T.cmask[:], T.r32[:], Fn.Identity, "r32", "K1", bias=3584.0)
+    ts(T.crst[:], T.tB[:], 0.5, Op.is_gt, r="tB", w="crst")
+    cp(T.crst[:, 15::16], dum, "dum crst", "crst K1")
+    for h in range(2):
+        ts(col[:, 10 + h:11 + h], hc_, float(h), Op.is_equal, r="hc", w="hs%d" % h)
+        for e in range(2):
+            q = 2 * h + e
+            ts(col[:, 12 + q:13 + q], pc_, float(16 * (e - h)), Op.add, r="pc", w="ps%d" % q)
+            ts(T.PM[:, q * 128:q * 128 + 128], J[:, 0:128], col[:, 12 + q:13 + q], Op.is_equal, col[:, 10 + h:11 + h], Op.mult,
+               r="J ps%d hs%d" % (q, h), w="K1")
+    op("G", lambda: g.iota(T.cB[:], [[0, 4], [256, 4], [0, 16]], 0, 0, allow_small_or_imprecise_dtypes=True), 0.65, w="cB")
+    ts(T.r33[:], T.cB[:], T.IDf[:, 0:1], Op.mult, r="cB IDf", w="r33")
+    ts(T.eq[:], T.tB[:], T.IDf[:, 1:2], Op.mult, 16.0, Op.mult, r="tB IDf", w="eq")
+    tt(T.c16l[:], T.r33[:], T.eq[:], Op.add, "r33 eq", "K2")
+    act(T.tC[:, 128:256], T.tB[:, 0:128], Fn.Identity, "tB", "tD", bias=32.0, scale=32.0)
+    tt(T.BA[:], T.tC[:, 128:256], T.BO[:], Op.mult, "tD BO", "BA")
+    act(T.BB[:], T.BO[:], Fn.Identity, "BO", "BB", scale=-16.0)
+    ts(k4_, kc_, 1.0, Op.add, 4.0, Op.mult, r="kc", w="k4")
+    ts(bq_, k4_, k4_, Op.mult, -1.0, Op.mult, r="k4", w="K2")
+    for k in range(16):
+        act(T.FA[:, 128 * k:128 * k + 128], T.BA[:], Fn.Identity, "BA IDf", "K2", scale=T.IDf[:, k:k + 1])
+        ts(T.FB[:, 128 * k:128 * k + 128], T.BB[:], T.IDf[:, k:k + 1], Op.mult, r="BB IDf", w="K2", c=0.5)
+    cp(T.aL[:, 0:16], T.avi[:], "avi", "a0")
+    cp(T.bu[:], T.bvi[:], "bvi", "bu")
+    ts(T.bli[:, 0:16], T.bvi[:], 63, Op.bitwise_and, r="bvi", w="bli0")
+    ts(T.bli[:, 16:32], T.bvi[:], 6, Op.arith_shift_right, r="bvi", w="bli1")
+    cp(T.bl[:, 0:16], T.bli[:, 0:16], "bli0", "bl0")
+    ts(T.bl[:, 16:32], T.bli[:, 16:32], 64.0, Op.add, r="bli1", w="bl1")
+    ts(T.tI[:, 0:64], J[:, 0:64], wi_, Op.mult, r="J wi", w="tI0")
+    ts(T.tI[:, 64:96], J[:, 0:32], wi_, Op.mult, 64.0, Op.mult, r="J wi", w="tI1")
+    ts(T.tI[:, 96:192], T.tI[:, 0:96], 15, Op.arith_shift_right, 1, Op.bitwise_and, r="tI0 tI1", w="tI2")
+    ts(T.BT[:], T.tI[:, 96:192], 16.0, Op.mult, r="tI2", w="BT")
+    ts(T.thf[:], T.thi[:], -1.0, Op.mult, -0.5, Op.add, r="thi", w="thf")
+    ts(T.thA[:], T.thi[:], -1.0, Op.mult, -0.5, Op.add, r="thi", w="thA")
+    op("G", lambda: g.iota(T.sc[:], [[0, 4], [16, 64]], 0, 0, allow_small_or_imprecise_dtypes=True), 0.65, w="sc")
+    tt(T.tJ[:], T.sc[:], T.kci[:], Op.add, "sc kci", "tJ")
+    cp(T.offY[:], T.tJ[:], "tJ", "offY")
+    tt(T.wk[:], T.BT[:].indirect(T.bl[:, 0:16]), T.kci[:], Op.add, "BT bl0 kci", "wk", c="g")
+    tt(T.xk[:], T.BT[:].indirect(T.bl[:, 16:32]), T.wk[:], Op.add, "BT bl1 wk", "xk", c="g")
+    KB = [T.KB[:, 0:256], T.KB[:, 256:512], T.KB[:, 512:768], T.WB[:, 3 * 352 + 96:4 * 352], T.KB[:, 768:1024]]
+    act(KB[0], T.xk[:], Fn.Identity, "xk", "KB0", bias=1.0)
+    cp(T.rb[:], T.RP[:].indirect(T.bu[:]), "RP bu", "rb", c="g")
+
+    def gather(e, o, i, r, w):
+        if e == "V":
+            cp(o, i, r, w, c="g")
+        else:
+            act(o, i, Fn.Identity, r, w, c="g")
+
+    CH = PLAN["CH"]
+    yall = " ".join("y%d" % i for i in range(8)) + " yz"
+    xall = " ".join("x%d" % i for i in range(8))
+    DB = [(pa, "A0 A1"), (pb, "B0 B1"), (pc, "C0 C1")]
+    m = [T.m0[:, 64 * i:64 * i + 64] for i in range(5)]
+
+    for t in range(ST):
+        last, s = t == ST - 1, min(t, 1)
+        z, zk = (T.z0[:], " z0") if t == 0 else (T.zL[:, 256 * (t - 1):256 * t], " z%d" % t)
+        zh = [T.z0[:, 128 * h:128 * h + 128] if t == 0 else T.zL[:, 256 * (t - 1) + 128 * h:256 * (t - 1) + 128 * h + 128] for h in range(2)]
+        au, ak = T.aL[:, 16 * t:16 * t + 16], "a%d" % t
+        p0, PB, LT0, pt = (3 * 576 if last else 288 * t), (T.LT if last else T.PT), 576 * t, "PT%d" % t
+        cp(T.ra[:], T.RP[:].indirect(au), "RP " + ak, "ra", c="g")
+        for nm, buf, lst, lk in (("y", T.yy, T.rb, "X rb"), ("x", T.xx, T.ra, "X ra")):
+            i = 0
+            for piece in PLAN[nm][s].split():
+                j = i + int(piece[1:])
+                gather(piece[0], buf[:, 512 * i:512 * j], T.X[:, 0:V].indirect(lst[:, 32 * i:32 * j]), lk,
+                       " ".join("%s%d" % (nm, q) for q in range(i, j)))
+                i = j
+        ts(T.rbv[:], T.rb[:], -1536.0, Op.add, r="rb", w="rbv", c=0.5)
+        cp(T.af[:], au, ak, "af")
+        op("V", lambda t=t: g.vector.transpose(T.KT[:], KB[t]), 0.14, "KB%d" % t, "KT")
+        if not last:
+            send([(KB[t], [(rank + 1, T.WB[:, 352 * t + 96:352 * t + 352])], engines([rank + 1]))], "KB%d" % t, "WB%d" % t, "z", "sK%d" % t, ne)
+        for h in range(4):
+            mm([(pk[:, 256 + 16 * k + hh:256 + 16 * k + 16:2],
+                 [(T.PM[:, (2 * hh + e) * 128:(2 * hh + e + 1) * 128], T.KT[:, 16 * e + k::32]) for e in range(2)])
+                for k in range(4 * h, 4 * h + 4) for hh in range(2)], "KT", "K")
+        act(T.KL[:], pk[:, 256:512], Fn.Identity, "", "KL", "K", bias=-1.0)
+        mm([(pk[:, 256:512], [(Ih, z), (Iq, T.cm1[:]), (Ih, T.xx[:, 0::16])])], xall + zk, "K")
+        act(T.r32[:], pk[:, 256:512], Fn.Identity, "", "r32", "K", bias=MAGIC)
+        act(T.tt[:], T.r32[:], Fn.Identity, "r32", "tt", bias=-MAGIC)
+        for i in range(len(CH) - 1):
+            lo, hi = CH[i], CH[i + 1]
+            blk = range(lo // 32, (hi + 31) // 32)
+            dd, rl = T.dd[:, 16 * lo:16 * hi], T.rl[:, 16 * lo:16 * hi]
+            w0 = lo // 64
+            tt(dd, T.yy[:, 1024 * w0:1024 * w0 + 1024].indirect(T.offY[:, lo:hi]), T.xx[:, 16 * lo:16 * hi], Op.subtract,
+               "y%d y%d offY " % (2 * w0, 2 * w0 + 1) + " ".join("x%d" % q for q in blk), "d%d" % i, c="g")
+            if PLAN["r"][s][i] == "V":
+                ts(rl, dd, 0.0, Op.max, r="d%d" % i, w="r%d" % i, c=0.5)
+                mm([(pd[:, lo:hi], [(E(Zm, k), T.dd[:, 16 * lo + k:16 * hi:16]) for k in range(16)])], "d%d" % i, "D", end=False)
+                mm([(pd[:, lo:hi], [(E(Z2, k), T.rl[:, 16 * lo + k:16 * hi:16]) for k in range(16)])], "r%d" % i, "D", first=False)
+            else:
+                act(rl, dd, Fn.Abs, "d%d" % i, "r%d" % i)
+                mm([(pd[:, lo:hi], [(E(Z1, k), T.rl[:, 16 * lo + k:16 * hi:16]) for k in range(16)])], "r%d" % i, "D")
+        for j in range(4):
+            p, bk = DB[j % 3]
+            how = PLAN["z"][s][j]
+            az, ze = T.az[:, 1024 * j:1024 * j + 1024], T.ze[:, 1024 * j:1024 * j + 1024]
+            kp, kb = [(pk, "K"), (pb, "B0"), (pc, "C0"), (pa, "A0")][j]
+            head = [(I1, T.c32k[:, 64 * j:64 * j + 64]), (I1, T.KL[:, 64 * j:64 * j + 64])]
+            if how == "S":
+                for h in range(2):
+                    mm([(p[:, 256 * q + 128 * h:256 * q + 128 * h + 128], [(I1, T.xx[:, 2048 * h + 4 * j + q:2048 * h + 2048:16]), (Im, zh[h])])
+                        for q in range(4)], " ".join("x%d" % q for q in range(4 * h, 4 * h + 4)) + zk, bk)
+                act(az, p[:], Fn.Abs, "", "az%d" % j, bk)
+            else:
+                b1 = bk.split()[1]
+                mm([(p[:, 512:768], [(I1, z)])], zk, b1)
+                for q in range(4):
+                    tt(T.ze[:, 1024 * j + 256 * q:1024 * j + 256 * q + 256], T.xx[:, 4 * j + q::16], p[:, 512:768], Op.subtract, xall, "ze%d%d" % (j, q), b1)
+                zek = " ".join("ze%d%d" % (j, q) for q in range(4))
+                if how == "M":
+                    act(az, ze, Fn.Abs, zek, "az%d" % j)
+                else:
+                    ts(az, ze, 0.0, Op.max, 2.0, Op.mult, r=zek, w="az%d" % j, c=0.5)
+                    mm([(kp[:, 0:64], head + [(E(Zn, r), T.ze[:, 1024 * j + r:1024 * j + 1024:16]) for r in range(16)])], "KL " + zek, kb, end=False)
+            mm([(kp[:, 0:64], (head if how != "V" else []) + [(E(Zk, r), T.az[:, 1024 * j + r:1024 * j + 1024:16]) for r in range(16)])],
+               "KL az%d" % j, kb, first=how != "V")
+            if j == 0:
+                cp(m[0], kp[:, 0:64], "", "m0", kb)
+            else:
+                tt(m[j], kp[:, 0:64], m[j - 1], Op.min, "m%d" % (j - 1), "m%d" % j, kb)
+        act(T.sg[:], pd[:, 0:256], Fn.Sign, "thA", "sg", "D", bias=T.thA[:])
+        mm([(pd[:, 0:16], [(E(Z1, r), T.sg[:, r::16]) for r in range(16)])], "sg", "D")
+        mm([(pb[:, 512:768], [(T.BO[:], T.sg[:])])], "sg", "B1")
+        act(T.sB[:], pb[:, 512:768], Fn.Sign, "", "sB", "B1", bias=5.0)
+        ts(T.dv[:], pd[:, 0:16], -5.0, Op.is_gt, w="dv", b="D")
+        scan(T.cs[:], one, T.dv[:], 0.0, Op.mult, Op.add, "dv K1", "cs")
+        tt(T.t1[:], T.dv[:], c256, Op.mult, "dv K1", "t1")
+        mm([(pd[:, 0:16], [(T.BO[:], T.cs[:]), (T.Um[:], T.dv[:]), (Im, T.t1[:]), (I1, c255)]),
+            (pd[:, 16:17], [(T.BO[:], T.cs[:, 15:16])])], "cs dv t1", "D")
+        cp(PB[:, p0 + 16:p0 + 17], pd[:, 16:17], "", pt + "A", "D")
+        far = [1, 2, 3, 5] if last else [2, 3, 4]
+        send([(PB[:, p0 + 16:p0 + 18], [(rank + d, T.AF[:, 16 * t + 8 + 2 * i:16 * t + 10 + 2 * i]) for i, d in enumerate(far)],
+               engines([rank + d for d in far]))], pt + "A", "AFr", "A", "sA%d" % t, ne * len(far))
+        cp(T.off[:], pd[:, 0:16], "", "off", "D")
+        cp(PB[:, p0:p0 + 16], pd[:, 0:16], "", pt + "o", "D")
+        tt(PB[:, p0 + 32:p0 + 288].indirect(T.off[:]), KB[t], T.sg[:], Op.mult, "KB%d sg off" % t, pt + "p", c="s")
+        lt = "LT%d" % t
+        if last:
+            send([(PB[:, p0 + 16:p0 + 128], [(rank - 2, T.LT[:, LT0 + 304:LT0 + 416])], engines([rank - 2]))],
+                 "PT3A PT3p sndsA3", lt, "Q", "sQ3", ne)
+            lt += " PT3A PT3o PT3p"
+        else:
+            es = engines([rank + 1, rank - 1])
+            PT = T.PT[:, p0:p0 + 128]
+            send([(PT, [(rank + 1, T.LT[:, LT0:LT0 + 128])], es[:ne // 2]), (PT, [(rank - 1, T.LT[:, LT0 + 288:LT0 + 416])], es[ne // 2:])],
+                 "%sA %so %sp sndsA%d" % (pt, pt, pt, t), lt, "Q", "sQ%d" % t, ne)
+        cp(T.AF[:, 16 * t:16 * t + 1], pd[:, 16:17], "", "AF%d" % t, "D")
+        if not last:
+            cp(T.Ai[:, 0:1], pd[:, 16:17], "", "Ai0", "D")
+            ts(T.Ai[:, 1:2], T.Ai[:, 0:1], 31, Op.bitwise_and, r="Ai0", w="Ai1")
+            tt(T.thA[:], T.thf[:], T.Ai[:, 1:2], Op.subtract, "Ai1 thf", "thA")
+        ts(T.mar[:], T.dv[:], -1.0, Op.mult, 1.0, Op.add, r="dv", w="mar")
+        tt(m[4][:, 0:32], m[3][:, 0:32], m[3][:, 32:64], Op.min, "m3", "m4")
+        tt(T.vi[:], m[4][:, 0:16], m[4][:, 16:32], Op.min, "m4", "vi")
+        ts(T.Li[:, 16:32], T.vi[:], 15, Op.bitwise_and, r="vi", w="Li1")
+        ts(T.Li[:, 0:16], T.vi[:], 5, Op.arith_shift_right, 15, Op.bitwise_and, r="vi", w="Li0")
+        cp(T.Ku[:], T.Li[:, 16:32], "Li1", "Ku")
+        tt(T.Lj[:], T.Li[:], T.base[:], Op.add, "Li0 Li1 K1", "Lj")
+        cp(T.Lu[:], T.Lj[:], "Lj", "Lu")
+        tt(T.mm[:], T.ID[:].indirect(T.Ku[:]), T.rbv[:], Op.mult, "Ku rbv K1", "mm", c="g")
+        act(T.wk[:], T.yy[:].indirect(T.Lu[:, 16:32]), Fn.Identity, "Lu " + yall, "wk", c="g")
+        act(T.xk[:], T.xx[:].indirect(T.Lu[:, 0:16]), Fn.Identity, "Lu " + xall, "xk", c="g")
+        zn = T.zS[:, 256 * t:256 * t + 256]
+        mm([(pa[:, 0:256], [(Im, z), (I1, T.wk[:])])], "wk" + zk, "A0")
+        act(T.zm[:], pa[:, 0:256], Fn.Abs, "", "zm", "A0")
+        mm([(pa[:, 512:528], [(T.I4f[:], T.af[:])] + [(E(Zu, r), T.zm[:, r::16]) for r in range(16)])], "af zm", "A1", extra=192)
+        mm([(pa[:, 0:256], [(I1, T.tt[:]), (I256, T.sB[:])]), (pa[:, 256:512], [(I1, T.zm[:]), (Im256, T.sB[:])])], "tt sB zm", "A0")
+        act(T.zt[:], pa[:, 0:512], Fn.Relu, "", "zt", "A0", bias=-256.0)
+        mm([(pa[:, 0:256], [(I1, T.zt[:, 0:256]), (I1, T.zt[:, 256:512])])], "zt", "A0")
+        act(zn, pa[:, 0:256], Fn.Identity, "", "zn%d" % t, "A0")
+        tt(T.an1[:], pa[:, 512:528], T.mar[:], Op.mult, "mar", "an1", "A1")
+        tt(T.an2[:], T.an1[:], T.af[:], Op.add, "an1 af", "an2")
+        ts(T.an3[:], T.an2[:], 2047, Op.bitwise_and, r="an2", w="an3")
+        if not last:
+            cp(T.aS[:, 16 * t:16 * t + 16], T.an3[:], "an3", "aS%d" % t)
+            es = engines([rank + 1])
+            send([(T.aS[:, 16 * t:16 * t + 16], [(rank + 1, T.aL[:, 16 * t + 16:16 * t + 32])], es)], "aS%d" % t, "a%d" % (t + 1), "a", "sa%d" % t, ne)
+            send([(zn, [(rank + 1, T.zL[:, 256 * t:256 * t + 256])], es)], "zn%d sndsa%d" % (t, t), "z%d" % (t + 1), "z", "sz%d" % t, ne)
+        else:
+            cp(T.oa[:], T.an3[:], "an3", "oa")
+        mm([(pb[:, 0:256], [(T.BOh[:], T.mm[:])])], "mm", "B0", end=False)
+        mm([(pb[:, 0:256], [(I2k, T.sB[:])])], "sB", "B0", first=False)
+        mm([(pc[:, 512:528], [(I1, c1536)] + [(E(None, r), T.mm[:, r::16]) for r in range(16)])], "mm", "C1", end=False)
+        mm([(pc[:, 512:528], [(I4k, T.dv[:])])], "dv", "C1", first=False)
+        mm([(pc[:, 0:256], [(Iq, T.cm1[:]), (Ih, T.wk[:]), (Ih, T.xk[:])])], "wk xk", "C0")
+        act(T.r33[:], pc[:, 0:256], Fn.Identity, "", "r33", "C0", bias=MAGIC)
+        act(T.hf[:], T.r33[:], Fn.Identity, "r33", "hf", bias=-MAGIC)
+        tt(T.cB[:], pb[:, 0:256], T.cmask[:], Op.add, "K1", "cB", "B0")
+        cp(T.cL[:], pc[:, 512:528], "", "cL", "C1")
+        tt(T.cm[:], pc[:, 512:528], dum, Op.min, "K1", "cm", "C1")
+        tt(T.eq[:], T.cL[:].indirect(T.expl[:]), T.cB[:], Op.is_equal, "cL cB K1", "eq", c="g")
+        scan(T.sc[:], T.crst[:], T.eq[:], 0.0, Op.mult, Op.max, "eq K1", "sc")
+        tt(T.so[:], T.sc[:, 15::16], T.cm[:], Op.max, "sc cm", "so")
+        cp(T.su[:, 0::2], T.so[:], "so", "su")
+        for c in range(15, -1, -1):
+            cp(T.X[:].indirect(T.su[:, 2 * c:2 * c + 1]), T.hf[:, 16 * c:16 * c + 16], "su hf Xd", "X", c="s")
+        WB, aM, wbk = T.WB[:, 352 * t:352 * t + 352], T.WB[:, 352 * t:352 * t + 96], ("KB3" if last else "WB%d" % t)
+        act(aM, T.LT[:, LT0 + 320:LT0 + 416], Fn.Abs, lt, "aM")
+        act(T.aW[:], T.LT[:, LT0 + 32:LT0 + 128], Fn.Abs, lt, "aW")
+        op("V", lambda t=t, far=far: g.vector.tensor_reduce(T.nn[:, 0:1], T.AF[:, 16 * t:16 * t + 8 + 2 * len(far)], Ax.X, Op.min), 0.07,
+           "AFr AF%d" % t, "n0")
+        ts(T.nn[:, 1:2], T.nn[:, 0:1], T.LT[:, LT0 + 16:LT0 + 17], Op.min, T.LT[:, LT0 + 304:LT0 + 305], Op.min, r="n0 " + lt, w="n1")
+        ts(T.l1[:], T.LT[:, LT0:LT0 + 16], T.nn[:, 1:2], Op.is_ge, 512.0, Op.mult, r="n1 " + lt, w="l1")
+        tt(T.l2[:], T.l1[:], T.LT[:, LT0:LT0 + 16], Op.add, "l1 " + lt, "l2")
+        tt(T.l1[:], T.l2[:], c16i, Op.min, "l2 K1", "l1")
+        cp(T.l2u[:], T.l1[:], "l1", "l2u")
+        act(T.sn[:], WB.indirect(T.l2u[:]), Fn.Sign, "aM l2u " + wbk, "sn", bias=-16.5, c="g")
+        mm([(pc[:, 512:528], [(E(Zb, r), T.sn[:, r::16]) for r in range(16)])], "sn", "C1")
+        if last:
+            ts(T.ob[:], pc[:, 512:528], 32767.5, Op.add, w="ob", b="C1")
+        else:
+            ts(T.bu[:], pc[:, 512:528], 32767.5, Op.add, w="bu", b="C1")
+            cp(T.rb[:], T.RP[:].indirect(T.bu[:]), "RP bu", "rb", c="g")
+        sQ, sM = T.b16[:, 0:96], T.b16[:, 96:192]
+        act(sQ, T.aW[:, 0:96], Fn.Sign, "aW", "sQ", bias=-16.5)
+        act(sM, aM, Fn.Sign, "aM", "sM", bias=-16.5)
+        mm([(pd[:, 0:96], [(I1, T.LT[:, LT0 + 32:LT0 + 128]), (Im8, sQ)]), (pd[:, 128:224], [(I1, aM), (Im8, sM)])],
+           "aM sQ sM " + lt, "D")
+        act(T.uu[:], pd[:, 0:96], Fn.Relu, "", "uu", "D", bias=-8.0)
+        act(T.k2[:], pd[:, 128:224], Fn.Identity, "", "k2", "D", bias=-8.0)
+        act(T.u2[:], T.uu[:], Fn.Square, "uu", "u2")
+        for j in range(4):
+            p, bk = (pk, "K") if j % 2 == 0 else (pd, "D")
+            mm([(p[:, 96 * q:96 * q + 96], [(I1, T.k2[:]), (T.FA[:, 128 * (4 * j + q):128 * (4 * j + q) + 128], T.uu[:]),
+                                            (T.FB[:, 128 * (4 * j + q):128 * (4 * j + q) + 128], T.u2[:])]) for q in range(4)], "uu u2 k2 K2", bk)
+            act(T.TR[:, 384 * j:384 * j + 384], p[:, 0:384], Fn.Relu, "K2", "TR%d" % j, bk, bias=bq_)
+        mm([(pk[:, 0:96], [(Im, T.uu[:]), (I1, T.aW[:, 0:96]), (Im8, sQ), (I8, sM)] + [(E(Z1, k), T.TR[:, 96 * k:96 * k + 96]) for k in range(12)])],
+           "uu aW sQ sM TR0 TR1 TR2", "K", end=False)
+        mm([(pk[:, 0:96], [(E(Z1, k), T.TR[:, 96 * k:96 * k + 96]) for k in range(12, 16)])], "TR3", "K", first=False)
+        act(aM, pk[:, 0:96], Fn.Identity, "", "aM", "K")
+        act(KB[t + 1], WB.indirect(T.l2u[:]), Fn.Identity, "aM l2u " + wbk, "KB%d" % (t + 1), c="g")
+        if not last:
+            mm([(pd[:, 256:512], [(T.BO[:], T.c16l[:]), (Im8, T.sn[:]), (I1, KB[t + 1])])], "sn K2 KB%d" % (t + 1), "D")
+            ts(T.offY[:], pd[:, 256:512], -9.0, Op.add, w="offY", b="D")
+        else:
+            mm([(pd[:, 256:512], [(Im8, T.sn[:]), (I1, KB[4])])], "sn KB4", "D")
+            act(T.ok[:], pd[:, 256:512], Fn.Identity, "", "ok", "D", bias=-9.0)
+            for e, o, i, k, lat in (("Y", T.yz, zn, "zn3", 2.5), ("Y", T.ya, T.oa[:], "oa", 2.5), ("Y", T.yx, T.X[:, 0:V], "X", 5.5),
+                                    ("Y", T.yb, T.ob[:], "ob", 2.5), ("S", T.yk, T.ok[:], "ok", 2.5)):
+                dma(e, o[:], i, "out", k)
+                op("R", None, lat, "q" + e + "out", "")
+                wr.pop("q" + e + "out")
+                rd.pop("q" + e + "out")
+
+    if "order" not in ORDER:
+        ORDER["order"], ORDER["t"] = schedule(ops)
+    cnt = {"V": 0, "S": 0, "P": 0, "G": 0}
+    seen = {e: {} for e in Q}
+    for i in ORDER["order"]:
+        o = ops[i]
+        e = o["e"]
+        if e == "R":
+            continue
+        top = {}
+        for p, raw in o["pre"].items():
+            tok = ops[p]["tok"]
+            if tok and (raw or ops[p]["e"] != e):
+                top[tok[0]] = max(top.get(tok[0], 0), tok[1])
+        for k, n in top.items():
+            if seen[e].get(k, 0) < n:
+                Q[e].wait_ge(T.sem[k], n)
+                seen[e][k] = n
+        ins = o["f"]()
+        if ins is not None:
+            cnt[e] += 1
+            ins.then_inc(T.sem[e], 1)
+            o["tok"] = (e, cnt[e])
+    for k in cnt:
+        g.wait_ge(T.sem[k], cnt[k])
+    g.wait_ge(T.sem.sent, sent[0])
+    g.wait_ge(T.sem.out, 80)

@@ -5,7 +5,7 @@ N, V, L, ST = 6, 3072, 256, 4
 MAGIC = 12582912.0
 PLAN = {"y": ["V2 V2 V2 S2", "V1 S1 V2 V1 V1 S2"], "x": ["S1 V1 S2 S2 S2", "S2 S2 S2 S2"], "r": ["SVSV", "VSSV"], "CH": [0, 64, 128, 192, 256],
         "z": ["SSSS", "SSSS"], "rounds": 400, "seed": 1, "jit": 4, "tol": 0, "p": 0.02, "mix": 1.0}
-CY, PC, GA, SC, WAKE = 1.04e-3, 0.52e-3, 1.56, 3.8, 0.06
+CY, PC, GA, SC, WAKE = 0.83e-3, 0.417e-3, 1.56, 3.8, 0.2
 LAT = {"A": 5.0, "Q": 5.3, "a": 3.6, "z": 5.0, "small": 3.5, "RP": 9.0, "X": 13.0, "send": 0.6}
 
 

@@ -3,10 +3,32 @@ from concourse.mybir import AluOpType as Op, AxisListType as Ax, ActivationFunct
 
 N, V, L, ST = 6, 3072, 256, 4
 MAGIC = 12582912.0
-PLAN = {"y": ["V2 V2 V2 S2", "V1 S1 V2 V1 V1 S2"], "x": ["S1 V1 S2 S2 S2", "S2 S2 S2 S2"], "r": ["SVSV", "VSSV"], "CH": [0, 64, 128, 192, 256],
-        "z": ["SSSS", "SSSS"], "rounds": 400, "seed": 1, "jit": 4, "tol": 0, "p": 0.02, "mix": 1.0}
-CY, PC, GA, SC, WAKE = 0.83e-3, 0.417e-3, 1.56, 3.8, 0.2
-LAT = {"A": 5.0, "Q": 5.3, "a": 3.6, "z": 5.0, "small": 3.5, "RP": 9.0, "X": 13.0, "send": 0.6}
+QD = 4
+WQ = [16 * (q + 1) for q in range(QD)]
+RQ = {1: [0], 2: [0, 128], 4: [0, 64, 192, 512]}[QD]
+NB = 16 // QD
+NS = 2
+Y0 = V + 64 + 1536
+PLAN = {"rounds": 10000, "seed": 1, "alone": 0.15, "turn": 0.2, "jump": 6, "slack": 0.001}
+QUEUES = {
+    "V": """-mm -dv -cs -t1 -an -off -an3 -aS -oa -cL -PTp -Ai0 bs -hf -Ai1 bo rbo -thA -sc0 -sc3 -su2 -su1 -su0 -zl -su3 -X rbu -X:2 run0 -X:3 run1 -X:4 ra run2 y1
+            n17 run3 x6 x0 bn x2 nA gm OWo nB rbn l11 TR3 l12 x7 l13 KWn OWn qn af l2u ok ob n2 offY d3 d0 d5 bu d4 d1 d2 m0 r0 m1 d7 m2 d6 m3 bh m4 bl vi vj Lx mk
+            ZW1 rbv Lw""",
+    "S": """-ZW0 -PTA -cF -PTo -AF -ad0 -ad1 -ad2 -ad3 -ad4 -ad5 -ad6 -ad7 -ad8 -ad9 -ad10 -ad11 -ad12 -ad13 -ad14 -ad15 sq0 -zn OWy sq1 y0
+            m2 mo KWo aM x1 mM sM x3 TR0 TR1 kp x4 TR2 x5 n1 n0 cn code sn az0 az1 y3 y2 az2 az3 mp r1 r2 r3 wk xk sg""",
+    "P": """-ZW0 -dv -cs -mm -mm:2 -xk -cL -sg:2 -dv:3 -cL:2 -sg:3 -dv:4 -dv:2 E mp rbo rbo:2 rbo:3 rbo:4 mo mo:2 mM mM:2 sM mo:3 mM:3 mo:4 mM:4 TR0 TR1 TR2 TR3
+            x0 x4 x0:2 x4:2 sn x0:3 x4:3 az0 x0:4 x4:4 az1 az2 d0 az3 r0 d2 x0:5 r1 d4 r2 d6 r3 mk wk sg""",
+    "G": "-snda -sndQ -sndA -sndz sndE",
+}
+FIRST = {
+    "V": "rbo rbu ra run0 run1 x2 run2 run3 x0 af OWo x6 offY y1 d0 d1 d3 d5 d4 d2 d6 m1 r0 m2 d7 m3 bu bh m4 bl vi vj Lx mk ZW1 rbv Lw",
+    "S": "sq1 OWy sq0 x3 x1 x5 x7 x4 sn y2 az0 y0 az1 y3 m0 az2 az3 r1 r2 r3 wk xk sg",
+    "P": "mp rbo rbo:2 rbo:3 rbo:4 x0:2 x0 x4 sn x4:2 az0 x0:3 x4:3 x0:4 x4:4 az1 d0 az2 az3 r0 d2 x0:5 r1 d4 r2 d6 r3 mk wk sg",
+    "G": "sndE",
+}
+PACE = [(0.83e-3, 0.42e-3, 1.25, 3.8, 0.25, 0.2, 1.0, 112), (1.2e-3, 0.7e-3, 1.2, 3.0, 0.3, 0.25, 1.2, 160),
+        (1.1e-3, 0.55e-3, 2.0, 5.5, 0.3, 0.25, 1.2, 165), (0.95e-3, 0.47e-3, 1.5, 3.8, 0.3, 0.25, 2.0, 155)]
+LAT = {"far": 2.5, "row": 0.005, "byte": 1.5e-5, "small": 3.5, "RP": 9.0, "X": 13.0, "send": 0.6}
 
 
 def sb(n, dt="bfloat16"):
@@ -14,90 +36,185 @@ def sb(n, dt="bfloat16"):
 
 
 SCRATCH = {
-    "X": sb(V + L), "RP": sb(2048, "int32"), "xx": sb(4096), "yy": sb(4112), "dd": sb(4096), "rl": sb(4096), "az": sb(4096),
+    "X": sb(Y0 + 4096), "rbu": sb(256, "uint16"), "RP": sb(2048, "int32"), "xx": sb(4096), "dd": sb(4096), "rl": sb(4096), "az": sb(4096), "IDp": sb(4096),
+    "SEL": sb(2048, "float16"), "IB": sb(7 * 128), "drop": sb(4096), "run": sb(4096, "float32"),
     "avi": sb(16, "int32"), "bvi": sb(16, "int32"), "kci": sb(256, "int32"), "thi": sb(1, "int32"), "z0": sb(256),
     "J": sb(256, "float32"), "pci": sb(8, "int32"), "pcj": sb(8, "int32"), "col": sb(24, "float32"),
-    "IS": sb(10 * 128), "I4f": sb(128, "float32"), "BO": sb(128), "Um": sb(128), "BOh": sb(128, "float16"), "Zh": sb(144, "float16"),
-    "ZS": sb(7 * 144), "ze": sb(4096), "zm": sb(256), "FA": sb(2048), "FB": sb(2048), "BA": sb(128), "BB": sb(128), "PM": sb(512), "ID": sb(16), "IDf": sb(16, "float32"),
-    "tA": sb(256, "float32"), "tB": sb(256, "float32"), "tI": sb(256, "int32"), "tJ": sb(256, "int32"), "tC": sb(256, "float32"),
-    "cm1": sb(256), "c32k": sb(256), "c16l": sb(256), "cmask": sb(256, "float32"), "crst": sb(256, "float32"),
-    "cf": sb(64, "float32"), "cb": sb(48), "pw": sb(112, "float32"),
-    "base": sb(32, "int32"), "expl": sb(16, "uint16"), "BT": sb(96), "bl": sb(32, "uint16"), "bli": sb(32, "int32"),
-    "ra": sb(256, "uint16"), "rb": sb(256, "uint16"), "rbv": sb(256, "float16"), "offY": sb(256, "uint16"), "bu": sb(16, "uint16"),
-    "KB": sb(1024), "WB": sb(4 * 352), "KT": sb(256), "KL": sb(256), "sg": sb(256), "sB": sb(256), "tt": sb(256), "zt": sb(512), "r32": sb(256, "float32"),
-    "r33": sb(256, "float32"), "thA": sb(1, "float32"), "thf": sb(1, "float32"), "Ai": sb(2, "int32"), "dv": sb(16), "cs": sb(16), "t1": sb(16),
-    "off": sb(16, "uint16"), "af": sb(16, "float32"), "mar": sb(16, "float32"), "m0": sb(320, "float32"), "vi": sb(16, "int32"),
-    "Li": sb(32, "int32"), "Lj": sb(32, "int32"), "Lu": sb(32, "uint16"), "Ku": sb(16, "uint16"), "wk": sb(256), "xk": sb(256), "hf": sb(256),
-    "mm": sb(256, "float16"), "cB": sb(256, "float32"), "cL": sb(16, "float32"), "cm": sb(16, "float32"), "eq": sb(256, "float32"),
-    "sc": sb(256, "float32"), "so": sb(16, "float32"), "su": sb(32, "uint16"), "an1": sb(16, "float32"), "an2": sb(16, "int32"), "an3": sb(16, "int32"),
-    "nn": sb(2, "float32"), "l1": sb(16, "float32"), "l2": sb(16, "float32"), "l2u": sb(16, "uint16"), "aW": sb(96), "b16": sb(192), "sn": sb(256),
-    "uu": sb(96), "u2": sb(96), "k2": sb(96), "TR": sb(1536), "oa": sb(16, "float32"), "ob": sb(16, "float32"), "ok": sb(256),
-    "PT": sb(3 * 288), "LT": sb(4 * 576), "AF": sb(4 * 16), "aS": sb(3 * 16, "uint16"), "aL": sb(4 * 16, "uint16"), "zS": sb(4 * 256), "zL": sb(3 * 256),
+    "IS": sb(10 * 128), "IH": sb(2 * 128, "float16"), "I5f": sb(128, "float32"), "BO": sb(128), "BOm": sb(128), "Um": sb(128),
+    "BOh": sb(128, "float16"), "Zh": sb(144, "float16"),
+    "ZS": sb(6 * 144), "FA": sb(2048), "FB": sb(2048), "BA": sb(128), "BB": sb(128), "IDf": sb(16, "float32"),
+    "tA": sb(256, "float32"), "tB": sb(256, "float32"), "tI": sb(256, "int32"), "tJ": sb(256, "int32"), "tC": sb(256, "float32"), "tL": sb(256, "float32"),
+    "cm1": sb(256), "kA": sb(64), "kB": sb(256), "l1t": sb(256), "cj": sb(96, "float32"), "cf": sb(48, "float32"), "cb": sb(48), "pw": sb(112, "float32"),
+    "pos": sb(768, "float32"), "mask": sb(768), "crst": sb(768), "ad": sb(768), "sc": sb(768, "float32"),
+    "BT": sb(96), "bl": sb(32, "uint16"), "bli": sb(32, "int32"), "s0": sb(256), "s1": sb(256),
+    "an": sb(32, "int32"), "af": sb(16, "float32"), "bo": sb(16, "uint16"), "bu": sb(16, "uint16"), "bn": sb(16, "uint16"),
+    "ra": sb(256, "uint16"), "rbo": sb(256, "float16"), "rbn": sb(96, "uint16"), "rbv": sb(256, "float16"), "offY": sb(256, "uint16"),
+    "OW": sb(352, "float32"), "KW": sb(352), "ZW": sb(512), "sg": sb(256), "sn": sb(256), "dv": sb(16),
+    "thA": sb(1, "float32"), "thf": sb(1, "float32"), "Ai": sb(2, "int32"), "cs": sb(16), "t1": sb(16), "off": sb(16, "uint16"), "zl": sb(16, "uint16"),
+    "m0": sb(320, "float32"), "vi": sb(32, "int32"), "Lx": sb(16, "uint16"), "Lw": sb(16, "uint16"), "wk": sb(256), "xk": sb(256), "hf": sb(256),
+    "mk": sb(256), "mm": sb(256, "float16"), "cL": sb(16, "float16"), "cF": sb(16, "float32"), "su": sb(16, "uint16"),
+    "nn": sb(2, "float32"), "l1": sb(64, "float32"), "l2u": sb(16, "uint16"), "l2h": sb(16, "float16"),
+    "cq": sb(9 * 96), "TR": sb(1536), "oa": sb(16, "float32"), "ob": sb(16, "float32"), "ok": sb(256),
+    "PT": sb(3 * 288), "LT": sb(4 * 576), "AF": sb(4 * 16), "ES": sb(4 * 640), "EL": sb(3 * 640), "ZO": sb(4 * 256), "ZL": sb(3 * 256),
+    "aS": sb(3 * 16, "uint16"), "aL": sb(4 * 16, "uint16"),
     "pa": ("psum", [128, 1024], "float32"), "pb": ("psum", [128, 1024], "float32"), "pc": ("psum", [128, 1024], "float32"),
     "pd": ("psum", [128, 512], "float32"), "pk": ("psum", [128, 512], "float32"),
 }
 SEMAPHORES = (["V", "S", "P", "G", "ld0", "ld1", "ld2", "out", "sent"]
-              + ["%s%d" % (s, t) for s in ("sA", "sQ", "sa", "sz", "sK") for t in range(ST)])
+              + ["%s%d" % (s, t) for s in ("sA", "sQ", "sa", "sz", "sE") for t in range(ST)])
 ORDER = {}
 
 
-def place(eng, dur, pre, rank):
-    n = len(eng)
-    suc = [[] for _ in eng]
-    for i in range(n):
-        for p in pre[i]:
-            suc[p].append(i)
-    left = [len(p) for p in pre]
-    start, busy = [0.0] * n, {}
-    cand = sorted([(-rank[i], i) for i in range(n) if not left[i]])
-    while cand:
-        f = cand.pop()[1]
-        s = max([start[p] + dur[p] + lag for p, lag in pre[f].items()] + [0.0])
-        if eng[f] != "R":
-            b = busy.setdefault(eng[f], [])
-            k = len(b)
-            while k and b[k - 1][1] > s:
-                k -= 1
-            while k < len(b) and b[k][0] < s + dur[f] - 1e-9:
-                s = max(s, b[k][1])
-                k += 1
-            b.insert(k, (s, s + dur[f]))
-        start[f] = s
-        for k in suc[f]:
-            left[k] -= 1
-            if not left[k]:
-                cand.append((-rank[k], k))
-                cand.sort()
-    return start, max(start[i] + dur[i] for i in range(n))
+def listed(ops, tail):
+    places = [{}, {}]
+    for place, lists in zip(places, (QUEUES, FIRST)):
+        for e, s in lists.items():
+            for j, w in enumerate(s.split()):
+                name, nth = (w.lstrip("-").split(":") + ["1"])[:2]
+                place[e, name, int(nth)] = j + (1000 if w[0] == "-" else 0)
+    rank, eng = [], []
+    for o, left in zip(ops, tail):
+        keys = [(e, o["kind"][1], o["kind"][2]) for e in o["e"]]
+        place = places[o["step"] == 1 and any(k in places[1] for k in keys)]
+        e = ([k[0] for k in keys if k in place] + [o["e"][-1]])[0]
+        rank.append(1000 * o["step"] + place.get((e, o["kind"][1], o["kind"][2]), 999) if o["step"] else -left)
+        eng.append(e)
+    order = sorted(range(len(ops)), key=lambda i: (rank[i], i))
+    return {e: [i for i in order if eng[i] == e] for e in "VSPGY"}, eng
+
+
+def timing(ops, pace, can):
+    cy, pc, ga, sc, same, other, far, whole = pace
+    return [[0.0 if o["for"] and can[o["for"]] == "S" else c[0] + cy * (c[1] + ga * c[2] + sc * c[3]) + pc * c[4] + far * c[5]
+             for o, c in [(o, o["c"][k]) for o in ops]] for k in (0, -1)]
 
 
 def schedule(ops):
     n = len(ops)
-    eng, dur = [o["e"] for o in ops], [o["c"] for o in ops]
-    pre = [{p: WAKE if (eng[p] != o["e"] or raw) and eng[p] != "R" else 0.0 for p, raw in o["pre"].items()} for o in ops]
-    suc = [{} for _ in ops]
-    for i in range(n):
-        for p, lag in pre[i].items():
-            suc[p][i] = lag
-    tail = [0.0] * n
+    pre, suc, like = [list(o["pre"].items()) for o in ops], [[] for _ in ops], {}
+    for i, o in enumerate(ops):
+        for p, raw in pre[i]:
+            suc[p].append(i)
+        like.setdefault(o["kind"], {})[o["step"]] = i
+    tied, seed, count = {o["for"] for o in ops}, [PLAN["seed"]], [len(p) for p in pre]
+    none, same, other = (0.0,) * 4, tuple(p[4] for p in PACE), tuple(p[5] for p in PACE)
+
+    def rnd(k=1.0):
+        seed[0] = (seed[0] * 1103515245 + 12345) % 2147483648
+        return k * seed[0] / 2147483648
+
+    def times(eng):
+        tm = [timing(ops, p, eng) for p in PACE]
+        return [list(zip(*[d[k] for d in tm])) for k in (0, 1)]
+
+    def judge(seq, eng, tm):
+        left, at, order, go = list(count), {e: 0 for e in seq}, [], True
+        end, free, ready = [none] * n, {e: none for e in "VSPGYLR"}, []
+        while go:
+            go = False
+            for e, q in seq.items():
+                k = at[e]
+                while k < len(q) and not left[q[k]]:
+                    ready.append(q[k])
+                    k += 1
+                    while ready:
+                        f = ready.pop()
+                        order.append(f)
+                        x = eng[f]
+                        a, b, c, d = free[x]
+                        for p, raw in pre[f]:
+                            y = eng[p]
+                            u, v = end[p], (none if x in "RL" or y in "RL" else other if x != y else same if raw else none)
+                            if u[0] + v[0] > a:
+                                a = u[0] + v[0]
+                            if u[1] + v[1] > b:
+                                b = u[1] + v[1]
+                            if u[2] + v[2] > c:
+                                c = u[2] + v[2]
+                            if u[3] + v[3] > d:
+                                d = u[3] + v[3]
+                        u = tm[x == "S"][f]
+                        end[f] = (a + u[0], b + u[1], c + u[2], d + u[3])
+                        if x != "R":
+                            free[x] = end[f]
+                        for s in suc[f]:
+                            left[s] -= 1
+                            if not left[s] and eng[s] in "RL":
+                                ready.append(s)
+                go, at[e] = go or k > at[e], k
+        if len(order) < n:
+            return None
+        ts = [max(v) for v in zip(*end[-40:])]
+        return sum(t / p[7] for t, p in zip(ts, PACE)), seq, eng, tm, end, order, ts
+
+    def longest(state, k):
+        _, seq, eng, tm, end, order, ts = state
+        end = [v[k] for v in end]
+        start = [end[i] - tm[eng[i] == "S"][i][k] for i in range(n)]
+        before, last, way = {}, {}, []
+        for i in order:
+            before[i], last[eng[i]] = last.get(eng[i]), i
+        i = max(range(n), key=lambda i: end[i])
+        while start[i] > 1e-6:
+            p = before[i]
+            if eng[i] != "R" and p is not None and end[p] >= start[i] - 1e-6:
+                if p not in ops[i]["pre"] and eng[i] != "L":
+                    way.append((i, p))
+                i = p
+            else:
+                i = max([q for q, raw in pre[i]], key=lambda q: end[q] + (0.0 if eng[q] in "RL" else PACE[k][4 if eng[q] == eng[i] else 5]))
+        return way, start
+
+    dur, tail = timing(ops, PACE[0], [o["e"] for o in ops])[0], [0.0] * n
     for i in range(n - 1, -1, -1):
-        tail[i] = dur[i] + max([tail[k] + lag for k, lag in suc[i].items()] + [0.0])
-    rank, best, x = [-v for v in tail], None, PLAN["seed"]
-    for _ in range(PLAN["rounds"]):
-        start, t = place(eng, dur, pre, rank)
-        if best is None or t < best[1]:
-            best = (start, t)
-        elif t > best[1] + PLAN["tol"]:
-            start = best[0]
-        back, tb = place(eng, dur, suc, [-(start[i] + dur[i]) for i in range(n)])
-        rank = []
-        for i in range(n):
-            x = (x * 1103515245 + 12345) % 2147483648
-            u = x / 2147483648
-            rank.append(PLAN["mix"] * (tb - back[i] - dur[i]) + (1 - PLAN["mix"]) * start[i]
-                        + (PLAN["jit"] * (2 * u / PLAN["p"] - 1) if u < PLAN["p"] else 0.0))
-    ORDER["dbg"] = (ops, best[0], pre, max(tail))
-    return sorted(range(n), key=lambda i: (best[0][i], i)), best[1]
+        tail[i] = dur[i] + max([tail[k] + other[0] for k in suc[i]] + [0.0])
+    seq, eng = listed(ops, tail)
+    best = now = judge(seq, eng, times(eng))
+    ways = {}
+    for r in range(PLAN["rounds"]):
+        _, seq, eng, tm, end, order, ts = now
+        k = int(rnd(4))
+        if k not in ways:
+            ways[k] = longest(now, k)
+        way, start = ways[k]
+        b, a = way[int(rnd(len(way)))]
+        alone, how, seq = rnd() < PLAN["alone"], rnd(), dict(seq)
+        if how < PLAN["turn"]:
+            f = a if len(ops[a]["e"]) == 2 else b
+            if len(ops[f]["e"]) < 2:
+                continue
+            to, eng, shift = "S" if eng[f] == "V" else "V", list(eng), rnd(2.0) - 1.0
+            seq["V"], seq["S"] = list(seq["V"]), list(seq["S"])
+            for i in [f] if alone else like[ops[f]["kind"]].values():
+                if eng[i] != to:
+                    seq[eng[i]].remove(i)
+                    eng[i] = to
+                    j = 0
+                    while j < len(seq[to]) and start[seq[to][j]] < start[i] + shift:
+                        j += 1
+                    seq[to].insert(j, i)
+            if f in tied:
+                tm = times(eng)
+        else:
+            e, far, gap = eng[b], int(rnd() ** 3 * PLAN["jump"]), ops[b]["step"] - ops[a]["step"]
+            q = seq[e] = list(seq[e])
+            for s, i in [(ops[b]["step"], b)] if alone else like[ops[b]["kind"]].items():
+                j = a if i == b else like[ops[a]["kind"]].get(s - gap)
+                if j is None or eng[i] != e or eng[j] != e:
+                    continue
+                if how < (1 + PLAN["turn"]) / 2:
+                    q.remove(i)
+                    q.insert(max(0, q.index(j) - far), i)
+                else:
+                    q.remove(j)
+                    q.insert(q.index(i) + 1 + far, j)
+        new = judge(seq, eng, tm)
+        if new and new[0] <= now[0] * (1 + PLAN["slack"] * (1 - r / PLAN["rounds"]) * rnd()):
+            now, ways = new, {}
+            if new[0] < best[0]:
+                best = new
+    ORDER["ops"], ORDER["best"] = ops, best
+    return best[5], best[2], best[6]
 
 
 def rank_program(g, core, T, topo):
@@ -105,11 +222,12 @@ def rank_program(g, core, T, topo):
     if rank is None:
         return
     Q = {"V": g.vector, "S": g.scalar, "P": g.tensor, "G": g, "Y": g.sync}
-    ops, wr, rd, bank, alias = [], {}, {}, {}, {"K1": [], "K2": []}
-    sent = [0]
+    ops, wr, rd, bank, alias = [], {}, {}, {}, {"K1": [], "K2": [], "K3": [], "K4": []}
+    sent, step, kinds = [0], [0], {}
 
-    def op(e, f, c, r="", w="", b="", tok=None):
+    def op(e, f, c, r="", w="", b="", tok=None, serves=None):
         i = len(ops)
+        f, c = (f, c) if len(e) == 2 else ([f], [c])
         pre = {}
         ws = []
         for k in w.split():
@@ -132,11 +250,17 @@ def rank_program(g, core, T, topo):
         for k in ws:
             wr[k], rd[k] = [i], []
         pre.pop(i, None)
-        ops.append({"e": e, "f": f, "c": c, "pre": pre, "tok": tok, "w": w or r})
+        name = (w or r or "-").split()[0].split("@")[0]
+        kinds[e, name, step[0]] = kinds.get((e, name, step[0]), 0) + 1
+        ops.append({"e": e, "f": f, "c": c, "pre": pre, "tok": tok, "w": w or r, "for": serves, "step": step[0],
+                    "kind": (e, name, kinds[e, name, step[0]], min(step[0], 2))})
+
+    def fixed(v):
+        return (v, 0, 0, 0, 0, 0)
 
     def cost(out, per):
         n = out.shape[1]
-        return {"g": 0.065 + n * GA * CY, "s": 0.065 + n * SC * CY}[per] if per in ("g", "s") else max(64, n * per) * CY
+        return {"g": (0.06, 0, n, 0, 0, 0), "s": (0.06, 0, 0, n, 0, 0)}[per] if per in ("g", "s") else (0, max(64, n * per), 0, 0, 0, 0)
 
     def ts(out, in0, s1, o0, s2=None, o1=None, r="", w="", b="", c=1):
         if o1 is None:
@@ -153,20 +277,33 @@ def rank_program(g, core, T, topo):
     def act(out, a, fn, r="", w="", b="", bias=0.0, scale=1.0, c=1):
         op("S", lambda: g.scalar.activation(out, a, fn, bias=bias, scale=scale), cost(out, c), r, w, b)
 
-    def scan(out, a, x, ini, o0, o1, r, w):
-        op("V", lambda: g.vector.tensor_tensor_scan(out, a, x, ini, o0, o1), cost(out, 1), r, w)
+    def lin(out, a, r="", w="", b="", bias=0.0, scale=1.0, c=1, relu=False):
+        def v():
+            if relu:
+                return g.vector.tensor_scalar(out, a, bias, 0.0, Op.add, Op.max)
+            if bias == 0.0 and scale == 1.0:
+                return g.vector.tensor_copy(out, a)
+            return g.vector.tensor_scalar(out, a, scale, bias, Op.mult, Op.add)
+        op("VS", [v, lambda: g.scalar.activation(out, a, Fn.Relu if relu else Fn.Identity, bias=bias, scale=scale)],
+           [cost(out, c), cost(out, 1 if c == 0.5 else c)], r, w, b)
+
+    def scan(out, a, x, ini, o0, o1, r, w, b=""):
+        op("V", lambda: g.vector.tensor_tensor_scan(out, a, x, ini, o0, o1), cost(out, 1), r, w, b)
 
     def ms(ap, v, w):
         op("V", lambda: g.vector.memset(ap, v), cost(ap, 0.5), w=w)
 
-    def mm(groups, r="", b="", first=True, end=True, extra=0):
+    def iota(out, pattern, w, base=0):
+        op("G", lambda: g.iota(out, pattern, base, 0, allow_small_or_imprecise_dtypes=True), (0.13, 2 * out.shape[1], 0, 0, 0, 0), w=w)
+
+    def mm(groups, r="", b="", first=True, end=True, one=False):
         def f():
             ins = None
-            for out, terms in groups:
+            for n, (out, terms) in enumerate(groups):
                 for i, (a, c) in enumerate(terms):
-                    ins = g.tensor.matmul(out, a, c, first and i == 0, end and i == len(terms) - 1)
+                    ins = g.tensor.matmul(out, a, c, first and i == 0 and not (one and n), end and i == len(terms) - 1 and not (one and n < len(groups) - 1))
             return ins
-        op("P", f, PC * (extra + sum(max(64, o.shape[1]) * len(x) for o, x in groups)), r + " K1", "", b)
+        op("P", f, (0, 0, 0, 0, sum(max(64, o.shape[1]) * len(x) for o, x in groups), 0), r + " K1", "", b)
 
     def dst(h):
         a = topo.addr(T.cores[h % N])
@@ -178,117 +315,146 @@ def rank_program(g, core, T, topo):
             out = [e for e in out if e in topo.engines(core, T.cores[h % N])]
         return out
 
-    def send(transfers, r, name, kind, sem, count):
+    def send(transfers, r, name, kind, t, count):
+        sem = "s%s%d" % (kind, t)
+
         def f():
             g.remote_dma_fused([RemoteDMATransfer(dst_ids=[dst(h) for h, _ in ds], dma_engine_mask=sum(1 << e for e in es), remote_sem=T.sem[sem],
                                                   srcs=[src], dsts=[d for _, d in ds]) for src, ds, es in transfers], local_sem=T.sem.sent)
         sent[0] += sum(len(x[2]) for x in transfers)
-        op("G", f, LAT["send"], r, "snd" + sem)
-        op("R", None, LAT[kind], "snd" + sem, name, tok=(sem, count))
+        op("G", f, fixed(LAT["send"]), r, "snd%s@%d" % (kind, t))
+        rows = 128 * sum(len(x[1]) for x in transfers)
+        op("L", None, (0, 0, 0, 0, 0, rows * (LAT["row"] + LAT["byte"] * 2 * transfers[0][0].shape[1])), "snd%s@%d" % (kind, t), "fly%s@%d" % (kind, t))
+        op("R", None, (0, 0, 0, 0, 0, LAT["far"]), "fly%s@%d" % (kind, t), name, tok=(sem, count))
 
     def dma(e, o, i, sem, r=""):
         def f():
             Q[e].dma_start(o, i).then_inc(T.sem[sem], 16)
-        op(e, f, 0.1, r, "q" + e + sem)
+        op(e, f, fixed(0.1), r, "q" + e + sem)
+
+    def names(nm, i, j):
+        return " ".join("%s%d" % (nm, q) for q in range(i, j))
 
     ne = len(engines([rank + 1]))
     pa, pb, pc, pd, pk = T.pa, T.pb, T.pc, T.pd, T.pk
     col, J = T.col, T.J
-    kc_, gc_, pc_, hc_, zc_, w2_, wb_, wi_, bq_, k4_ = [col[:, i:i + 1] for i in range(10)]
-    I1, Im, I256, Ih, Iq, Im256, I4k, Im8, I8, I2k = [T.IS[:, 128 * i:128 * i + 128] for i in range(10)]
-    Z1, Z2, Zm, Zk, Zu, Zb, Zn = range(7)
-    lL, dum, one, c16i = [T.cf[:, 16 * i:16 * i + 16] for i in range(4)]
-    c256, c255, c1536 = [T.cb[:, 16 * i:16 * i + 16] for i in range(3)]
+    kc_, gc_, pc_, zc_, w2_, wb_, wi_, bq_, k4_, k16_ = [col[:, i:i + 1] for i in range(10)]
+    dum_, lim_ = [col[:, 10 + q:11 + q] for q in range(QD)], [col[:, 14 + q:15 + q] for q in range(QD)]
+    I1, Im, I256, Ih, Iq, I16, Ibig, I4k, Im32, Im17 = [T.IS[:, 128 * i:128 * i + 128] for i in range(10)]
+    H1, H16 = T.IH[:, 0:128], T.IH[:, 128:256]
+    Z1, Z2, Zm, Zk, Zu, Zb = range(6)
+    lL, one, l96 = [T.cf[:, 16 * i:16 * i + 16] for i in range(3)]
+    c256, c255, lane = [T.cb[:, 16 * i:16 * i + 16] for i in range(3)]
 
     def E(z, r):
         return T.Zh[:, 15 - r:143 - r] if z is None else T.ZS[:, 144 * z + 15 - r:144 * z + 143 - r]
 
-    for o, i in ((T.avi, T.av), (T.bvi, T.bv), (T.kci, T.kc), (T.z0, T.zs), (T.thi, T.th)):
-        dma("Y", o[:], i[:], "ld0")
-    dma("Y", T.RP[:], T.rp[:], "ld1", "qYld0")
-    dma("Y", T.X[:, 0:V], T.ph[:], "ld2", "qYld1")
-    op("R", None, LAT["small"], "qYld0", "avi bvi kci z0 thi", tok=("ld0", 80))
-    op("R", None, LAT["RP"], "qYld1", "RP", tok=("ld1", 16))
-    op("R", None, LAT["X"], "qYld2", "X", tok=("ld2", 16))
+    def to_list(z, x):
+        return [(E(z, r), x[:, r::16]) for r in range(16)]
 
-    op("G", lambda: g.iota(T.pci[:, 0:1], [[0, 1]], 0, 1), 0.15, w="pci")
-    op("G", lambda: g.iota(J[:], [[1, 256]], 0, 0, allow_small_or_imprecise_dtypes=True), 0.65, w="J")
-    op("G", lambda: g.iota(T.tA[:], [[1, 16], [0, 16]], 0, 0, allow_small_or_imprecise_dtypes=True), 0.65, w="tA")
-    op("G", lambda: g.iota(T.tB[:], [[0, 16], [1, 16]], 0, 0, allow_small_or_imprecise_dtypes=True), 0.65, w="tB")
-    ms(T.yy[:, 4096:4112], 0.0, "yz")
-    ms(T.X[:, V:V + L], 0.0, "Xd")
-    ms(T.PT[:], 96.0, "PT0A PT1A PT2A PT0o PT1o PT2o PT0p PT1p PT2p")
-    ms(T.LT[:, 3 * 576:3 * 576 + 304], 96.0, "PT3A PT3o PT3p")
+    def ends(buf, q):
+        return buf[:, RQ[q] + WQ[q] - 1:RQ[q] + NB * WQ[q]:WQ[q]]
+
+    dma("Y", T.RP[:], T.rp[:], "ld1")
+    dma("Y", T.X[:, 0:V], T.ph[:], "ld2", "qYld1")
+    for o, i in ((T.avi, T.av), (T.bvi, T.bv), (T.kci, T.kc), (T.z0, T.zs), (T.thi, T.th)):
+        dma("S", o[:], i[:], "ld0")
+    op("R", None, fixed(LAT["small"]), "qSld0", "avi bvi kci z@0 thi", tok=("ld0", 80))
+    op("R", None, fixed(LAT["RP"]), "qYld1", "RP", tok=("ld1", 16))
+    op("R", None, fixed(LAT["X"]), "qYld2", "X", tok=("ld2", 16))
+
+    op("G", lambda: g.iota(T.pci[:, 0:1], [[0, 1]], 0, 1), fixed(0.15), w="pci")
+    iota(J[:], [[1, 256]], "J")
+    iota(T.tA[:], [[1, 16], [0, 16]], "tA")
+    iota(T.tB[:], [[0, 16], [1, 16]], "tB")
+    iota(T.X[:, V:Y0], [[0, Y0 - V]], "Xd n0 n1 n2")
+    iota(T.l1t[:], [[1, 256]], "K4", 1)
+    iota(T.PT[:], [[0, 3 * 288]], " ".join("PT%s@%d" % (k, t) for k in "Aop" for t in range(ST - 1)), 96)
+    ms(T.LT[:, 3 * 576:3 * 576 + 304], 96.0, "PTA@3 PTo@3 PTp@3")
     for t in range(ST):
-        ms(T.AF[:, 16 * t:16 * t + 8], 96.0, "AF%d" % t)
+        ms(T.AF[:, 16 * t:16 * t + 8], 96.0, "AF@%d" % t)
     ms(T.cm1[:], -1.0, "K1")
     ms(one, 1.0, "K1")
-    ms(c1536, 1536.0, "K1")
-    ms(T.su[:], 0, "su")
+    iota(T.ad[:], [[0, 768]], names("ad", 0, 16))
     ts(T.pcj[:, 0:1], T.pci[:, 0:1], 15, Op.bitwise_and, r="pci", w="pj0")
     ts(T.pcj[:, 1:2], T.pci[:, 0:1], 4, Op.arith_shift_right, r="pci", w="pj1")
-    ts(T.pcj[:, 3:4], T.pci[:, 0:1], 4, Op.arith_shift_right, 1, Op.bitwise_and, r="pci", w="pj3")
     cp(T.pcj[:, 2:3], T.pci[:, 0:1], "pci", "pj2")
-    cp(col[:, 0:4], T.pcj[:, 0:4], "pj0 pj1 pj2 pj3", "kc gc pc hc")
+    cp(col[:, 0:3], T.pcj[:, 0:3], "pj0 pj1 pj2", "kc gc pc")
     ts(zc_, gc_, 16.0, Op.mult, 15.0, Op.add, r="gc", w="zc")
     ts(w2_, kc_, 2.0, Op.mult, 1.0, Op.add, r="kc", w="w2")
+    ts(k16_, kc_, 16.0, Op.mult, r="kc", w="k16")
     ts(T.IDf[:], J[:, 0:16], kc_, Op.is_equal, r="J kc", w="IDf")
-    cp(T.ID[:], T.IDf[:], "IDf", "K1")
     pw = [T.pw[:, 16 * i:16 * i + 16] for i in range(7)]
     ms(pw[0], 2.0, "pw0")
     ms(pw[1], 0.5, "pw1")
     ms(pw[2], 0.0, "pw2")
     scan(pw[3], pw[0], pw[2], 0.25, Op.mult, Op.add, "pw0 pw2", "pw3")
     scan(pw[4], pw[1], pw[2], 65536.0, Op.mult, Op.add, "pw1 pw2", "pw4")
-    tt(pw[5], pw[3], T.IDf[:], Op.mult, "pw3 IDf", "pw5")
+    tt(pw[5][:, 0:11], pw[3][:, 0:11], T.IDf[:, 0:11], Op.mult, "pw3 IDf", "pw5")
     tt(pw[6], pw[4], T.IDf[:], Op.mult, "pw4 IDf", "pw6")
-    op("V", lambda: g.vector.tensor_reduce(wb_, pw[5], Ax.X, Op.add), 0.07, "pw5", "wb")
-    op("V", lambda: g.vector.tensor_reduce(wi_, pw[6], Ax.X, Op.add), 0.07, "pw6", "wi")
+    op("V", lambda: g.vector.tensor_reduce(wb_, pw[5][:, 0:11], Ax.X, Op.add), cost(wb_, 1), "pw5", "wb")
+    op("V", lambda: g.vector.tensor_reduce(wi_, pw[6], Ax.X, Op.add), cost(wi_, 1), "pw6", "wi")
     ts(I1, J[:, 0:128], pc_, Op.is_equal, r="J pc", w="I1 K1")
-    for buf, v in ((Im, -1.0), (I256, 256.0), (Ih, 0.5), (Iq, 0.25), (Im256, -256.0), (I4k, 4096.0), (I2k, 2048.0), (Im8, -8.0), (I8, 8.0), (T.I4f[:], 4.0)):
+    for buf, v in ((Im, -1.0), (I256, 256.0), (Ih, 0.5), (Iq, 0.25), (I16, 16.0), (T.I5f[:], 5.0), (Ibig, -131072.0), (I4k, 4096.0), (Im32, -32.0), (Im17, -17.0)):
         act(buf, I1, Fn.Identity, "I1", "K1", scale=v)
+    for buf, v in ((H1, 1.0), (H16, 16.0)):
+        ts(buf, I1, v, Op.mult, r="I1", w="K1", c=0.5)
     ts(T.ZS[:, 0:144], J[:, 0:144], zc_, Op.is_equal, r="J zc", w="Z1 K1")
     ts(T.Zh[:], J[:, 0:144], zc_, Op.is_equal, r="J zc", w="K1")
-    for zi, v in ((Z2, 2.0), (Zm, -1.0), (Zk, 512.0), (Zn, -512.0), (Zu, w2_), (Zb, wb_)):
+    for zi, v in ((Z2, 2.0), (Zm, -1.0), (Zk, 4096.0), (Zu, w2_), (Zb, wb_)):
         act(T.ZS[:, 144 * zi:144 * zi + 144], T.ZS[:, 0:144], Fn.Identity, "Z1 w2 wb", "K1", scale=v)
     ts(T.BO[:], T.tA[:, 0:128], gc_, Op.is_equal, r="tA gc", w="BO K1")
     ts(T.BOh[:], T.tA[:, 0:128], gc_, Op.is_equal, r="tA gc", w="K1")
+    act(T.BOm[:], T.BO[:], Fn.Identity, "BO", "K1", scale=-1.0)
     ts(T.tC[:, 0:128], T.tB[:, 0:128], kc_, Op.is_lt, -1.0, Op.mult, r="tB kc", w="tC")
     tt(T.Um[:], T.tC[:, 0:128], T.BO[:], Op.mult, "tC BO", "K1")
-    ts(lL, J[:, 0:16], 16.0, Op.mult, kc_, Op.add, r="J kc", w="lL")
+    ts(lL, J[:, 0:16], 16.0, Op.mult, kc_, Op.add, r="J kc", w="lL K1")
     ts(c256, lL, -1.0, Op.mult, 256.0, Op.add, r="lL", w="K1")
     ts(c255, lL, -1.0, Op.mult, 255.0, Op.add, r="lL", w="K1")
-    ts(dum, lL, float(V), Op.add, r="lL", w="dum K1")
-    ts(c16i, lL, 96.0, Op.add, r="lL", w="K1")
-    ts(T.base[:, 16:32], lL, 16.0, Op.mult, r="lL", w="K1")
-    ts(T.base[:, 0:16], lL, 16.0, Op.mult, r="lL", w="K1")
-    cp(T.expl[:], J[:, 0:16], "J", "K1")
-    act(T.c32k[:], T.tA[:], Fn.Identity, "tA", "K1", scale=32.0)
-    ts(T.r32[:], T.tB[:], kc_, Op.is_ge, 16384.0, Op.mult, r="tB kc", w="r32")
-    act(T.cmask[:], T.r32[:], Fn.Identity, "r32", "K1", bias=3584.0)
-    ts(T.crst[:], T.tB[:], 0.5, Op.is_gt, r="tB", w="crst")
-    cp(T.crst[:, 15::16], dum, "dum crst", "crst K1")
+    cp(lane, lL, "lL", "K1")
+    ts(l96, lL, 96.0, Op.add, r="lL", w="K1")
+    act(T.kA[:], T.tB[:, 0:64], Fn.Identity, "tB", "K1", scale=256.0)
+    act(T.kB[:], T.tA[:], Fn.Identity, "tA k16", "K1", bias=k16_)
+    act(T.cj[:], J[:, 0:96], Fn.Identity, "J", "K2", bias=V + 64 + 16 - 1536.0, scale=16.0)
+    ts(T.IDp[:, 0:256], T.tB[:], kc_, Op.is_equal, r="tB kc", w="ID0 K3")
+    for lo in (256, 512):
+        cp(T.IDp[:, lo:2 * lo], T.IDp[:, 0:lo], "ID0 ID%d" % (lo - 256), "ID%d K3" % lo, c=0.5)
+    for lo in range(1024, 4096, 1024):
+        lin(T.IDp[:, lo:lo + 1024], T.IDp[:, 0:1024], "ID512", "K3", c=0.5)
+    for r in range(16):
+        ts(T.SEL[:, 128 * r:128 * r + 128], T.BO[:], T.IDf[:, r:r + 1], Op.mult, r="BO IDf", w="K4", c=0.5)
+    for j in range(7):
+        lin(T.IB[:, 128 * j:128 * j + 128], I1, "I1", "K4", scale=8192.0 * (7 - j), c=0.5)
     for h in range(2):
-        ts(col[:, 10 + h:11 + h], hc_, float(h), Op.is_equal, r="hc", w="hs%d" % h)
-        for e in range(2):
-            q = 2 * h + e
-            ts(col[:, 12 + q:13 + q], pc_, float(16 * (e - h)), Op.add, r="pc", w="ps%d" % q)
-            ts(T.PM[:, q * 128:q * 128 + 128], J[:, 0:128], col[:, 12 + q:13 + q], Op.is_equal, col[:, 10 + h:11 + h], Op.mult,
-               r="J ps%d hs%d" % (q, h), w="K1")
-    op("G", lambda: g.iota(T.cB[:], [[0, 4], [256, 4], [0, 16]], 0, 0, allow_small_or_imprecise_dtypes=True), 0.65, w="cB")
-    ts(T.r33[:], T.cB[:], T.IDf[:, 0:1], Op.mult, r="cB IDf", w="r33")
-    ts(T.eq[:], T.tB[:], T.IDf[:, 1:2], Op.mult, 16.0, Op.mult, r="tB IDf", w="eq")
-    tt(T.c16l[:], T.r33[:], T.eq[:], Op.add, "r33 eq", "K2")
-    act(T.tC[:, 128:256], T.tB[:, 0:128], Fn.Identity, "tB", "tD", bias=32.0, scale=32.0)
+        iota(T.drop[:, 2048 * h:2048 * h + 512 * NS], [[0, 64 * NS], [-8192, 8]], "sq%d" % h, 4096 * (31 - 16 * h))
+    for q in range(QD):
+        reg = slice(RQ[q], RQ[q] + NB * WQ[q])
+        iota(T.pos[:, reg], [[0, NB], [1, WQ[q]]], "pos%d" % q)
+        ts(lim_[q], kc_, 16.0 * q, Op.add, r="kc", w="lim%d" % q)
+        ts(dum_[q], kc_, float(V + 16 * q), Op.add, r="kc", w="K1")
+        ts(T.sc[:, reg], T.pos[:, reg], lim_[q], Op.is_ge, -59.0, Op.mult, r="pos%d lim%d" % (q, q), w="sc%d" % q)
+        act(T.mask[:, reg], T.sc[:, reg], Fn.Identity, "sc%d" % q, "mask%d" % q, bias=-5.0)
+        ms(ends(T.mask, q), 1536.0, "mask%d K3" % q)
+        ts(T.crst[:, reg], T.pos[:, reg], 0.5, Op.is_gt, r="pos%d" % q, w="crst%d" % q)
+        ms(ends(T.crst, q), 4096.0, "crst%d K3" % q)
+    act(T.tC[:, 128:256], T.tB[:, 0:128], Fn.Identity, "tB", "tD", bias=512.0, scale=-32.0)
     tt(T.BA[:], T.tC[:, 128:256], T.BO[:], Op.mult, "tD BO", "BA")
     act(T.BB[:], T.BO[:], Fn.Identity, "BO", "BB", scale=-16.0)
-    ts(k4_, kc_, 1.0, Op.add, 4.0, Op.mult, r="kc", w="k4")
+    ts(k4_, kc_, -16.0, Op.add, 4.0, Op.mult, r="kc", w="k4")
     ts(bq_, k4_, k4_, Op.mult, -1.0, Op.mult, r="k4", w="K2")
     for k in range(16):
         act(T.FA[:, 128 * k:128 * k + 128], T.BA[:], Fn.Identity, "BA IDf", "K2", scale=T.IDf[:, k:k + 1])
-        ts(T.FB[:, 128 * k:128 * k + 128], T.BB[:], T.IDf[:, k:k + 1], Op.mult, r="BB IDf", w="K2", c=0.5)
-    cp(T.aL[:, 0:16], T.avi[:], "avi", "a0")
-    cp(T.bu[:], T.bvi[:], "bvi", "bu")
+        op("VS", [lambda k=k: g.vector.tensor_scalar(T.FB[:, 128 * k:128 * k + 128], T.BB[:], T.IDf[:, k:k + 1], None, Op.mult),
+                  lambda k=k: g.scalar.activation(T.FB[:, 128 * k:128 * k + 128], T.BB[:], Fn.Identity, scale=T.IDf[:, k:k + 1])],
+           [cost(T.BB, 0.5), cost(T.BB, 1)], "BB IDf", "K2")
+
+    def planes(buf, o):
+        return [buf[:, o + 352:o + 608], buf[:, o + 608:o + 624], buf[:, o + 624:o + 640], buf[:, o + 96:o + 352], buf[:, o:o + 352], buf[:, o + 96:o + 640]]
+
+    ES = [planes(T.ES, 640 * t) for t in range(ST)]
+    EL = [planes(T.EL, 640 * t) for t in range(ST - 1)]
+    cp(T.aL[:, 0:16], T.avi[:], "avi", "a@0")
+    cp(T.bo[:], T.bvi[:], "bvi", "bo")
     ts(T.bli[:, 0:16], T.bvi[:], 63, Op.bitwise_and, r="bvi", w="bli0")
     ts(T.bli[:, 16:32], T.bvi[:], 6, Op.arith_shift_right, r="bvi", w="bli1")
     cp(T.bl[:, 0:16], T.bli[:, 0:16], "bli0", "bl0")
@@ -296,231 +462,249 @@ def rank_program(g, core, T, topo):
     ts(T.tI[:, 0:64], J[:, 0:64], wi_, Op.mult, r="J wi", w="tI0")
     ts(T.tI[:, 64:96], J[:, 0:32], wi_, Op.mult, 64.0, Op.mult, r="J wi", w="tI1")
     ts(T.tI[:, 96:192], T.tI[:, 0:96], 15, Op.arith_shift_right, 1, Op.bitwise_and, r="tI0 tI1", w="tI2")
-    ts(T.BT[:], T.tI[:, 96:192], 16.0, Op.mult, r="tI2", w="BT")
+    ts(T.BT[:], T.tI[:, 96:192], 2.0, Op.mult, r="tI2", w="BT")
     ts(T.thf[:], T.thi[:], -1.0, Op.mult, -0.5, Op.add, r="thi", w="thf")
     ts(T.thA[:], T.thi[:], -1.0, Op.mult, -0.5, Op.add, r="thi", w="thA")
-    op("G", lambda: g.iota(T.sc[:], [[0, 4], [16, 64]], 0, 0, allow_small_or_imprecise_dtypes=True), 0.65, w="sc")
-    tt(T.tJ[:], T.sc[:], T.kci[:], Op.add, "sc kci", "tJ")
-    cp(T.offY[:], T.tJ[:], "tJ", "offY")
-    tt(T.wk[:], T.BT[:].indirect(T.bl[:, 0:16]), T.kci[:], Op.add, "BT bl0 kci", "wk", c="g")
-    tt(T.xk[:], T.BT[:].indirect(T.bl[:, 16:32]), T.wk[:], Op.add, "BT bl1 wk", "xk", c="g")
-    KB = [T.KB[:, 0:256], T.KB[:, 256:512], T.KB[:, 512:768], T.WB[:, 3 * 352 + 96:4 * 352], T.KB[:, 768:1024]]
-    act(KB[0], T.xk[:], Fn.Identity, "xk", "KB0", bias=1.0)
-    cp(T.rb[:], T.RP[:].indirect(T.bu[:]), "RP bu", "rb", c="g")
+    act(T.s0[:], T.BT[:].indirect(T.bl[:, 0:16]), Fn.Identity, "BT bl0", "s0", bias=-1.0, c="g")
+    tt(T.s1[:], T.BT[:].indirect(T.bl[:, 16:32]), T.s0[:], Op.add, "BT bl1 s0", "s1", c="g")
+    ts(ES[0][0], T.kci[:], -1.0, Op.mult, 16.0, Op.add, r="kci", w="mp@0")
+    tt(T.s0[:], T.s1[:], ES[0][0], Op.mult, "s1 mp@0", "s0")
+    act(ES[0][3], T.s0[:], Fn.Identity, "s0", "code@0", bias=17.0)
 
-    def gather(e, o, i, r, w):
-        if e == "V":
-            cp(o, i, r, w, c="g")
+    def gathers(n, buf, lst, lk, nm):
+        for i in range(n):
+            lin(buf[:, 512 * i:512 * i + 512], T.X[:, 0:V].indirect(lst[:, 32 * i:32 * i + 32]), "X " + lk, "%s%d" % (nm, i), c="g")
+
+    def exchange(t):
+        last, LT0 = t == ST - 1, 576 * t
+        lt = "LT@3 PTA@3 PTo@3 PTp@3" if last else "LT@%d" % t
+        own, mate, off = T.LT[:, LT0 + 32:LT0 + 128], T.LT[:, LT0 + 320:LT0 + 416], T.LT[:, LT0:LT0 + 16]
+        mo, m2, aM, mM, sM, n17, kp, gm, qn = [T.cq[:, 96 * i:96 * i + 96] for i in range(9)]
+        if last:
+            aM = ES[t][4][:, 0:96]
+        act(aM, mate, Fn.Abs, lt, "aM")
+        act(mo, own, Fn.Abs, lt, "mo", bias=-17.0)
+        act(m2, own, Fn.Square, lt, "m2", bias=-17.0)
+        act(mM, aM, Fn.Abs, "aM", "mM", bias=-17.0)
+        ts(n17, own, 0.0, Op.min, 17.0, Op.add, r=lt, w="n17")
+        ts(gm, own, 0.0, Op.is_gt, r=lt, w="gm")
+        act(kp, n17, Fn.Abs, "n17", "kp")
+        nf = 4 if last else 3
+        op("V", lambda: g.vector.tensor_reduce(T.nn[:, 0:1], T.AF[:, 16 * t:16 * t + 8 + 2 * nf], Ax.X, Op.min), cost(wb_, 1), "AFr AF@%d" % t, "nA")
+        ts(T.nn[:, 1:2], T.nn[:, 0:1], T.LT[:, LT0 + 16:LT0 + 17], Op.min, T.LT[:, LT0 + 304:LT0 + 305], Op.min, r="nA " + lt, w="nB")
+        l1 = [T.l1[:, 16 * i:16 * i + 16] for i in range(4)]
+        ts(l1[1], off, T.nn[:, 1:2], Op.is_ge, 512.0, Op.mult, r="nB " + lt, w="l11")
+        tt(l1[2], l1[1], off, Op.add, "l11 " + lt, "l12")
+        tt(l1[3], l1[2], l96, Op.min, "l12 K1", "l13")
+        cp(T.l2u[:], l1[3], "l13", "l2u")
+        if last:
+            act(T.sn[:], ES[t][4].indirect(T.l2u[:]), Fn.Sign, "aM l2u code@3", "sn", bias=-17.0, c="g")
+            mm([(pd[:, 0:16], to_list(Zb, T.sn))], "sn", "D")
+            ts(T.ob[:], pd[:, 0:16], 1023.5, Op.add, w="ob", b="D")
         else:
-            act(o, i, Fn.Identity, r, w, c="g")
+            act(sM, aM, Fn.Sign, "aM", "sM", bias=-17.0)
+            mm([(pd[:, 0:6], to_list(Zb, sM))], "sM", "D")
+            ts(T.bn[:, 0:6], pd[:, 0:6], 1023.5, Op.add, w="bn", b="D")
+            cp(T.rbn[:], T.RP[:].indirect(T.bn[:, 0:6]), "RP bn", "rbn", c="g")
+            gathers(3, T.X[:, V + 64:V + 64 + 1536], T.rbn, "rbn", "n")
+        for j in range(4):
+            p, bk = pc[:, 512 * (j % 2):512 * (j % 2) + 384], "C%d" % (j % 2)
+            parts = [(p[:, 96 * q:96 * q + 96], 128 * (4 * j + q)) for q in range(4)]
+            mm([(o, [(T.FA[:, k:k + 128], mo), (T.FB[:, k:k + 128], m2)]) for o, k in parts], "mo m2 K2", bk, end=False, one=True)
+            mm([(o, [(I1, mM)]) for o, k in parts], "mM", bk, first=False, one=True)
+            lin(T.TR[:, 384 * j:384 * j + 384], p, "K2", "TR%d" % j, bk, bias=bq_, relu=True)
+        for j in range(4):
+            mm([(pk[:, 0:96], ([(I1, kp), (Im17, gm)] if j == 0 else []) + [(E(Z1, k), T.TR[:, 96 * k:96 * k + 96]) for k in range(4 * j, 4 * j + 4)])],
+               "TR%d kp gm" % j, "K", first=j == 0, end=j == 3)
+        return sM, qn
 
-    CH = PLAN["CH"]
-    yall = " ".join("y%d" % i for i in range(8)) + " yz"
-    xall = " ".join("x%d" % i for i in range(8))
-    DB = [(pa, "A0 A1"), (pb, "B0 B1"), (pc, "C0 C1")]
+    def pick(mo, mk):
+        if NS < 4:
+            cp(T.rbu[:, 64 * NS:256], T.RP[:].indirect(T.bo[:, 4 * NS:16]), "RP bo", "rbu", c="g")
+            gathers(8 - 2 * NS, T.X[:, Y0:Y0 + 1024 * (4 - NS)], T.rbu[:, 64 * NS:256], "rbu", "y")
+            mm([(pb[:, 512:768 - 64 * NS], [(I16, T.l1t[:, 0:256 - 64 * NS]), (Im, mo[:, 64 * NS:256])])], mk + " K4", "B1")
+            lin(T.OW[:, 96 + 64 * NS:352], pb[:, 512:768 - 64 * NS], "", "OWy", "B1", bias=Y0 - 1536.0)
+        if not NS:
+            return
+        ts(T.rbo[:, 0:64 * NS], T.RP[:].indirect(T.bo[:, 0:4 * NS]), -1536.0, Op.add, r="RP bo", w="rbo", c="g")
+        for h in range(2):
+            act(T.drop[:, 2048 * h + 7:2048 * h + 512 * NS:8], mo[:, 0:64 * NS], Fn.Square, mk, "sq%d" % h, bias=-64.0 * (9 - 8 * h), scale=64.0)
+        for n in range(2 * NS):
+            b, h = divmod(n, 2)
+            p, bk, o = [pa, pb][h][:, 512:1024], "AB"[h] + "1", 2048 * h + 512 * b
+            mm([(p[:, j::8], [(T.SEL[:, 128 * (8 * h + j):128 * (8 * h + j + 1)], T.rbo[:, 64 * b:64 * b + 64])]
+                 + ([(T.IB[:, 128 * j:128 * j + 128], mo[:, 64 * b:64 * b + 64])] if j < 7 else [])) for j in range(8)], "rbo K4 " + mk, bk, one=True)
+            scan(T.run[:, o:o + 512], p, T.drop[:, o:o + 512], 0.0, Op.max, Op.subtract, "sq%d K4" % h, "run%d" % n, bk)
+        tt(T.OW[:, 96:96 + 64 * NS], T.run[:, 7:512 * NS:8], T.run[:, 2055:2048 + 512 * NS:8], Op.max, names("run", 0, 2 * NS), "OWo")
+
+    def sums(i):
+        dd, rl, out, dk, r = T.dd[:, 1024 * i:1024 * i + 1024], T.rl[:, 1024 * i:1024 * i + 1024], pd[:, 64 * i:64 * i + 64], names("d", 2 * i, 2 * i + 2), len(ops)
+
+        def total(z, x, first, end):
+            return [g.tensor.matmul(out, a, c, first and k == 0, end and k == 15) for k, (a, c) in enumerate(to_list(z, x))][-1]
+        op("VS", [lambda: g.vector.tensor_scalar(rl, dd, 0.0, None, Op.max), lambda: g.scalar.activation(rl, dd, Fn.Abs)], [cost(rl, 0.5), cost(rl, 1)], dk, "r%d" % i)
+        op("P", lambda: total(Zm, dd, True, False) if ORDER["eng"][r] == "V" else None, (0, 0, 0, 0, 1024, 0), dk + " K1", "", "D", serves=r)
+        op("P", lambda: total(Z2, rl, False, True) if ORDER["eng"][r] == "V" else total(Z1, rl, True, True), (0, 0, 0, 0, 1024, 0), "r%d K1" % i, "", "D")
+
+    xall = names("x", 0, 8)
     m = [T.m0[:, 64 * i:64 * i + 64] for i in range(5)]
+    banks = [[q for q in range(QD) if RQ[q] // 512 == n] for n in range(1 + RQ[-1] // 512)]
+    regs = [slice(RQ[qs[0]], RQ[qs[-1]] + NB * WQ[qs[-1]]) for qs in banks]
 
     for t in range(ST):
+        step[0] += 1
         last, s = t == ST - 1, min(t, 1)
-        z, zk = (T.z0[:], " z0") if t == 0 else (T.zL[:, 256 * (t - 1):256 * t], " z%d" % t)
-        zh = [T.z0[:, 128 * h:128 * h + 128] if t == 0 else T.zL[:, 256 * (t - 1) + 128 * h:256 * (t - 1) + 128 * h + 128] for h in range(2)]
-        au, ak = T.aL[:, 16 * t:16 * t + 16], "a%d" % t
-        p0, PB, LT0, pt = (3 * 576 if last else 288 * t), (T.LT if last else T.PT), 576 * t, "PT%d" % t
+        mp, code, mk_, ck = ES[t][0], ES[t][3], "mp@%d" % t, "code@%d" % t
+        z, zk = (T.z0[:] if t == 0 else T.ZL[:, 256 * (t - 1):256 * t]), "z@%d" % t
+        au, ak = T.aL[:, 16 * t:16 * t + 16], "a@%d" % t
+        if t:
+            el, ek = EL[t - 1], "E@%d" % t
+            tt(T.l1[:, 0:16], el[1], el[2], Op.add, ek, "bs")
+            ts(T.bo[:], T.l1[:, 0:16], 1023.5, Op.add, r="bs", w="bo")
+        pick(*((el[0], ek) if t else (mp, mk_)))
+        if not t:
+            ts(T.offY[:], T.OW[:, 96:352], 1536.0, Op.add, r="OWo OWy", w="offY")
         cp(T.ra[:], T.RP[:].indirect(au), "RP " + ak, "ra", c="g")
-        for nm, buf, lst, lk in (("y", T.yy, T.rb, "X rb"), ("x", T.xx, T.ra, "X ra")):
-            i = 0
-            for piece in PLAN[nm][s].split():
-                j = i + int(piece[1:])
-                gather(piece[0], buf[:, 512 * i:512 * j], T.X[:, 0:V].indirect(lst[:, 32 * i:32 * j]), lk,
-                       " ".join("%s%d" % (nm, q) for q in range(i, j)))
-                i = j
-        ts(T.rbv[:], T.rb[:], -1536.0, Op.add, r="rb", w="rbv", c=0.5)
+        gathers(8, T.xx, T.ra, "ra", "x")
+        if t:
+            sM, qn = exchange(t - 1)
+            tt(T.OW[:, 0:96], T.cj[:], pk[:, 0:96], Op.subtract, "K2", "OWn", "K")
+            tt(qn, pk[:, 0:96], sM, Op.mult, "sM", "qn", "K")
+            ts(T.offY[:], T.OW[:].indirect(T.l2u[:]), 1536.0, Op.add, r="OWo OWy OWn l2u", w="offY", c="g")
+            lin(el[4][:, 0:96], qn, "qn", "cn", bias=17.0)
+            lin(code, el[4].indirect(T.l2u[:]), "cn l2u " + ek, ck, c="g")
+            act(mp, code, Fn.Abs, ck, mk_, bias=-17.0)
         cp(T.af[:], au, ak, "af")
-        op("V", lambda t=t: g.vector.transpose(T.KT[:], KB[t]), 0.14, "KB%d" % t, "KT")
-        if not last:
-            send([(KB[t], [(rank + 1, T.WB[:, 352 * t + 96:352 * t + 352])], engines([rank + 1]))], "KB%d" % t, "WB%d" % t, "z", "sK%d" % t, ne)
-        for h in range(4):
-            mm([(pk[:, 256 + 16 * k + hh:256 + 16 * k + 16:2],
-                 [(T.PM[:, (2 * hh + e) * 128:(2 * hh + e + 1) * 128], T.KT[:, 16 * e + k::32]) for e in range(2)])
-                for k in range(4 * h, 4 * h + 4) for hh in range(2)], "KT", "K")
-        act(T.KL[:], pk[:, 256:512], Fn.Identity, "", "KL", "K", bias=-1.0)
-        mm([(pk[:, 256:512], [(Ih, z), (Iq, T.cm1[:]), (Ih, T.xx[:, 0::16])])], xall + zk, "K")
-        act(T.r32[:], pk[:, 256:512], Fn.Identity, "", "r32", "K", bias=MAGIC)
-        act(T.tt[:], T.r32[:], Fn.Identity, "r32", "tt", bias=-MAGIC)
-        for i in range(len(CH) - 1):
-            lo, hi = CH[i], CH[i + 1]
-            blk = range(lo // 32, (hi + 31) // 32)
-            dd, rl = T.dd[:, 16 * lo:16 * hi], T.rl[:, 16 * lo:16 * hi]
-            w0 = lo // 64
-            tt(dd, T.yy[:, 1024 * w0:1024 * w0 + 1024].indirect(T.offY[:, lo:hi]), T.xx[:, 16 * lo:16 * hi], Op.subtract,
-               "y%d y%d offY " % (2 * w0, 2 * w0 + 1) + " ".join("x%d" % q for q in blk), "d%d" % i, c="g")
-            if PLAN["r"][s][i] == "V":
-                ts(rl, dd, 0.0, Op.max, r="d%d" % i, w="r%d" % i, c=0.5)
-                mm([(pd[:, lo:hi], [(E(Zm, k), T.dd[:, 16 * lo + k:16 * hi:16]) for k in range(16)])], "d%d" % i, "D", end=False)
-                mm([(pd[:, lo:hi], [(E(Z2, k), T.rl[:, 16 * lo + k:16 * hi:16]) for k in range(16)])], "r%d" % i, "D", first=False)
-            else:
-                act(rl, dd, Fn.Abs, "d%d" % i, "r%d" % i)
-                mm([(pd[:, lo:hi], [(E(Z1, k), T.rl[:, 16 * lo + k:16 * hi:16]) for k in range(16)])], "r%d" % i, "D")
         for j in range(4):
-            p, bk = DB[j % 3]
-            how = PLAN["z"][s][j]
-            az, ze = T.az[:, 1024 * j:1024 * j + 1024], T.ze[:, 1024 * j:1024 * j + 1024]
-            kp, kb = [(pk, "K"), (pb, "B0"), (pc, "C0"), (pa, "A0")][j]
-            head = [(I1, T.c32k[:, 64 * j:64 * j + 64]), (I1, T.KL[:, 64 * j:64 * j + 64])]
-            if how == "S":
-                for h in range(2):
-                    mm([(p[:, 256 * q + 128 * h:256 * q + 128 * h + 128], [(I1, T.xx[:, 2048 * h + 4 * j + q:2048 * h + 2048:16]), (Im, zh[h])])
-                        for q in range(4)], " ".join("x%d" % q for q in range(4 * h, 4 * h + 4)) + zk, bk)
-                act(az, p[:], Fn.Abs, "", "az%d" % j, bk)
-            else:
-                b1 = bk.split()[1]
-                mm([(p[:, 512:768], [(I1, z)])], zk, b1)
-                for q in range(4):
-                    tt(T.ze[:, 1024 * j + 256 * q:1024 * j + 256 * q + 256], T.xx[:, 4 * j + q::16], p[:, 512:768], Op.subtract, xall, "ze%d%d" % (j, q), b1)
-                zek = " ".join("ze%d%d" % (j, q) for q in range(4))
-                if how == "M":
-                    act(az, ze, Fn.Abs, zek, "az%d" % j)
-                else:
-                    ts(az, ze, 0.0, Op.max, 2.0, Op.mult, r=zek, w="az%d" % j, c=0.5)
-                    mm([(kp[:, 0:64], head + [(E(Zn, r), T.ze[:, 1024 * j + r:1024 * j + 1024:16]) for r in range(16)])], "KL " + zek, kb, end=False)
-            mm([(kp[:, 0:64], (head if how != "V" else []) + [(E(Zk, r), T.az[:, 1024 * j + r:1024 * j + 1024:16]) for r in range(16)])],
-               "KL az%d" % j, kb, first=how != "V")
+            p, bk = [(pa, "A0 A1"), (pb, "B0 B1")][j % 2]
+            for h in range(2):
+                mm([(p[:, 256 * q + 128 * h:256 * q + 128 * h + 128], [(I1, T.xx[:, 2048 * h + 4 * j + q:2048 * h + 2048:16]), (Im, z[:, 128 * h:128 * h + 128])])
+                    for q in range(4)], names("x", 4 * h, 4 * h + 4) + " " + zk, bk)
+            act(T.az[:, 1024 * j:1024 * j + 1024], p[:], Fn.Abs, "", "az%d" % j, bk)
+        for j in range(4):
+            kp, kb = pc[:, 512 * (j % 2):512 * (j % 2) + 64], "C%d" % (j % 2)
+            mm([(kp, [(I1, T.kA[:]), (I1, T.kB[:, 64 * j:64 * j + 64])] + to_list(Zk, T.az[:, 1024 * j:1024 * j + 1024]))], "az%d" % j, kb)
             if j == 0:
-                cp(m[0], kp[:, 0:64], "", "m0", kb)
+                lin(m[0], kp, "", "m0", kb)
             else:
-                tt(m[j], kp[:, 0:64], m[j - 1], Op.min, "m%d" % (j - 1), "m%d" % j, kb)
+                tt(m[j], kp, m[j - 1], Op.min, "m%d" % (j - 1), "m%d" % j, kb)
+        act(T.sn[:], code, Fn.Sign, ck, "sn", bias=-17.0)
+        mm([(pk[:, 0:16], to_list(Zb, T.sn))], "sn", "K")
+        ts(T.bu[:], pk[:, 0:16], 1023.5, Op.add, w="bu", b="K")
+        if not last:
+            lin(ES[t][1], pk[:, 0:16], "", "bh@%d" % t, "K")
+            tt(ES[t][2], pk[:, 0:16], ES[t][1], Op.subtract, "bh@%d" % t, "bl@%d" % t, "K")
+            send([(ES[t][5], [(rank + 1, EL[t][5])], engines([rank + 1]))],
+                 "%s %s bh@%d bl@%d" % (ck, mk_, t, t), "E@%d" % (t + 1), "E", t, ne)
+        ts(T.rbv[:], T.RP[:].indirect(T.bu[:]), -1536.0, Op.add, r="RP bu", w="rbv", c="g")
+        for i in range(8):
+            ny = max(0, i + 1 - 2 * NS)
+            tt(T.dd[:, 512 * i:512 * i + 512], T.X[:, 0:Y0 + 512 * ny].indirect(T.offY[:, 32 * i:32 * i + 32]), T.xx[:, 512 * i:512 * i + 512], Op.subtract,
+               "X Xd n0 n1 n2 %s offY x%d" % (names("y", 0, ny), i), "d%d" % i, c="g")
+        for i in range(4):
+            sums(i)
+        tt(m[4][:, 0:32], m[3][:, 0:32], m[3][:, 32:64], Op.min, "m3", "m4")
+        tt(T.vi[:, 0:16], m[4][:, 0:16], m[4][:, 16:32], Op.min, "m4", "vi")
+        ts(T.vi[:, 16:32], T.vi[:, 0:16], 4095, Op.bitwise_and, r="vi", w="vj")
+        cp(T.Lx[:], T.vi[:, 16:32], "vj", "Lx")
+        tt(T.mk[:], T.IDp[:].indirect(T.Lx[:]), mp, Op.mult, "Lx K3 " + mk_, "mk", c="g")
+        lin(T.xk[:], T.xx[:].indirect(T.Lx[:]), "Lx " + xall, "xk", c="g")
+        mm([(pb[:, 256:272], to_list(Zm, T.mk))], "mk", "B0")
+        ts(T.Lw[:], pb[:, 256:272], 16.0, Op.add, w="Lw", b="B0")
+        tt(T.mm[:], T.IDp[:, 0:16].indirect(T.Lw[:]), T.rbv[:], Op.mult, "Lw rbv K3", "mm", c="g")
+        lin(T.wk[:], T.dd[:].indirect(T.Lx[:]), "Lx " + names("d", 0, 8), "wk", c="g")
+        mm([(pa[:, 0:256], [(Iq, T.cm1[:]), (Ih, z), (Ih, T.xx[:, 0::16])])], xall + " " + zk, "A0")
+        ts(T.ZW[:, 256:512], pa[:, 0:256], MAGIC, Op.add, MAGIC, Op.subtract, w="ZW1", b="A0")
+        mm([(pb[:, 256:272], to_list(None, T.mm))], "mm", "B0")
+        mm([(pb[:, 0:256], [(T.BOh[:], T.mm[:])])], "mm", "B0")
+        lin(T.cF[:], pb[:, 256:272], "", "cF", "B0", scale=-1.0)
+        cp(T.cL[:], pb[:, 256:272], "", "cL", "B0")
+        mm([(pa[:, 0:256], [(I1, z), (Im, T.xk[:]), (Im, T.wk[:])])], "wk xk " + zk, "A0")
+        act(T.ZW[:, 0:256], pa[:, 0:256], Fn.Abs, "", "ZW0", "A0")
+        mm([(pk[:, 0:16], [(T.I5f[:], T.af[:])] + to_list(Zu, T.ZW[:, 0:256]))], "ZW0 af", "K", end=False)
+        mm([(pa[:, 256:512], [(Iq, T.cm1[:]), (I1, T.xk[:]), (Ih, T.wk[:])])], "xk wk", "A0")
+        ts(T.hf[:], pa[:, 256:512], MAGIC, Op.add, MAGIC, Op.subtract, w="hf", b="A0")
+        for c in range(16):
+            b, q = divmod(c, QD)
+            o, x = T.ad[:, RQ[q] + b * WQ[q]:RQ[q] + (b + 1) * WQ[q] - 1], pb[:, 16 * QD * b:16 * QD * b + WQ[q] - 1]
+            act(o, x, Fn.Abs, "cF", "ad%d" % c, "B0", bias=T.cF[:, c:c + 1])
+        for n, qs in enumerate(banks):
+            mm([(pc[:, regs[n]], [(I1, T.mask[:, regs[n]]), (Im32, T.ad[:, regs[n]])])] + [(ends(pc, q), [(H1, T.cL[:, q::QD])]) for q in qs],
+               "cL K3 " + " ".join("ad%d" % c for c in range(16) if c % QD in qs), "C%d" % n, end=False, one=True)
+        zn, dv = T.ZO[:, 256 * t:256 * t + 256], T.dv[:]
+        p0, PB, LT0, pt = (3 * 576 if last else 288 * t), (T.LT if last else T.PT), 576 * t, ["PT%s@%d" % (k, t) for k in "Aop"]
         act(T.sg[:], pd[:, 0:256], Fn.Sign, "thA", "sg", "D", bias=T.thA[:])
-        mm([(pd[:, 0:16], [(E(Z1, r), T.sg[:, r::16]) for r in range(16)])], "sg", "D")
-        mm([(pb[:, 512:768], [(T.BO[:], T.sg[:])])], "sg", "B1")
-        act(T.sB[:], pb[:, 512:768], Fn.Sign, "", "sB", "B1", bias=5.0)
-        ts(T.dv[:], pd[:, 0:16], -5.0, Op.is_gt, w="dv", b="D")
-        scan(T.cs[:], one, T.dv[:], 0.0, Op.mult, Op.add, "dv K1", "cs")
-        tt(T.t1[:], T.dv[:], c256, Op.mult, "dv K1", "t1")
-        mm([(pd[:, 0:16], [(T.BO[:], T.cs[:]), (T.Um[:], T.dv[:]), (Im, T.t1[:]), (I1, c255)]),
-            (pd[:, 16:17], [(T.BO[:], T.cs[:, 15:16])])], "cs dv t1", "D")
-        cp(PB[:, p0 + 16:p0 + 17], pd[:, 16:17], "", pt + "A", "D")
+        mm([(pd[:, 0:16], to_list(Z1, T.sg))], "sg", "D")
+        for n, qs in enumerate(banks):
+            mm([(pc[:, RQ[q] + b * WQ[q]:RQ[q] + (b + 1) * WQ[q] - 1], [(T.BOm[:], T.sg[:, 16 * QD * b:16 * QD * b + WQ[q] - 1])]) for q in qs for b in range(NB)],
+               "sg", "C%d" % n, first=False, end=False)
+        ts(dv, pd[:, 0:16], -5.0, Op.is_gt, w="dv", b="D")
+        scan(T.cs[:], one, dv, 0.0, Op.mult, Op.add, "dv K1", "cs")
+        tt(T.t1[:], dv, c256, Op.mult, "dv K1", "t1")
+        mm([(pk[:, 0:16], [(Ibig, dv)])], "dv", "K", first=False)
+        mm([(pa[:, 0:16], [(I256, dv), (I1, lane)])], "dv", "A0")
+        for n, qs in enumerate(banks):
+            mm([(ends(pc, q), [(I4k, dv[:, q::QD])]) for q in qs], "dv", "C%d" % n, first=False, one=True)
+        mm([(pd[:, 0:16], [(T.BO[:], T.cs[:]), (T.Um[:], dv), (Im, T.t1[:]), (I1, c255)]),
+            (pd[:, 16:17], [(T.BO[:], T.cs[:, 15:16])])], "cs t1 dv", "D")
+        cp(T.zl[:], pa[:, 0:16], "", "zl", "A0")
+        tt(T.an[:, 0:16], pk[:, 0:16], T.af[:], Op.max, "af", "an", "K")
+        ts(T.an[:, 16:32], T.an[:, 0:16], 2047, Op.bitwise_and, r="an", w="an3")
+        if last:
+            cp(T.oa[:], T.an[:, 16:32], "an3", "oa")
+        else:
+            cp(T.aS[:, 16 * t:16 * t + 16], T.an[:, 16:32], "an3", "aS@%d" % t)
+            send([(T.aS[:, 16 * t:16 * t + 16], [(rank + 1, T.aL[:, 16 * t + 16:16 * t + 32])], engines([rank + 1]))], "aS@%d" % t, "a@%d" % (t + 1), "a", t, ne)
+        cp(T.off[:], pd[:, 0:16], "", "off", "D")
+        lin(PB[:, p0 + 16:p0 + 17], pd[:, 16:17], "", pt[0], "D")
         far = [1, 2, 3, 5] if last else [2, 3, 4]
         send([(PB[:, p0 + 16:p0 + 18], [(rank + d, T.AF[:, 16 * t + 8 + 2 * i:16 * t + 10 + 2 * i]) for i, d in enumerate(far)],
-               engines([rank + d for d in far]))], pt + "A", "AFr", "A", "sA%d" % t, ne * len(far))
-        cp(T.off[:], pd[:, 0:16], "", "off", "D")
-        cp(PB[:, p0:p0 + 16], pd[:, 0:16], "", pt + "o", "D")
-        tt(PB[:, p0 + 32:p0 + 288].indirect(T.off[:]), KB[t], T.sg[:], Op.mult, "KB%d sg off" % t, pt + "p", c="s")
-        lt = "LT%d" % t
+               engines([rank + d for d in far]))], pt[0], "AFr", "A", t, ne * len(far))
+        tt(PB[:, p0 + 32:p0 + 288].indirect(T.off[:]), code, T.sg[:], Op.mult, ck + " sg off", pt[2], c="s")
+        lin(PB[:, p0:p0 + 16], pd[:, 0:16], "", pt[1], "D")
+        lin(zn, T.ZW[:].indirect(T.zl[:]), "ZW0 ZW1 zl", "zn@%d" % t, c="g")
         if last:
-            send([(PB[:, p0 + 16:p0 + 128], [(rank - 2, T.LT[:, LT0 + 304:LT0 + 416])], engines([rank - 2]))],
-                 "PT3A PT3p sndsA3", lt, "Q", "sQ3", ne)
-            lt += " PT3A PT3o PT3p"
+            send([(PB[:, p0 + 16:p0 + 128], [(rank - 2, T.LT[:, LT0 + 304:LT0 + 416])], engines([rank - 2]))], "PTA@3 PTp@3", "LT@3", "Q", t, ne)
         else:
+            send([(zn, [(rank + 1, T.ZL[:, 256 * t:256 * t + 256])], engines([rank + 1]))], "zn@%d" % t, "z@%d" % (t + 1), "z", t, ne)
             es = engines([rank + 1, rank - 1])
             PT = T.PT[:, p0:p0 + 128]
             send([(PT, [(rank + 1, T.LT[:, LT0:LT0 + 128])], es[:ne // 2]), (PT, [(rank - 1, T.LT[:, LT0 + 288:LT0 + 416])], es[ne // 2:])],
-                 "%sA %so %sp sndsA%d" % (pt, pt, pt, t), lt, "Q", "sQ%d" % t, ne)
-        cp(T.AF[:, 16 * t:16 * t + 1], pd[:, 16:17], "", "AF%d" % t, "D")
+                 " ".join(pt), "LT@%d" % t, "Q", t, ne)
+        lin(T.AF[:, 16 * t:16 * t + 1], pd[:, 16:17], "", "AF@%d" % t, "D")
         if not last:
             cp(T.Ai[:, 0:1], pd[:, 16:17], "", "Ai0", "D")
             ts(T.Ai[:, 1:2], T.Ai[:, 0:1], 31, Op.bitwise_and, r="Ai0", w="Ai1")
             tt(T.thA[:], T.thf[:], T.Ai[:, 1:2], Op.subtract, "Ai1 thf", "thA")
-        ts(T.mar[:], T.dv[:], -1.0, Op.mult, 1.0, Op.add, r="dv", w="mar")
-        tt(m[4][:, 0:32], m[3][:, 0:32], m[3][:, 32:64], Op.min, "m3", "m4")
-        tt(T.vi[:], m[4][:, 0:16], m[4][:, 16:32], Op.min, "m4", "vi")
-        ts(T.Li[:, 16:32], T.vi[:], 15, Op.bitwise_and, r="vi", w="Li1")
-        ts(T.Li[:, 0:16], T.vi[:], 5, Op.arith_shift_right, 15, Op.bitwise_and, r="vi", w="Li0")
-        cp(T.Ku[:], T.Li[:, 16:32], "Li1", "Ku")
-        tt(T.Lj[:], T.Li[:], T.base[:], Op.add, "Li0 Li1 K1", "Lj")
-        cp(T.Lu[:], T.Lj[:], "Lj", "Lu")
-        tt(T.mm[:], T.ID[:].indirect(T.Ku[:]), T.rbv[:], Op.mult, "Ku rbv K1", "mm", c="g")
-        act(T.wk[:], T.yy[:].indirect(T.Lu[:, 16:32]), Fn.Identity, "Lu " + yall, "wk", c="g")
-        act(T.xk[:], T.xx[:].indirect(T.Lu[:, 0:16]), Fn.Identity, "Lu " + xall, "xk", c="g")
-        zn = T.zS[:, 256 * t:256 * t + 256]
-        mm([(pa[:, 0:256], [(Im, z), (I1, T.wk[:])])], "wk" + zk, "A0")
-        act(T.zm[:], pa[:, 0:256], Fn.Abs, "", "zm", "A0")
-        mm([(pa[:, 512:528], [(T.I4f[:], T.af[:])] + [(E(Zu, r), T.zm[:, r::16]) for r in range(16)])], "af zm", "A1", extra=192)
-        mm([(pa[:, 0:256], [(I1, T.tt[:]), (I256, T.sB[:])]), (pa[:, 256:512], [(I1, T.zm[:]), (Im256, T.sB[:])])], "tt sB zm", "A0")
-        act(T.zt[:], pa[:, 0:512], Fn.Relu, "", "zt", "A0", bias=-256.0)
-        mm([(pa[:, 0:256], [(I1, T.zt[:, 0:256]), (I1, T.zt[:, 256:512])])], "zt", "A0")
-        act(zn, pa[:, 0:256], Fn.Identity, "", "zn%d" % t, "A0")
-        tt(T.an1[:], pa[:, 512:528], T.mar[:], Op.mult, "mar", "an1", "A1")
-        tt(T.an2[:], T.an1[:], T.af[:], Op.add, "an1 af", "an2")
-        ts(T.an3[:], T.an2[:], 2047, Op.bitwise_and, r="an2", w="an3")
-        if not last:
-            cp(T.aS[:, 16 * t:16 * t + 16], T.an3[:], "an3", "aS%d" % t)
-            es = engines([rank + 1])
-            send([(T.aS[:, 16 * t:16 * t + 16], [(rank + 1, T.aL[:, 16 * t + 16:16 * t + 32])], es)], "aS%d" % t, "a%d" % (t + 1), "a", "sa%d" % t, ne)
-            send([(zn, [(rank + 1, T.zL[:, 256 * t:256 * t + 256])], es)], "zn%d sndsa%d" % (t, t), "z%d" % (t + 1), "z", "sz%d" % t, ne)
-        else:
-            cp(T.oa[:], T.an3[:], "an3", "oa")
-        mm([(pb[:, 0:256], [(T.BOh[:], T.mm[:])])], "mm", "B0", end=False)
-        mm([(pb[:, 0:256], [(I2k, T.sB[:])])], "sB", "B0", first=False)
-        mm([(pc[:, 512:528], [(I1, c1536)] + [(E(None, r), T.mm[:, r::16]) for r in range(16)])], "mm", "C1", end=False)
-        mm([(pc[:, 512:528], [(I4k, T.dv[:])])], "dv", "C1", first=False)
-        mm([(pc[:, 0:256], [(Iq, T.cm1[:]), (Ih, T.wk[:]), (Ih, T.xk[:])])], "wk xk", "C0")
-        act(T.r33[:], pc[:, 0:256], Fn.Identity, "", "r33", "C0", bias=MAGIC)
-        act(T.hf[:], T.r33[:], Fn.Identity, "r33", "hf", bias=-MAGIC)
-        tt(T.cB[:], pb[:, 0:256], T.cmask[:], Op.add, "K1", "cB", "B0")
-        cp(T.cL[:], pc[:, 512:528], "", "cL", "C1")
-        tt(T.cm[:], pc[:, 512:528], dum, Op.min, "K1", "cm", "C1")
-        tt(T.eq[:], T.cL[:].indirect(T.expl[:]), T.cB[:], Op.is_equal, "cL cB K1", "eq", c="g")
-        scan(T.sc[:], T.crst[:], T.eq[:], 0.0, Op.mult, Op.max, "eq K1", "sc")
-        tt(T.so[:], T.sc[:, 15::16], T.cm[:], Op.max, "sc cm", "so")
-        cp(T.su[:, 0::2], T.so[:], "so", "su")
-        for c in range(15, -1, -1):
-            cp(T.X[:].indirect(T.su[:, 2 * c:2 * c + 1]), T.hf[:, 16 * c:16 * c + 16], "su hf Xd", "X", c="s")
-        WB, aM, wbk = T.WB[:, 352 * t:352 * t + 352], T.WB[:, 352 * t:352 * t + 96], ("KB3" if last else "WB%d" % t)
-        act(aM, T.LT[:, LT0 + 320:LT0 + 416], Fn.Abs, lt, "aM")
-        act(T.aW[:], T.LT[:, LT0 + 32:LT0 + 128], Fn.Abs, lt, "aW")
-        op("V", lambda t=t, far=far: g.vector.tensor_reduce(T.nn[:, 0:1], T.AF[:, 16 * t:16 * t + 8 + 2 * len(far)], Ax.X, Op.min), 0.07,
-           "AFr AF%d" % t, "n0")
-        ts(T.nn[:, 1:2], T.nn[:, 0:1], T.LT[:, LT0 + 16:LT0 + 17], Op.min, T.LT[:, LT0 + 304:LT0 + 305], Op.min, r="n0 " + lt, w="n1")
-        ts(T.l1[:], T.LT[:, LT0:LT0 + 16], T.nn[:, 1:2], Op.is_ge, 512.0, Op.mult, r="n1 " + lt, w="l1")
-        tt(T.l2[:], T.l1[:], T.LT[:, LT0:LT0 + 16], Op.add, "l1 " + lt, "l2")
-        tt(T.l1[:], T.l2[:], c16i, Op.min, "l2 K1", "l1")
-        cp(T.l2u[:], T.l1[:], "l1", "l2u")
-        act(T.sn[:], WB.indirect(T.l2u[:]), Fn.Sign, "aM l2u " + wbk, "sn", bias=-16.5, c="g")
-        mm([(pc[:, 512:528], [(E(Zb, r), T.sn[:, r::16]) for r in range(16)])], "sn", "C1")
-        if last:
-            ts(T.ob[:], pc[:, 512:528], 32767.5, Op.add, w="ob", b="C1")
-        else:
-            ts(T.bu[:], pc[:, 512:528], 32767.5, Op.add, w="bu", b="C1")
-            cp(T.rb[:], T.RP[:].indirect(T.bu[:]), "RP bu", "rb", c="g")
-        sQ, sM = T.b16[:, 0:96], T.b16[:, 96:192]
-        act(sQ, T.aW[:, 0:96], Fn.Sign, "aW", "sQ", bias=-16.5)
-        act(sM, aM, Fn.Sign, "aM", "sM", bias=-16.5)
-        mm([(pd[:, 0:96], [(I1, T.LT[:, LT0 + 32:LT0 + 128]), (Im8, sQ)]), (pd[:, 128:224], [(I1, aM), (Im8, sM)])],
-           "aM sQ sM " + lt, "D")
-        act(T.uu[:], pd[:, 0:96], Fn.Relu, "", "uu", "D", bias=-8.0)
-        act(T.k2[:], pd[:, 128:224], Fn.Identity, "", "k2", "D", bias=-8.0)
-        act(T.u2[:], T.uu[:], Fn.Square, "uu", "u2")
-        for j in range(4):
-            p, bk = (pk, "K") if j % 2 == 0 else (pd, "D")
-            mm([(p[:, 96 * q:96 * q + 96], [(I1, T.k2[:]), (T.FA[:, 128 * (4 * j + q):128 * (4 * j + q) + 128], T.uu[:]),
-                                            (T.FB[:, 128 * (4 * j + q):128 * (4 * j + q) + 128], T.u2[:])]) for q in range(4)], "uu u2 k2 K2", bk)
-            act(T.TR[:, 384 * j:384 * j + 384], p[:, 0:384], Fn.Relu, "K2", "TR%d" % j, bk, bias=bq_)
-        mm([(pk[:, 0:96], [(Im, T.uu[:]), (I1, T.aW[:, 0:96]), (Im8, sQ), (I8, sM)] + [(E(Z1, k), T.TR[:, 96 * k:96 * k + 96]) for k in range(12)])],
-           "uu aW sQ sM TR0 TR1 TR2", "K", end=False)
-        mm([(pk[:, 0:96], [(E(Z1, k), T.TR[:, 96 * k:96 * k + 96]) for k in range(12, 16)])], "TR3", "K", first=False)
-        act(aM, pk[:, 0:96], Fn.Identity, "", "aM", "K")
-        act(KB[t + 1], WB.indirect(T.l2u[:]), Fn.Identity, "aM l2u " + wbk, "KB%d" % (t + 1), c="g")
-        if not last:
-            mm([(pd[:, 256:512], [(T.BO[:], T.c16l[:]), (Im8, T.sn[:]), (I1, KB[t + 1])])], "sn K2 KB%d" % (t + 1), "D")
-            ts(T.offY[:], pd[:, 256:512], -9.0, Op.add, w="offY", b="D")
-        else:
-            mm([(pd[:, 256:512], [(Im8, T.sn[:]), (I1, KB[4])])], "sn KB4", "D")
-            act(T.ok[:], pd[:, 256:512], Fn.Identity, "", "ok", "D", bias=-9.0)
-            for e, o, i, k, lat in (("Y", T.yz, zn, "zn3", 2.5), ("Y", T.ya, T.oa[:], "oa", 2.5), ("Y", T.yx, T.X[:, 0:V], "X", 5.5),
-                                    ("Y", T.yb, T.ob[:], "ob", 2.5), ("S", T.yk, T.ok[:], "ok", 2.5)):
-                dma(e, o[:], i, "out", k)
-                op("R", None, lat, "q" + e + "out", "")
-                wr.pop("q" + e + "out")
-                rd.pop("q" + e + "out")
+        for n, qs in enumerate(banks):
+            scan(T.sc[:, regs[n]], T.crst[:, regs[n]], pc[:, regs[n]], 0.0, Op.mult, Op.max, "K3", " ".join("sc%d" % q for q in qs), "C%d" % n)
+        for q in range(QD):
+            ts(T.su[:, q::QD], ends(T.sc, q), dum_[q], Op.min, r="sc%d K1" % q, w="su%d" % q)
+        for b in range(NB - 1, -1, -1):
+            cp(T.X[:, 0:V + 64].indirect(T.su[:, QD * b:QD * b + QD]), T.hf[:, 16 * QD * b:16 * QD * (b + 1)], "hf Xd " + names("su", 0, QD), "X", c="s")
+
+    step[0] += 1
+    lin(T.KW[:, 96:352], mp, mk_, "KWo", bias=16.0, scale=-1.0, c=0.5)
+    exchange(ST - 1)
+    lin(T.KW[:, 0:96], pk[:, 0:96], "", "KWn", "K", bias=16.0, scale=-1.0)
+    lin(T.ok[:], T.KW[:].indirect(T.l2u[:]), "KWo KWn l2u", "ok", c="g")
+    for e, o, i, k, lat in (("Y", T.yz, zn, "zn@3", 2.5), ("Y", T.ya, T.oa[:], "oa", 2.5), ("Y", T.yx, T.X[:, 0:V], "X", 5.5),
+                            ("Y", T.yb, T.ob[:], "ob", 2.5), ("S", T.yk, T.ok[:], "ok", 2.5)):
+        dma(e, o[:], i, "out", k)
+        op("R", None, fixed(lat), "q" + e + "out", "")
+        wr.pop("q" + e + "out")
+        rd.pop("q" + e + "out")
 
     if "order" not in ORDER:
-        ORDER["order"], ORDER["t"] = schedule(ops)
+        ORDER["order"], ORDER["eng"], ORDER["t"] = schedule(ops)
+    for o, e in zip(ops, ORDER["eng"]):
+        o["e"] = e
     cnt = {"V": 0, "S": 0, "P": 0, "G": 0}
     seen = {e: {} for e in Q}
     for i in ORDER["order"]:
         o = ops[i]
         e = o["e"]
-        if e == "R":
+        if e in "RL":
             continue
         top = {}
         for p, raw in o["pre"].items():
@@ -531,7 +715,7 @@ def rank_program(g, core, T, topo):
             if seen[e].get(k, 0) < n:
                 Q[e].wait_ge(T.sem[k], n)
                 seen[e][k] = n
-        ins = o["f"]()
+        ins = o["f"][-1 if e == "S" else 0]()
         if ins is not None:
             cnt[e] += 1
             ins.then_inc(T.sem[e], 1)

from concourse.bass import DstId, RemoteDMATransfer
from concourse.mybir import AluOpType as Op, AxisListType as Ax, ActivationFunctionType as Fn

N, V, L, ST = 6, 3072, 256, 4
MAGIC = 12582912.0
QD = 4
WQ = [16 * (q + 1) for q in range(QD)]
RQ = {1: [0], 2: [0, 128], 4: [0, 64, 192, 512]}[QD]
NB = 16 // QD
NS = 2
Y0 = V + 64 + 1536
PLAN = {"rounds": 10000, "seed": 1, "alone": 0.15, "turn": 0.2, "jump": 6, "slack": 0.001}
QUEUES = {
    "V": """-mm -dv -cs -t1 -an -off -an3 -aS -oa -cL -PTp -Ai0 bs -hf -Ai1 bo rbo -thA -sc0 -sc3 -su2 -su1 -su0 -zl -su3 -X rbu -X:2 run0 -X:3 run1 -X:4 ra run2 y1
            n17 run3 x6 x0 bn x2 nA gm OWo nB rbn l11 TR3 l12 x7 l13 KWn OWn qn af l2u ok ob n2 offY d3 d0 d5 bu d4 d1 d2 m0 r0 m1 d7 m2 d6 m3 bh m4 bl vi vj Lx mk
            ZW1 rbv Lw""",
    "S": """-ZW0 -PTA -cF -PTo -AF -ad0 -ad1 -ad2 -ad3 -ad4 -ad5 -ad6 -ad7 -ad8 -ad9 -ad10 -ad11 -ad12 -ad13 -ad14 -ad15 sq0 -zn OWy sq1 y0
            m2 mo KWo aM x1 mM sM x3 TR0 TR1 kp x4 TR2 x5 n1 n0 cn code sn az0 az1 y3 y2 az2 az3 mp r1 r2 r3 wk xk sg""",
    "P": """-ZW0 -dv -cs -mm -mm:2 -xk -cL -sg:2 -dv:3 -cL:2 -sg:3 -dv:4 -dv:2 E mp rbo rbo:2 rbo:3 rbo:4 mo mo:2 mM mM:2 sM mo:3 mM:3 mo:4 mM:4 TR0 TR1 TR2 TR3
            x0 x4 x0:2 x4:2 sn x0:3 x4:3 az0 x0:4 x4:4 az1 az2 d0 az3 r0 d2 x0:5 r1 d4 r2 d6 r3 mk wk sg""",
    "G": "-snda -sndQ -sndA -sndz sndE",
}
FIRST = {
    "V": "rbo rbu ra run0 run1 x2 run2 run3 x0 af OWo x6 offY y1 d0 d1 d3 d5 d4 d2 d6 m1 r0 m2 d7 m3 bu bh m4 bl vi vj Lx mk ZW1 rbv Lw",
    "S": "sq1 OWy sq0 x3 x1 x5 x7 x4 sn y2 az0 y0 az1 y3 m0 az2 az3 r1 r2 r3 wk xk sg",
    "P": "mp rbo rbo:2 rbo:3 rbo:4 x0:2 x0 x4 sn x4:2 az0 x0:3 x4:3 x0:4 x4:4 az1 d0 az2 az3 r0 d2 x0:5 r1 d4 r2 d6 r3 mk wk sg",
    "G": "sndE",
}
PACE = [(0.83e-3, 0.42e-3, 1.25, 3.8, 0.25, 0.2, 1.0, 112), (1.2e-3, 0.7e-3, 1.2, 3.0, 0.3, 0.25, 1.2, 160),
        (1.1e-3, 0.55e-3, 2.0, 5.5, 0.3, 0.25, 1.2, 165), (0.95e-3, 0.47e-3, 1.5, 3.8, 0.3, 0.25, 2.0, 155)]
LAT = {"far": 2.5, "row": 0.005, "byte": 1.5e-5, "small": 3.5, "RP": 9.0, "X": 13.0, "send": 0.6}


def sb(n, dt="bfloat16"):
    return ("sbuf", [128, n], dt)


SCRATCH = {
    "X": sb(Y0 + 4096), "rbu": sb(256, "uint16"), "RP": sb(2048, "int32"), "xx": sb(4096), "dd": sb(4096), "rl": sb(4096), "az": sb(4096), "IDp": sb(4096),
    "SEL": sb(2048, "float16"), "IB": sb(7 * 128), "drop": sb(4096), "run": sb(4096, "float32"),
    "avi": sb(16, "int32"), "bvi": sb(16, "int32"), "kci": sb(256, "int32"), "thi": sb(1, "int32"), "z0": sb(256),
    "J": sb(256, "float32"), "pci": sb(8, "int32"), "pcj": sb(8, "int32"), "col": sb(24, "float32"),
    "IS": sb(10 * 128), "IH": sb(2 * 128, "float16"), "I5f": sb(128, "float32"), "BO": sb(128), "BOm": sb(128), "Um": sb(128),
    "BOh": sb(128, "float16"), "Zh": sb(144, "float16"),
    "ZS": sb(6 * 144), "FA": sb(2048), "FB": sb(2048), "BA": sb(128), "BB": sb(128), "IDf": sb(16, "float32"),
    "tA": sb(256, "float32"), "tB": sb(256, "float32"), "tI": sb(256, "int32"), "tJ": sb(256, "int32"), "tC": sb(256, "float32"), "tL": sb(256, "float32"),
    "cm1": sb(256), "kA": sb(64), "kB": sb(256), "l1t": sb(256), "cj": sb(96, "float32"), "cf": sb(48, "float32"), "cb": sb(48), "pw": sb(112, "float32"),
    "pos": sb(768, "float32"), "mask": sb(768), "crst": sb(768), "ad": sb(768), "sc": sb(768, "float32"),
    "BT": sb(96), "bl": sb(32, "uint16"), "bli": sb(32, "int32"), "s0": sb(256), "s1": sb(256),
    "an": sb(32, "int32"), "af": sb(16, "float32"), "bo": sb(16, "uint16"), "bu": sb(16, "uint16"), "bn": sb(16, "uint16"),
    "ra": sb(256, "uint16"), "rbo": sb(256, "float16"), "rbn": sb(96, "uint16"), "rbv": sb(256, "float16"), "offY": sb(256, "uint16"),
    "OW": sb(352, "float32"), "KW": sb(352), "ZW": sb(512), "sg": sb(256), "sn": sb(256), "dv": sb(16),
    "thA": sb(1, "float32"), "thf": sb(1, "float32"), "Ai": sb(2, "int32"), "cs": sb(16), "t1": sb(16), "off": sb(16, "uint16"), "zl": sb(16, "uint16"),
    "m0": sb(320, "float32"), "vi": sb(32, "int32"), "Lx": sb(16, "uint16"), "Lw": sb(16, "uint16"), "wk": sb(256), "xk": sb(256), "hf": sb(256),
    "mk": sb(256), "mm": sb(256, "float16"), "cL": sb(16, "float16"), "cF": sb(16, "float32"), "su": sb(16, "uint16"),
    "nn": sb(2, "float32"), "l1": sb(64, "float32"), "l2u": sb(16, "uint16"), "l2h": sb(16, "float16"),
    "cq": sb(9 * 96), "TR": sb(1536), "oa": sb(16, "float32"), "ob": sb(16, "float32"), "ok": sb(256),
    "PT": sb(3 * 288), "LT": sb(4 * 576), "AF": sb(4 * 16), "ES": sb(4 * 640), "EL": sb(3 * 640), "ZO": sb(4 * 256), "ZL": sb(3 * 256),
    "aS": sb(3 * 16, "uint16"), "aL": sb(4 * 16, "uint16"),
    "pa": ("psum", [128, 1024], "float32"), "pb": ("psum", [128, 1024], "float32"), "pc": ("psum", [128, 1024], "float32"),
    "pd": ("psum", [128, 512], "float32"), "pk": ("psum", [128, 512], "float32"),
}
SEMAPHORES = (["V", "S", "P", "G", "ld0", "ld1", "ld2", "out", "sent"]
              + ["%s%d" % (s, t) for s in ("sA", "sQ", "sa", "sz", "sE") for t in range(ST)])
ORDER = {}


def listed(ops, tail):
    places = [{}, {}]
    for place, lists in zip(places, (QUEUES, FIRST)):
        for e, s in lists.items():
            for j, w in enumerate(s.split()):
                name, nth = (w.lstrip("-").split(":") + ["1"])[:2]
                place[e, name, int(nth)] = j + (1000 if w[0] == "-" else 0)
    rank, eng = [], []
    for o, left in zip(ops, tail):
        keys = [(e, o["kind"][1], o["kind"][2]) for e in o["e"]]
        place = places[o["step"] == 1 and any(k in places[1] for k in keys)]
        e = ([k[0] for k in keys if k in place] + [o["e"][-1]])[0]
        rank.append(1000 * o["step"] + place.get((e, o["kind"][1], o["kind"][2]), 999) if o["step"] else -left)
        eng.append(e)
    order = sorted(range(len(ops)), key=lambda i: (rank[i], i))
    return {e: [i for i in order if eng[i] == e] for e in "VSPGY"}, eng


def timing(ops, pace, can):
    cy, pc, ga, sc, same, other, far, whole = pace
    return [[0.0 if o["for"] and can[o["for"]] == "S" else c[0] + cy * (c[1] + ga * c[2] + sc * c[3]) + pc * c[4] + far * c[5]
             for o, c in [(o, o["c"][k]) for o in ops]] for k in (0, -1)]


def schedule(ops):
    n = len(ops)
    pre, suc, like = [list(o["pre"].items()) for o in ops], [[] for _ in ops], {}
    for i, o in enumerate(ops):
        for p, raw in pre[i]:
            suc[p].append(i)
        like.setdefault(o["kind"], {})[o["step"]] = i
    tied, seed, count = {o["for"] for o in ops}, [PLAN["seed"]], [len(p) for p in pre]
    none, same, other = (0.0,) * 4, tuple(p[4] for p in PACE), tuple(p[5] for p in PACE)

    def rnd(k=1.0):
        seed[0] = (seed[0] * 1103515245 + 12345) % 2147483648
        return k * seed[0] / 2147483648

    def times(eng):
        tm = [timing(ops, p, eng) for p in PACE]
        return [list(zip(*[d[k] for d in tm])) for k in (0, 1)]

    def judge(seq, eng, tm):
        left, at, order, go = list(count), {e: 0 for e in seq}, [], True
        end, free, ready = [none] * n, {e: none for e in "VSPGYLR"}, []
        while go:
            go = False
            for e, q in seq.items():
                k = at[e]
                while k < len(q) and not left[q[k]]:
                    ready.append(q[k])
                    k += 1
                    while ready:
                        f = ready.pop()
                        order.append(f)
                        x = eng[f]
                        a, b, c, d = free[x]
                        for p, raw in pre[f]:
                            y = eng[p]
                            u, v = end[p], (none if x in "RL" or y in "RL" else other if x != y else same if raw else none)
                            if u[0] + v[0] > a:
                                a = u[0] + v[0]
                            if u[1] + v[1] > b:
                                b = u[1] + v[1]
                            if u[2] + v[2] > c:
                                c = u[2] + v[2]
                            if u[3] + v[3] > d:
                                d = u[3] + v[3]
                        u = tm[x == "S"][f]
                        end[f] = (a + u[0], b + u[1], c + u[2], d + u[3])
                        if x != "R":
                            free[x] = end[f]
                        for s in suc[f]:
                            left[s] -= 1
                            if not left[s] and eng[s] in "RL":
                                ready.append(s)
                go, at[e] = go or k > at[e], k
        if len(order) < n:
            return None
        ts = [max(v) for v in zip(*end[-40:])]
        return sum(t / p[7] for t, p in zip(ts, PACE)), seq, eng, tm, end, order, ts

    def longest(state, k):
        _, seq, eng, tm, end, order, ts = state
        end = [v[k] for v in end]
        start = [end[i] - tm[eng[i] == "S"][i][k] for i in range(n)]
        before, last, way = {}, {}, []
        for i in order:
            before[i], last[eng[i]] = last.get(eng[i]), i
        i = max(range(n), key=lambda i: end[i])
        while start[i] > 1e-6:
            p = before[i]
            if eng[i] != "R" and p is not None and end[p] >= start[i] - 1e-6:
                if p not in ops[i]["pre"] and eng[i] != "L":
                    way.append((i, p))
                i = p
            else:
                i = max([q for q, raw in pre[i]], key=lambda q: end[q] + (0.0 if eng[q] in "RL" else PACE[k][4 if eng[q] == eng[i] else 5]))
        return way, start

    dur, tail = timing(ops, PACE[0], [o["e"] for o in ops])[0], [0.0] * n
    for i in range(n - 1, -1, -1):
        tail[i] = dur[i] + max([tail[k] + other[0] for k in suc[i]] + [0.0])
    seq, eng = listed(ops, tail)
    best = now = judge(seq, eng, times(eng))
    ways = {}
    for r in range(PLAN["rounds"]):
        _, seq, eng, tm, end, order, ts = now
        k = int(rnd(4))
        if k not in ways:
            ways[k] = longest(now, k)
        way, start = ways[k]
        b, a = way[int(rnd(len(way)))]
        alone, how, seq = rnd() < PLAN["alone"], rnd(), dict(seq)
        if how < PLAN["turn"]:
            f = a if len(ops[a]["e"]) == 2 else b
            if len(ops[f]["e"]) < 2:
                continue
            to, eng, shift = "S" if eng[f] == "V" else "V", list(eng), rnd(2.0) - 1.0
            seq["V"], seq["S"] = list(seq["V"]), list(seq["S"])
            for i in [f] if alone else like[ops[f]["kind"]].values():
                if eng[i] != to:
                    seq[eng[i]].remove(i)
                    eng[i] = to
                    j = 0
                    while j < len(seq[to]) and start[seq[to][j]] < start[i] + shift:
                        j += 1
                    seq[to].insert(j, i)
            if f in tied:
                tm = times(eng)
        else:
            e, far, gap = eng[b], int(rnd() ** 3 * PLAN["jump"]), ops[b]["step"] - ops[a]["step"]
            q = seq[e] = list(seq[e])
            for s, i in [(ops[b]["step"], b)] if alone else like[ops[b]["kind"]].items():
                j = a if i == b else like[ops[a]["kind"]].get(s - gap)
                if j is None or eng[i] != e or eng[j] != e:
                    continue
                if how < (1 + PLAN["turn"]) / 2:
                    q.remove(i)
                    q.insert(max(0, q.index(j) - far), i)
                else:
                    q.remove(j)
                    q.insert(q.index(i) + 1 + far, j)
        new = judge(seq, eng, tm)
        if new and new[0] <= now[0] * (1 + PLAN["slack"] * (1 - r / PLAN["rounds"]) * rnd()):
            now, ways = new, {}
            if new[0] < best[0]:
                best = new
    ORDER["ops"], ORDER["best"] = ops, best
    return best[5], best[2], best[6]


def rank_program(g, core, T, topo):
    rank = T.rank_of(core)
    if rank is None:
        return
    Q = {"V": g.vector, "S": g.scalar, "P": g.tensor, "G": g, "Y": g.sync}
    ops, wr, rd, bank, alias = [], {}, {}, {}, {"K1": [], "K2": [], "K3": [], "K4": []}
    sent, step, kinds = [0], [0], {}

    def op(e, f, c, r="", w="", b="", tok=None, serves=None):
        i = len(ops)
        f, c = (f, c) if len(e) == 2 else ([f], [c])
        pre = {}
        ws = []
        for k in w.split():
            if k in alias:
                alias[k].append(i)
            else:
                ws.append(k)
        for k in ws:
            for p in rd.get(k, []) + wr.get(k, []):
                pre[p] = True
        for k in b.split():
            if k in bank:
                pre.setdefault(bank[k], False)
            bank[k] = i
        for k in r.split():
            for p in (alias[k] if k in alias else wr.get(k, [])):
                pre[p] = True
            if k not in alias:
                rd.setdefault(k, []).append(i)
        for k in ws:
            wr[k], rd[k] = [i], []
        pre.pop(i, None)
        name = (w or r or "-").split()[0].split("@")[0]
        kinds[e, name, step[0]] = kinds.get((e, name, step[0]), 0) + 1
        ops.append({"e": e, "f": f, "c": c, "pre": pre, "tok": tok, "w": w or r, "for": serves, "step": step[0],
                    "kind": (e, name, kinds[e, name, step[0]], min(step[0], 2))})

    def fixed(v):
        return (v, 0, 0, 0, 0, 0)

    def cost(out, per):
        n = out.shape[1]
        return {"g": (0.06, 0, n, 0, 0, 0), "s": (0.06, 0, 0, n, 0, 0)}[per] if per in ("g", "s") else (0, max(64, n * per), 0, 0, 0, 0)

    def ts(out, in0, s1, o0, s2=None, o1=None, r="", w="", b="", c=1):
        if o1 is None:
            op("V", lambda: g.vector.tensor_scalar(out, in0, s1, None, o0), cost(out, c), r, w, b)
        else:
            op("V", lambda: g.vector.tensor_scalar(out, in0, s1, s2, o0, o1), cost(out, c), r, w, b)

    def tt(out, a, x, o, r="", w="", b="", c=None):
        op("V", lambda: g.vector.tensor_tensor(out, a, x, o), cost(x, c or (1 if b else 2)), r, w, b)

    def cp(out, a, r="", w="", b="", c=1):
        op("V", lambda: g.vector.tensor_copy(out, a), cost(a if c == "s" else out, c), r, w, b)

    def act(out, a, fn, r="", w="", b="", bias=0.0, scale=1.0, c=1):
        op("S", lambda: g.scalar.activation(out, a, fn, bias=bias, scale=scale), cost(out, c), r, w, b)

    def lin(out, a, r="", w="", b="", bias=0.0, scale=1.0, c=1, relu=False):
        def v():
            if relu:
                return g.vector.tensor_scalar(out, a, bias, 0.0, Op.add, Op.max)
            if bias == 0.0 and scale == 1.0:
                return g.vector.tensor_copy(out, a)
            return g.vector.tensor_scalar(out, a, scale, bias, Op.mult, Op.add)
        op("VS", [v, lambda: g.scalar.activation(out, a, Fn.Relu if relu else Fn.Identity, bias=bias, scale=scale)],
           [cost(out, c), cost(out, 1 if c == 0.5 else c)], r, w, b)

    def scan(out, a, x, ini, o0, o1, r, w, b=""):
        op("V", lambda: g.vector.tensor_tensor_scan(out, a, x, ini, o0, o1), cost(out, 1), r, w, b)

    def ms(ap, v, w):
        op("V", lambda: g.vector.memset(ap, v), cost(ap, 0.5), w=w)

    def iota(out, pattern, w, base=0):
        op("G", lambda: g.iota(out, pattern, base, 0, allow_small_or_imprecise_dtypes=True), (0.13, 2 * out.shape[1], 0, 0, 0, 0), w=w)

    def mm(groups, r="", b="", first=True, end=True, one=False):
        def f():
            ins = None
            for n, (out, terms) in enumerate(groups):
                for i, (a, c) in enumerate(terms):
                    ins = g.tensor.matmul(out, a, c, first and i == 0 and not (one and n), end and i == len(terms) - 1 and not (one and n < len(groups) - 1))
            return ins
        op("P", f, (0, 0, 0, 0, sum(max(64, o.shape[1]) * len(x) for o, x in groups), 0), r + " K1", "", b)

    def dst(h):
        a = topo.addr(T.cores[h % N])
        return DstId(rid=a[0], pnc=a[1])

    def engines(hs):
        out = topo.engines(core, T.cores[hs[0] % N])
        for h in hs[1:]:
            out = [e for e in out if e in topo.engines(core, T.cores[h % N])]
        return out

    def send(transfers, r, name, kind, t, count):
        sem = "s%s%d" % (kind, t)

        def f():
            g.remote_dma_fused([RemoteDMATransfer(dst_ids=[dst(h) for h, _ in ds], dma_engine_mask=sum(1 << e for e in es), remote_sem=T.sem[sem],
                                                  srcs=[src], dsts=[d for _, d in ds]) for src, ds, es in transfers], local_sem=T.sem.sent)
        sent[0] += sum(len(x[2]) for x in transfers)
        op("G", f, fixed(LAT["send"]), r, "snd%s@%d" % (kind, t))
        rows = 128 * sum(len(x[1]) for x in transfers)
        op("L", None, (0, 0, 0, 0, 0, rows * (LAT["row"] + LAT["byte"] * 2 * transfers[0][0].shape[1])), "snd%s@%d" % (kind, t), "fly%s@%d" % (kind, t))
        op("R", None, (0, 0, 0, 0, 0, LAT["far"]), "fly%s@%d" % (kind, t), name, tok=(sem, count))

    def dma(e, o, i, sem, r=""):
        def f():
            Q[e].dma_start(o, i).then_inc(T.sem[sem], 16)
        op(e, f, fixed(0.1), r, "q" + e + sem)

    def names(nm, i, j):
        return " ".join("%s%d" % (nm, q) for q in range(i, j))

    ne = len(engines([rank + 1]))
    pa, pb, pc, pd, pk = T.pa, T.pb, T.pc, T.pd, T.pk
    col, J = T.col, T.J
    kc_, gc_, pc_, zc_, w2_, wb_, wi_, bq_, k4_, k16_ = [col[:, i:i + 1] for i in range(10)]
    dum_, lim_ = [col[:, 10 + q:11 + q] for q in range(QD)], [col[:, 14 + q:15 + q] for q in range(QD)]
    I1, Im, I256, Ih, Iq, I16, Ibig, I4k, Im32, Im17 = [T.IS[:, 128 * i:128 * i + 128] for i in range(10)]
    H1, H16 = T.IH[:, 0:128], T.IH[:, 128:256]
    Z1, Z2, Zm, Zk, Zu, Zb = range(6)
    lL, one, l96 = [T.cf[:, 16 * i:16 * i + 16] for i in range(3)]
    c256, c255, lane = [T.cb[:, 16 * i:16 * i + 16] for i in range(3)]

    def E(z, r):
        return T.Zh[:, 15 - r:143 - r] if z is None else T.ZS[:, 144 * z + 15 - r:144 * z + 143 - r]

    def to_list(z, x):
        return [(E(z, r), x[:, r::16]) for r in range(16)]

    def ends(buf, q):
        return buf[:, RQ[q] + WQ[q] - 1:RQ[q] + NB * WQ[q]:WQ[q]]

    dma("Y", T.RP[:], T.rp[:], "ld1")
    dma("Y", T.X[:, 0:V], T.ph[:], "ld2", "qYld1")
    for o, i in ((T.avi, T.av), (T.bvi, T.bv), (T.kci, T.kc), (T.z0, T.zs), (T.thi, T.th)):
        dma("S", o[:], i[:], "ld0")
    op("R", None, fixed(LAT["small"]), "qSld0", "avi bvi kci z@0 thi", tok=("ld0", 80))
    op("R", None, fixed(LAT["RP"]), "qYld1", "RP", tok=("ld1", 16))
    op("R", None, fixed(LAT["X"]), "qYld2", "X", tok=("ld2", 16))

    op("G", lambda: g.iota(T.pci[:, 0:1], [[0, 1]], 0, 1), fixed(0.15), w="pci")
    iota(J[:], [[1, 256]], "J")
    iota(T.tA[:], [[1, 16], [0, 16]], "tA")
    iota(T.tB[:], [[0, 16], [1, 16]], "tB")
    iota(T.X[:, V:Y0], [[0, Y0 - V]], "Xd n0 n1 n2")
    iota(T.l1t[:], [[1, 256]], "K4", 1)
    iota(T.PT[:], [[0, 3 * 288]], " ".join("PT%s@%d" % (k, t) for k in "Aop" for t in range(ST - 1)), 96)
    ms(T.LT[:, 3 * 576:3 * 576 + 304], 96.0, "PTA@3 PTo@3 PTp@3")
    for t in range(ST):
        ms(T.AF[:, 16 * t:16 * t + 8], 96.0, "AF@%d" % t)
    ms(T.cm1[:], -1.0, "K1")
    ms(one, 1.0, "K1")
    iota(T.ad[:], [[0, 768]], names("ad", 0, 16))
    ts(T.pcj[:, 0:1], T.pci[:, 0:1], 15, Op.bitwise_and, r="pci", w="pj0")
    ts(T.pcj[:, 1:2], T.pci[:, 0:1], 4, Op.arith_shift_right, r="pci", w="pj1")
    cp(T.pcj[:, 2:3], T.pci[:, 0:1], "pci", "pj2")
    cp(col[:, 0:3], T.pcj[:, 0:3], "pj0 pj1 pj2", "kc gc pc")
    ts(zc_, gc_, 16.0, Op.mult, 15.0, Op.add, r="gc", w="zc")
    ts(w2_, kc_, 2.0, Op.mult, 1.0, Op.add, r="kc", w="w2")
    ts(k16_, kc_, 16.0, Op.mult, r="kc", w="k16")
    ts(T.IDf[:], J[:, 0:16], kc_, Op.is_equal, r="J kc", w="IDf")
    pw = [T.pw[:, 16 * i:16 * i + 16] for i in range(7)]
    ms(pw[0], 2.0, "pw0")
    ms(pw[1], 0.5, "pw1")
    ms(pw[2], 0.0, "pw2")
    scan(pw[3], pw[0], pw[2], 0.25, Op.mult, Op.add, "pw0 pw2", "pw3")
    scan(pw[4], pw[1], pw[2], 65536.0, Op.mult, Op.add, "pw1 pw2", "pw4")
    tt(pw[5][:, 0:11], pw[3][:, 0:11], T.IDf[:, 0:11], Op.mult, "pw3 IDf", "pw5")
    tt(pw[6], pw[4], T.IDf[:], Op.mult, "pw4 IDf", "pw6")
    op("V", lambda: g.vector.tensor_reduce(wb_, pw[5][:, 0:11], Ax.X, Op.add), cost(wb_, 1), "pw5", "wb")
    op("V", lambda: g.vector.tensor_reduce(wi_, pw[6], Ax.X, Op.add), cost(wi_, 1), "pw6", "wi")
    ts(I1, J[:, 0:128], pc_, Op.is_equal, r="J pc", w="I1 K1")
    for buf, v in ((Im, -1.0), (I256, 256.0), (Ih, 0.5), (Iq, 0.25), (I16, 16.0), (T.I5f[:], 5.0), (Ibig, -131072.0), (I4k, 4096.0), (Im32, -32.0), (Im17, -17.0)):
        act(buf, I1, Fn.Identity, "I1", "K1", scale=v)
    for buf, v in ((H1, 1.0), (H16, 16.0)):
        ts(buf, I1, v, Op.mult, r="I1", w="K1", c=0.5)
    ts(T.ZS[:, 0:144], J[:, 0:144], zc_, Op.is_equal, r="J zc", w="Z1 K1")
    ts(T.Zh[:], J[:, 0:144], zc_, Op.is_equal, r="J zc", w="K1")
    for zi, v in ((Z2, 2.0), (Zm, -1.0), (Zk, 4096.0), (Zu, w2_), (Zb, wb_)):
        act(T.ZS[:, 144 * zi:144 * zi + 144], T.ZS[:, 0:144], Fn.Identity, "Z1 w2 wb", "K1", scale=v)
    ts(T.BO[:], T.tA[:, 0:128], gc_, Op.is_equal, r="tA gc", w="BO K1")
    ts(T.BOh[:], T.tA[:, 0:128], gc_, Op.is_equal, r="tA gc", w="K1")
    act(T.BOm[:], T.BO[:], Fn.Identity, "BO", "K1", scale=-1.0)
    ts(T.tC[:, 0:128], T.tB[:, 0:128], kc_, Op.is_lt, -1.0, Op.mult, r="tB kc", w="tC")
    tt(T.Um[:], T.tC[:, 0:128], T.BO[:], Op.mult, "tC BO", "K1")
    ts(lL, J[:, 0:16], 16.0, Op.mult, kc_, Op.add, r="J kc", w="lL K1")
    ts(c256, lL, -1.0, Op.mult, 256.0, Op.add, r="lL", w="K1")
    ts(c255, lL, -1.0, Op.mult, 255.0, Op.add, r="lL", w="K1")
    cp(lane, lL, "lL", "K1")
    ts(l96, lL, 96.0, Op.add, r="lL", w="K1")
    act(T.kA[:], T.tB[:, 0:64], Fn.Identity, "tB", "K1", scale=256.0)
    act(T.kB[:], T.tA[:], Fn.Identity, "tA k16", "K1", bias=k16_)
    act(T.cj[:], J[:, 0:96], Fn.Identity, "J", "K2", bias=V + 64 + 16 - 1536.0, scale=16.0)
    ts(T.IDp[:, 0:256], T.tB[:], kc_, Op.is_equal, r="tB kc", w="ID0 K3")
    for lo in (256, 512):
        cp(T.IDp[:, lo:2 * lo], T.IDp[:, 0:lo], "ID0 ID%d" % (lo - 256), "ID%d K3" % lo, c=0.5)
    for lo in range(1024, 4096, 1024):
        lin(T.IDp[:, lo:lo + 1024], T.IDp[:, 0:1024], "ID512", "K3", c=0.5)
    for r in range(16):
        ts(T.SEL[:, 128 * r:128 * r + 128], T.BO[:], T.IDf[:, r:r + 1], Op.mult, r="BO IDf", w="K4", c=0.5)
    for j in range(7):
        lin(T.IB[:, 128 * j:128 * j + 128], I1, "I1", "K4", scale=8192.0 * (7 - j), c=0.5)
    for h in range(2):
        iota(T.drop[:, 2048 * h:2048 * h + 512 * NS], [[0, 64 * NS], [-8192, 8]], "sq%d" % h, 4096 * (31 - 16 * h))
    for q in range(QD):
        reg = slice(RQ[q], RQ[q] + NB * WQ[q])
        iota(T.pos[:, reg], [[0, NB], [1, WQ[q]]], "pos%d" % q)
        ts(lim_[q], kc_, 16.0 * q, Op.add, r="kc", w="lim%d" % q)
        ts(dum_[q], kc_, float(V + 16 * q), Op.add, r="kc", w="K1")
        ts(T.sc[:, reg], T.pos[:, reg], lim_[q], Op.is_ge, -59.0, Op.mult, r="pos%d lim%d" % (q, q), w="sc%d" % q)
        act(T.mask[:, reg], T.sc[:, reg], Fn.Identity, "sc%d" % q, "mask%d" % q, bias=-5.0)
        ms(ends(T.mask, q), 1536.0, "mask%d K3" % q)
        ts(T.crst[:, reg], T.pos[:, reg], 0.5, Op.is_gt, r="pos%d" % q, w="crst%d" % q)
        ms(ends(T.crst, q), 4096.0, "crst%d K3" % q)
    act(T.tC[:, 128:256], T.tB[:, 0:128], Fn.Identity, "tB", "tD", bias=512.0, scale=-32.0)
    tt(T.BA[:], T.tC[:, 128:256], T.BO[:], Op.mult, "tD BO", "BA")
    act(T.BB[:], T.BO[:], Fn.Identity, "BO", "BB", scale=-16.0)
    ts(k4_, kc_, -16.0, Op.add, 4.0, Op.mult, r="kc", w="k4")
    ts(bq_, k4_, k4_, Op.mult, -1.0, Op.mult, r="k4", w="K2")
    for k in range(16):
        act(T.FA[:, 128 * k:128 * k + 128], T.BA[:], Fn.Identity, "BA IDf", "K2", scale=T.IDf[:, k:k + 1])
        op("VS", [lambda k=k: g.vector.tensor_scalar(T.FB[:, 128 * k:128 * k + 128], T.BB[:], T.IDf[:, k:k + 1], None, Op.mult),
                  lambda k=k: g.scalar.activation(T.FB[:, 128 * k:128 * k + 128], T.BB[:], Fn.Identity, scale=T.IDf[:, k:k + 1])],
           [cost(T.BB, 0.5), cost(T.BB, 1)], "BB IDf", "K2")

    def planes(buf, o):
        return [buf[:, o + 352:o + 608], buf[:, o + 608:o + 624], buf[:, o + 624:o + 640], buf[:, o + 96:o + 352], buf[:, o:o + 352], buf[:, o + 96:o + 640]]

    ES = [planes(T.ES, 640 * t) for t in range(ST)]
    EL = [planes(T.EL, 640 * t) for t in range(ST - 1)]
    cp(T.aL[:, 0:16], T.avi[:], "avi", "a@0")
    cp(T.bo[:], T.bvi[:], "bvi", "bo")
    ts(T.bli[:, 0:16], T.bvi[:], 63, Op.bitwise_and, r="bvi", w="bli0")
    ts(T.bli[:, 16:32], T.bvi[:], 6, Op.arith_shift_right, r="bvi", w="bli1")
    cp(T.bl[:, 0:16], T.bli[:, 0:16], "bli0", "bl0")
    ts(T.bl[:, 16:32], T.bli[:, 16:32], 64.0, Op.add, r="bli1", w="bl1")
    ts(T.tI[:, 0:64], J[:, 0:64], wi_, Op.mult, r="J wi", w="tI0")
    ts(T.tI[:, 64:96], J[:, 0:32], wi_, Op.mult, 64.0, Op.mult, r="J wi", w="tI1")
    ts(T.tI[:, 96:192], T.tI[:, 0:96], 15, Op.arith_shift_right, 1, Op.bitwise_and, r="tI0 tI1", w="tI2")
    ts(T.BT[:], T.tI[:, 96:192], 2.0, Op.mult, r="tI2", w="BT")
    ts(T.thf[:], T.thi[:], -1.0, Op.mult, -0.5, Op.add, r="thi", w="thf")
    ts(T.thA[:], T.thi[:], -1.0, Op.mult, -0.5, Op.add, r="thi", w="thA")
    act(T.s0[:], T.BT[:].indirect(T.bl[:, 0:16]), Fn.Identity, "BT bl0", "s0", bias=-1.0, c="g")
    tt(T.s1[:], T.BT[:].indirect(T.bl[:, 16:32]), T.s0[:], Op.add, "BT bl1 s0", "s1", c="g")
    ts(ES[0][0], T.kci[:], -1.0, Op.mult, 16.0, Op.add, r="kci", w="mp@0")
    tt(T.s0[:], T.s1[:], ES[0][0], Op.mult, "s1 mp@0", "s0")
    act(ES[0][3], T.s0[:], Fn.Identity, "s0", "code@0", bias=17.0)

    def gathers(n, buf, lst, lk, nm):
        for i in range(n):
            lin(buf[:, 512 * i:512 * i + 512], T.X[:, 0:V].indirect(lst[:, 32 * i:32 * i + 32]), "X " + lk, "%s%d" % (nm, i), c="g")

    def exchange(t):
        last, LT0 = t == ST - 1, 576 * t
        lt = "LT@3 PTA@3 PTo@3 PTp@3" if last else "LT@%d" % t
        own, mate, off = T.LT[:, LT0 + 32:LT0 + 128], T.LT[:, LT0 + 320:LT0 + 416], T.LT[:, LT0:LT0 + 16]
        mo, m2, aM, mM, sM, n17, kp, gm, qn = [T.cq[:, 96 * i:96 * i + 96] for i in range(9)]
        if last:
            aM = ES[t][4][:, 0:96]
        act(aM, mate, Fn.Abs, lt, "aM")
        act(mo, own, Fn.Abs, lt, "mo", bias=-17.0)
        act(m2, own, Fn.Square, lt, "m2", bias=-17.0)
        act(mM, aM, Fn.Abs, "aM", "mM", bias=-17.0)
        ts(n17, own, 0.0, Op.min, 17.0, Op.add, r=lt, w="n17")
        ts(gm, own, 0.0, Op.is_gt, r=lt, w="gm")
        act(kp, n17, Fn.Abs, "n17", "kp")
        nf = 4 if last else 3
        op("V", lambda: g.vector.tensor_reduce(T.nn[:, 0:1], T.AF[:, 16 * t:16 * t + 8 + 2 * nf], Ax.X, Op.min), cost(wb_, 1), "AFr AF@%d" % t, "nA")
        ts(T.nn[:, 1:2], T.nn[:, 0:1], T.LT[:, LT0 + 16:LT0 + 17], Op.min, T.LT[:, LT0 + 304:LT0 + 305], Op.min, r="nA " + lt, w="nB")
        l1 = [T.l1[:, 16 * i:16 * i + 16] for i in range(4)]
        ts(l1[1], off, T.nn[:, 1:2], Op.is_ge, 512.0, Op.mult, r="nB " + lt, w="l11")
        tt(l1[2], l1[1], off, Op.add, "l11 " + lt, "l12")
        tt(l1[3], l1[2], l96, Op.min, "l12 K1", "l13")
        cp(T.l2u[:], l1[3], "l13", "l2u")
        if last:
            act(T.sn[:], ES[t][4].indirect(T.l2u[:]), Fn.Sign, "aM l2u code@3", "sn", bias=-17.0, c="g")
            mm([(pd[:, 0:16], to_list(Zb, T.sn))], "sn", "D")
            ts(T.ob[:], pd[:, 0:16], 1023.5, Op.add, w="ob", b="D")
        else:
            act(sM, aM, Fn.Sign, "aM", "sM", bias=-17.0)
            mm([(pd[:, 0:6], to_list(Zb, sM))], "sM", "D")
            ts(T.bn[:, 0:6], pd[:, 0:6], 1023.5, Op.add, w="bn", b="D")
            cp(T.rbn[:], T.RP[:].indirect(T.bn[:, 0:6]), "RP bn", "rbn", c="g")
            gathers(3, T.X[:, V + 64:V + 64 + 1536], T.rbn, "rbn", "n")
        for j in range(4):
            p, bk = pc[:, 512 * (j % 2):512 * (j % 2) + 384], "C%d" % (j % 2)
            parts = [(p[:, 96 * q:96 * q + 96], 128 * (4 * j + q)) for q in range(4)]
            mm([(o, [(T.FA[:, k:k + 128], mo), (T.FB[:, k:k + 128], m2)]) for o, k in parts], "mo m2 K2", bk, end=False, one=True)
            mm([(o, [(I1, mM)]) for o, k in parts], "mM", bk, first=False, one=True)
            lin(T.TR[:, 384 * j:384 * j + 384], p, "K2", "TR%d" % j, bk, bias=bq_, relu=True)
        for j in range(4):
            mm([(pk[:, 0:96], ([(I1, kp), (Im17, gm)] if j == 0 else []) + [(E(Z1, k), T.TR[:, 96 * k:96 * k + 96]) for k in range(4 * j, 4 * j + 4)])],
               "TR%d kp gm" % j, "K", first=j == 0, end=j == 3)
        return sM, qn

    def pick(mo, mk):
        if NS < 4:
            cp(T.rbu[:, 64 * NS:256], T.RP[:].indirect(T.bo[:, 4 * NS:16]), "RP bo", "rbu", c="g")
            gathers(8 - 2 * NS, T.X[:, Y0:Y0 + 1024 * (4 - NS)], T.rbu[:, 64 * NS:256], "rbu", "y")
            mm([(pb[:, 512:768 - 64 * NS], [(I16, T.l1t[:, 0:256 - 64 * NS]), (Im, mo[:, 64 * NS:256])])], mk + " K4", "B1")
            lin(T.OW[:, 96 + 64 * NS:352], pb[:, 512:768 - 64 * NS], "", "OWy", "B1", bias=Y0 - 1536.0)
        if not NS:
            return
        ts(T.rbo[:, 0:64 * NS], T.RP[:].indirect(T.bo[:, 0:4 * NS]), -1536.0, Op.add, r="RP bo", w="rbo", c="g")
        for h in range(2):
            act(T.drop[:, 2048 * h + 7:2048 * h + 512 * NS:8], mo[:, 0:64 * NS], Fn.Square, mk, "sq%d" % h, bias=-64.0 * (9 - 8 * h), scale=64.0)
        for n in range(2 * NS):
            b, h = divmod(n, 2)
            p, bk, o = [pa, pb][h][:, 512:1024], "AB"[h] + "1", 2048 * h + 512 * b
            mm([(p[:, j::8], [(T.SEL[:, 128 * (8 * h + j):128 * (8 * h + j + 1)], T.rbo[:, 64 * b:64 * b + 64])]
                 + ([(T.IB[:, 128 * j:128 * j + 128], mo[:, 64 * b:64 * b + 64])] if j < 7 else [])) for j in range(8)], "rbo K4 " + mk, bk, one=True)
            scan(T.run[:, o:o + 512], p, T.drop[:, o:o + 512], 0.0, Op.max, Op.subtract, "sq%d K4" % h, "run%d" % n, bk)
        tt(T.OW[:, 96:96 + 64 * NS], T.run[:, 7:512 * NS:8], T.run[:, 2055:2048 + 512 * NS:8], Op.max, names("run", 0, 2 * NS), "OWo")

    def sums(i):
        dd, rl, out, dk, r = T.dd[:, 1024 * i:1024 * i + 1024], T.rl[:, 1024 * i:1024 * i + 1024], pd[:, 64 * i:64 * i + 64], names("d", 2 * i, 2 * i + 2), len(ops)

        def total(z, x, first, end):
            return [g.tensor.matmul(out, a, c, first and k == 0, end and k == 15) for k, (a, c) in enumerate(to_list(z, x))][-1]
        op("VS", [lambda: g.vector.tensor_scalar(rl, dd, 0.0, None, Op.max), lambda: g.scalar.activation(rl, dd, Fn.Abs)], [cost(rl, 0.5), cost(rl, 1)], dk, "r%d" % i)
        op("P", lambda: total(Zm, dd, True, False) if ORDER["eng"][r] == "V" else None, (0, 0, 0, 0, 1024, 0), dk + " K1", "", "D", serves=r)
        op("P", lambda: total(Z2, rl, False, True) if ORDER["eng"][r] == "V" else total(Z1, rl, True, True), (0, 0, 0, 0, 1024, 0), "r%d K1" % i, "", "D")

    xall = names("x", 0, 8)
    m = [T.m0[:, 64 * i:64 * i + 64] for i in range(5)]
    banks = [[q for q in range(QD) if RQ[q] // 512 == n] for n in range(1 + RQ[-1] // 512)]
    regs = [slice(RQ[qs[0]], RQ[qs[-1]] + NB * WQ[qs[-1]]) for qs in banks]

    for t in range(ST):
        step[0] += 1
        last, s = t == ST - 1, min(t, 1)
        mp, code, mk_, ck = ES[t][0], ES[t][3], "mp@%d" % t, "code@%d" % t
        z, zk = (T.z0[:] if t == 0 else T.ZL[:, 256 * (t - 1):256 * t]), "z@%d" % t
        au, ak = T.aL[:, 16 * t:16 * t + 16], "a@%d" % t
        if t:
            el, ek = EL[t - 1], "E@%d" % t
            tt(T.l1[:, 0:16], el[1], el[2], Op.add, ek, "bs")
            ts(T.bo[:], T.l1[:, 0:16], 1023.5, Op.add, r="bs", w="bo")
        pick(*((el[0], ek) if t else (mp, mk_)))
        if not t:
            ts(T.offY[:], T.OW[:, 96:352], 1536.0, Op.add, r="OWo OWy", w="offY")
        cp(T.ra[:], T.RP[:].indirect(au), "RP " + ak, "ra", c="g")
        gathers(8, T.xx, T.ra, "ra", "x")
        if t:
            sM, qn = exchange(t - 1)
            tt(T.OW[:, 0:96], T.cj[:], pk[:, 0:96], Op.subtract, "K2", "OWn", "K")
            tt(qn, pk[:, 0:96], sM, Op.mult, "sM", "qn", "K")
            ts(T.offY[:], T.OW[:].indirect(T.l2u[:]), 1536.0, Op.add, r="OWo OWy OWn l2u", w="offY", c="g")
            lin(el[4][:, 0:96], qn, "qn", "cn", bias=17.0)
            lin(code, el[4].indirect(T.l2u[:]), "cn l2u " + ek, ck, c="g")
            act(mp, code, Fn.Abs, ck, mk_, bias=-17.0)
        cp(T.af[:], au, ak, "af")
        for j in range(4):
            p, bk = [(pa, "A0 A1"), (pb, "B0 B1")][j % 2]
            for h in range(2):
                mm([(p[:, 256 * q + 128 * h:256 * q + 128 * h + 128], [(I1, T.xx[:, 2048 * h + 4 * j + q:2048 * h + 2048:16]), (Im, z[:, 128 * h:128 * h + 128])])
                    for q in range(4)], names("x", 4 * h, 4 * h + 4) + " " + zk, bk)
            act(T.az[:, 1024 * j:1024 * j + 1024], p[:], Fn.Abs, "", "az%d" % j, bk)
        for j in range(4):
            kp, kb = pc[:, 512 * (j % 2):512 * (j % 2) + 64], "C%d" % (j % 2)
            mm([(kp, [(I1, T.kA[:]), (I1, T.kB[:, 64 * j:64 * j + 64])] + to_list(Zk, T.az[:, 1024 * j:1024 * j + 1024]))], "az%d" % j, kb)
            if j == 0:
                lin(m[0], kp, "", "m0", kb)
            else:
                tt(m[j], kp, m[j - 1], Op.min, "m%d" % (j - 1), "m%d" % j, kb)
        act(T.sn[:], code, Fn.Sign, ck, "sn", bias=-17.0)
        mm([(pk[:, 0:16], to_list(Zb, T.sn))], "sn", "K")
        ts(T.bu[:], pk[:, 0:16], 1023.5, Op.add, w="bu", b="K")
        if not last:
            lin(ES[t][1], pk[:, 0:16], "", "bh@%d" % t, "K")
            tt(ES[t][2], pk[:, 0:16], ES[t][1], Op.subtract, "bh@%d" % t, "bl@%d" % t, "K")
            send([(ES[t][5], [(rank + 1, EL[t][5])], engines([rank + 1]))],
                 "%s %s bh@%d bl@%d" % (ck, mk_, t, t), "E@%d" % (t + 1), "E", t, ne)
        ts(T.rbv[:], T.RP[:].indirect(T.bu[:]), -1536.0, Op.add, r="RP bu", w="rbv", c="g")
        for i in range(8):
            ny = max(0, i + 1 - 2 * NS)
            tt(T.dd[:, 512 * i:512 * i + 512], T.X[:, 0:Y0 + 512 * ny].indirect(T.offY[:, 32 * i:32 * i + 32]), T.xx[:, 512 * i:512 * i + 512], Op.subtract,
               "X Xd n0 n1 n2 %s offY x%d" % (names("y", 0, ny), i), "d%d" % i, c="g")
        for i in range(4):
            sums(i)
        tt(m[4][:, 0:32], m[3][:, 0:32], m[3][:, 32:64], Op.min, "m3", "m4")
        tt(T.vi[:, 0:16], m[4][:, 0:16], m[4][:, 16:32], Op.min, "m4", "vi")
        ts(T.vi[:, 16:32], T.vi[:, 0:16], 4095, Op.bitwise_and, r="vi", w="vj")
        cp(T.Lx[:], T.vi[:, 16:32], "vj", "Lx")
        tt(T.mk[:], T.IDp[:].indirect(T.Lx[:]), mp, Op.mult, "Lx K3 " + mk_, "mk", c="g")
        lin(T.xk[:], T.xx[:].indirect(T.Lx[:]), "Lx " + xall, "xk", c="g")
        mm([(pb[:, 256:272], to_list(Zm, T.mk))], "mk", "B0")
        ts(T.Lw[:], pb[:, 256:272], 16.0, Op.add, w="Lw", b="B0")
        tt(T.mm[:], T.IDp[:, 0:16].indirect(T.Lw[:]), T.rbv[:], Op.mult, "Lw rbv K3", "mm", c="g")
        lin(T.wk[:], T.dd[:].indirect(T.Lx[:]), "Lx " + names("d", 0, 8), "wk", c="g")
        mm([(pa[:, 0:256], [(Iq, T.cm1[:]), (Ih, z), (Ih, T.xx[:, 0::16])])], xall + " " + zk, "A0")
        ts(T.ZW[:, 256:512], pa[:, 0:256], MAGIC, Op.add, MAGIC, Op.subtract, w="ZW1", b="A0")
        mm([(pb[:, 256:272], to_list(None, T.mm))], "mm", "B0")
        mm([(pb[:, 0:256], [(T.BOh[:], T.mm[:])])], "mm", "B0")
        lin(T.cF[:], pb[:, 256:272], "", "cF", "B0", scale=-1.0)
        cp(T.cL[:], pb[:, 256:272], "", "cL", "B0")
        mm([(pa[:, 0:256], [(I1, z), (Im, T.xk[:]), (Im, T.wk[:])])], "wk xk " + zk, "A0")
        act(T.ZW[:, 0:256], pa[:, 0:256], Fn.Abs, "", "ZW0", "A0")
        mm([(pk[:, 0:16], [(T.I5f[:], T.af[:])] + to_list(Zu, T.ZW[:, 0:256]))], "ZW0 af", "K", end=False)
        mm([(pa[:, 256:512], [(Iq, T.cm1[:]), (I1, T.xk[:]), (Ih, T.wk[:])])], "xk wk", "A0")
        ts(T.hf[:], pa[:, 256:512], MAGIC, Op.add, MAGIC, Op.subtract, w="hf", b="A0")
        for c in range(16):
            b, q = divmod(c, QD)
            o, x = T.ad[:, RQ[q] + b * WQ[q]:RQ[q] + (b + 1) * WQ[q] - 1], pb[:, 16 * QD * b:16 * QD * b + WQ[q] - 1]
            act(o, x, Fn.Abs, "cF", "ad%d" % c, "B0", bias=T.cF[:, c:c + 1])
        for n, qs in enumerate(banks):
            mm([(pc[:, regs[n]], [(I1, T.mask[:, regs[n]]), (Im32, T.ad[:, regs[n]])])] + [(ends(pc, q), [(H1, T.cL[:, q::QD])]) for q in qs],
               "cL K3 " + " ".join("ad%d" % c for c in range(16) if c % QD in qs), "C%d" % n, end=False, one=True)
        zn, dv = T.ZO[:, 256 * t:256 * t + 256], T.dv[:]
        p0, PB, LT0, pt = (3 * 576 if last else 288 * t), (T.LT if last else T.PT), 576 * t, ["PT%s@%d" % (k, t) for k in "Aop"]
        act(T.sg[:], pd[:, 0:256], Fn.Sign, "thA", "sg", "D", bias=T.thA[:])
        mm([(pd[:, 0:16], to_list(Z1, T.sg))], "sg", "D")
        for n, qs in enumerate(banks):
            mm([(pc[:, RQ[q] + b * WQ[q]:RQ[q] + (b + 1) * WQ[q] - 1], [(T.BOm[:], T.sg[:, 16 * QD * b:16 * QD * b + WQ[q] - 1])]) for q in qs for b in range(NB)],
               "sg", "C%d" % n, first=False, end=False)
        ts(dv, pd[:, 0:16], -5.0, Op.is_gt, w="dv", b="D")
        scan(T.cs[:], one, dv, 0.0, Op.mult, Op.add, "dv K1", "cs")
        tt(T.t1[:], dv, c256, Op.mult, "dv K1", "t1")
        mm([(pk[:, 0:16], [(Ibig, dv)])], "dv", "K", first=False)
        mm([(pa[:, 0:16], [(I256, dv), (I1, lane)])], "dv", "A0")
        for n, qs in enumerate(banks):
            mm([(ends(pc, q), [(I4k, dv[:, q::QD])]) for q in qs], "dv", "C%d" % n, first=False, one=True)
        mm([(pd[:, 0:16], [(T.BO[:], T.cs[:]), (T.Um[:], dv), (Im, T.t1[:]), (I1, c255)]),
            (pd[:, 16:17], [(T.BO[:], T.cs[:, 15:16])])], "cs t1 dv", "D")
        cp(T.zl[:], pa[:, 0:16], "", "zl", "A0")
        tt(T.an[:, 0:16], pk[:, 0:16], T.af[:], Op.max, "af", "an", "K")
        ts(T.an[:, 16:32], T.an[:, 0:16], 2047, Op.bitwise_and, r="an", w="an3")
        if last:
            cp(T.oa[:], T.an[:, 16:32], "an3", "oa")
        else:
            cp(T.aS[:, 16 * t:16 * t + 16], T.an[:, 16:32], "an3", "aS@%d" % t)
            send([(T.aS[:, 16 * t:16 * t + 16], [(rank + 1, T.aL[:, 16 * t + 16:16 * t + 32])], engines([rank + 1]))], "aS@%d" % t, "a@%d" % (t + 1), "a", t, ne)
        cp(T.off[:], pd[:, 0:16], "", "off", "D")
        lin(PB[:, p0 + 16:p0 + 17], pd[:, 16:17], "", pt[0], "D")
        far = [1, 2, 3, 5] if last else [2, 3, 4]
        send([(PB[:, p0 + 16:p0 + 18], [(rank + d, T.AF[:, 16 * t + 8 + 2 * i:16 * t + 10 + 2 * i]) for i, d in enumerate(far)],
               engines([rank + d for d in far]))], pt[0], "AFr", "A", t, ne * len(far))
        tt(PB[:, p0 + 32:p0 + 288].indirect(T.off[:]), code, T.sg[:], Op.mult, ck + " sg off", pt[2], c="s")
        lin(PB[:, p0:p0 + 16], pd[:, 0:16], "", pt[1], "D")
        lin(zn, T.ZW[:].indirect(T.zl[:]), "ZW0 ZW1 zl", "zn@%d" % t, c="g")
        if last:
            send([(PB[:, p0 + 16:p0 + 128], [(rank - 2, T.LT[:, LT0 + 304:LT0 + 416])], engines([rank - 2]))], "PTA@3 PTp@3", "LT@3", "Q", t, ne)
        else:
            send([(zn, [(rank + 1, T.ZL[:, 256 * t:256 * t + 256])], engines([rank + 1]))], "zn@%d" % t, "z@%d" % (t + 1), "z", t, ne)
            es = engines([rank + 1, rank - 1])
            PT = T.PT[:, p0:p0 + 128]
            send([(PT, [(rank + 1, T.LT[:, LT0:LT0 + 128])], es[:ne // 2]), (PT, [(rank - 1, T.LT[:, LT0 + 288:LT0 + 416])], es[ne // 2:])],
                 " ".join(pt), "LT@%d" % t, "Q", t, ne)
        lin(T.AF[:, 16 * t:16 * t + 1], pd[:, 16:17], "", "AF@%d" % t, "D")
        if not last:
            cp(T.Ai[:, 0:1], pd[:, 16:17], "", "Ai0", "D")
            ts(T.Ai[:, 1:2], T.Ai[:, 0:1], 31, Op.bitwise_and, r="Ai0", w="Ai1")
            tt(T.thA[:], T.thf[:], T.Ai[:, 1:2], Op.subtract, "Ai1 thf", "thA")
        for n, qs in enumerate(banks):
            scan(T.sc[:, regs[n]], T.crst[:, regs[n]], pc[:, regs[n]], 0.0, Op.mult, Op.max, "K3", " ".join("sc%d" % q for q in qs), "C%d" % n)
        for q in range(QD):
            ts(T.su[:, q::QD], ends(T.sc, q), dum_[q], Op.min, r="sc%d K1" % q, w="su%d" % q)
        for b in range(NB - 1, -1, -1):
            cp(T.X[:, 0:V + 64].indirect(T.su[:, QD * b:QD * b + QD]), T.hf[:, 16 * QD * b:16 * QD * (b + 1)], "hf Xd " + names("su", 0, QD), "X", c="s")

    step[0] += 1
    lin(T.KW[:, 96:352], mp, mk_, "KWo", bias=16.0, scale=-1.0, c=0.5)
    exchange(ST - 1)
    lin(T.KW[:, 0:96], pk[:, 0:96], "", "KWn", "K", bias=16.0, scale=-1.0)
    lin(T.ok[:], T.KW[:].indirect(T.l2u[:]), "KWo KWn l2u", "ok", c="g")
    for e, o, i, k, lat in (("Y", T.yz, zn, "zn@3", 2.5), ("Y", T.ya, T.oa[:], "oa", 2.5), ("Y", T.yx, T.X[:, 0:V], "X", 5.5),
                            ("Y", T.yb, T.ob[:], "ob", 2.5), ("S", T.yk, T.ok[:], "ok", 2.5)):
        dma(e, o[:], i, "out", k)
        op("R", None, fixed(lat), "q" + e + "out", "")
        wr.pop("q" + e + "out")
        rd.pop("q" + e + "out")

    if "order" not in ORDER:
        ORDER["order"], ORDER["eng"], ORDER["t"] = schedule(ops)
    for o, e in zip(ops, ORDER["eng"]):
        o["e"] = e
    cnt = {"V": 0, "S": 0, "P": 0, "G": 0}
    seen = {e: {} for e in Q}
    for i in ORDER["order"]:
        o = ops[i]
        e = o["e"]
        if e in "RL":
            continue
        top = {}
        for p, raw in o["pre"].items():
            tok = ops[p]["tok"]
            if tok and (raw or ops[p]["e"] != e):
                top[tok[0]] = max(top.get(tok[0], 0), tok[1])
        for k, n in top.items():
            if seen[e].get(k, 0) < n:
                Q[e].wait_ge(T.sem[k], n)
                seen[e][k] = n
        ins = o["f"][-1 if e == "S" else 0]()
        if ins is not None:
            cnt[e] += 1
            ins.then_inc(T.sem[e], 1)
            o["tok"] = (e, cnt[e])
    for k in cnt:
        g.wait_ge(T.sem[k], cnt[k])
    g.wait_ge(T.sem.sent, sent[0])
    g.wait_ge(T.sem.out, 80)
